import numpy as np
import ml_dtypes


def mxq(x, axis, fmt="e4m3"):
    dtype, down = {"e4m3": (ml_dtypes.float8_e4m3fn, 7), "e5m2": (ml_dtypes.float8_e5m2, 14)}[fmt]
    v = np.moveaxis(np.asarray(x, np.float32).astype(ml_dtypes.bfloat16).astype(np.float64), axis, -1)
    blocks = v.reshape(v.shape[:-1] + (-1, 32))
    amax = np.abs(blocks).max(-1, keepdims=True)
    byte = np.maximum(np.where(amax > 0, np.frexp(amax)[1] - 1 + 127, 0) - down, 1)
    scale = np.exp2(byte - 127.0)
    codes = (blocks / scale).astype(np.float32).astype(dtype).astype(np.float64)
    return np.moveaxis((codes * scale).reshape(v.shape), -1, axis)


WIDE = False


def mx_kscale(k):
    if not WIDE:
        return np.ones(k)
    levels = np.array([10, -10, 5, -5, 0])
    if k % 512:
        return np.exp2(np.random.permutation(np.resize(levels, k // 32))).repeat(32)
    a = np.empty((k // 512, 16))
    for p in range(k // 512):
        a[p, :8] = np.random.permutation(np.resize(levels, 8))
        for g in range(8):
            far = levels[np.abs(levels - a[p, g]) >= 10]
            a[p, g + 8] = far[np.random.randint(len(far))]
    return np.exp2(a.ravel()).repeat(32)


def f64(x):
    return np.asarray(x).astype(np.float64)


def striped(idx):
    return np.tile(idx.reshape(-1, 16).T, (8, 1)).astype(np.uint16)


def unstriped(offs):
    return offs[:16].T.reshape(-1).astype(np.int64)


E2M1 = np.array([0.0, 0.5, 1.0, 1.5, 2.0, 3.0, 4.0, 6.0, -0.0, -0.5, -1.0, -1.5, -2.0, -3.0, -4.0, -6.0])


def pack_weight(w, fmt):
    k, n = w.shape
    w = f64(np.asarray(w, np.float32).astype(ml_dtypes.bfloat16)).reshape(k // 32, 32, n)
    amax = np.abs(w).max(1)
    if fmt == "e4m3":
        byte = np.frexp(amax)[1] - 1 + 127 - 7
    else:
        mant, ex = np.frexp(amax / 6.0)
        byte = np.where(mant > 0.5, ex, ex - 1) + 127
    byte = np.clip(np.where(amax > 0, byte, 1), 1, 254)
    scaled = (w * np.exp2(127.0 - byte)[:, None, :]).reshape(k, n).astype(np.float32)
    by_word = np.ascontiguousarray(scaled.reshape(k // 512, 128, 4, n).transpose(0, 1, 3, 2))
    if fmt == "e4m3":
        words = by_word.astype(ml_dtypes.float8_e4m3fn).view(np.uint8)
    else:
        c = by_word.astype(ml_dtypes.float4_e2m1fn).view(np.uint8) & 0xF
        words = (c[..., 0::2] | (c[..., 1::2] << 4)).reshape(k // 512, 128, 2 * n)
    return np.ascontiguousarray(words), np.ascontiguousarray(byte.astype(np.uint8).reshape(k // 512, 16, n))


def unpack_weight(words, scales, fmt):
    g, _, n = scales.shape
    words = np.ascontiguousarray(words).reshape(g, 128, n, -1)
    if fmt == "e4m3":
        vals = words.view(ml_dtypes.float8_e4m3fn).astype(np.float64)
    else:
        nib = np.empty((g, 128, n, 4), np.uint8)
        nib[..., 0::2] = words & 0xF
        nib[..., 1::2] = words >> 4
        vals = E2M1[nib]
    vals = vals * np.repeat(np.exp2(scales.astype(np.float64) - 127.0), 8, axis=1)[..., None]
    return vals.transpose(0, 1, 3, 2).reshape(g * 512, n)


def gelu(v):
    return 0.5 * v * (1.0 + np.tanh(np.sqrt(2.0 / np.pi) * (v + 0.044715 * v**3)))


T, S, K, H, N = 4096, 1024, 1024, 512, 256

def setup_inputs():
    n = np.random.standard_normal
    s = mx_kscale(K)[:, None]
    u = mx_kscale(H)[:, None]
    tab_words, tab_scales = pack_weight(n((K, T)) * s, "e4m3")
    w2_words, w2_scales = pack_weight(n((K, H)) / np.sqrt(K) / s, "e2m1")
    w3_words, w3_scales = pack_weight(n((K, H)) / np.sqrt(K) / s, "e4m3")
    return {
        "tab_words": tab_words, "tab_scales": tab_scales,
        "offs": striped(np.random.permutation(T)[:S]),
        "offs2": striped(np.random.permutation(T)[:S]),
        "offs3": striped(np.random.permutation(T)[:S]),
        "w1": (n((K, H)) / np.sqrt(K) / s * u.T).astype(np.float32),
        "w2_words": w2_words, "w2_scales": w2_scales,
        "w3_words": w3_words, "w3_scales": w3_scales,
        "w4": (2.0 * n((H, N)) / np.sqrt(H) / u).astype(np.float32),
        "fscale": np.exp(0.3 * n(N)).astype(np.float32),
        "fbase": (0.5 * n(N)).astype(np.float32),
    }

def reference(tab_words, tab_scales, offs, offs2, offs3, w1, w2_words, w2_scales,
              w3_words, w3_scales, w4, fscale, fbase):
    vs = unpack_weight(tab_words, tab_scales, "e4m3")[:, unstriped(offs)]
    vc = unpack_weight(tab_words, tab_scales, "e4m3")[:, unstriped(offs2)]
    vi = unpack_weight(tab_words, tab_scales, "e4m3")[:, unstriped(offs3)]
    w2 = unpack_weight(w2_words, w2_scales, "e2m1")
    w3 = unpack_weight(w3_words, w3_scales, "e4m3")
    a = mxq(f64(w1), 0, "e4m3").T @ vs
    m = w2.T @ vc + w3.T @ vi
    h = a / (1.0 + np.abs(m))
    y = mxq(f64(w4), 0, "e4m3").T @ mxq(h, 0, "e4m3")
    return y * f64(fscale)[:, None] + f64(fbase)[:, None]

@@ -1,0 +1,262 @@
+from contextlib import ExitStack
+
+import concourse.mybir as mybir
+
+T, S, K, H, N = 4096, 1024, 1024, 512, 256
+FLOPS = 2 * S * (3 * K * H + H * N)
+
+F32 = mybir.dt.float32
+BF16 = mybir.dt.bfloat16
+I32 = mybir.dt.int32
+U32 = mybir.dt.uint32
+U16 = mybir.dt.uint16
+U8 = mybir.dt.uint8
+FP8X4 = mybir.dt.float8_e4m3fn_x4
+FP4X4 = mybir.dt.float4_e2m1fn_x4
+ACT = mybir.ActivationFunctionType
+MULT = mybir.AluOpType.mult
+
+P = 128
+HALF = 512
+CHUNK = 128
+
+
+def tile_list_equity_factor_exposures_kernel(
+    tc, tab_words, tab_scales, offs, offs2, offs3, w1, w2_words, w2_scales, w3_words, w3_scales, w4, fscale, fbase, out
+):
+    nc = tc.nc
+    with ExitStack() as ctx:
+        keep = ctx.enter_context(tc.tile_pool(name="keep", bufs=1))
+        psum = ctx.enter_context(tc.psum_pool(name="psum", bufs=1))
+
+        def sb(name, cols, dtype):
+            return keep.tile([P, cols], dtype, name=name, align_bytes=64)
+
+        def bank(b):
+            return psum.tile([P, HALF], F32, name="bank%d" % b)
+
+        lists = {j: keep.tile([P, S // 16], U16, name="list%d" % j) for j in (1, 2, 3)}
+        scale_win = sb("scale_win", T, U8)
+        word_win = [sb("word_win%d" % a, T, U32) for a in range(2)]
+        ws_raw = sb("ws_raw", 4 * H, U8)
+        g2_pass0 = sb("g2_pass0", S, U8)
+        warm = sb("warm", 16, F32)
+        fs = sb("fs", 2, F32)
+        fb = sb("fb", 2, F32)
+
+        nc.gpsimd.memset(ws_raw[:].bitcast(I32), 0)
+        nc.gpsimd.memset(warm[:, 0:8], 1.0)
+        nc.gpsimd.memset(g2_pass0[:].bitcast(I32), 0)
+
+        w2_raw = sb("w2_raw", 4 * H, U8)
+        w3_raw = sb("w3_raw", 2 * H, U32)
+        w4_raw = sb("w4_raw", 4 * N, F32)
+        nc.sync.dma_start(
+            w2_raw[:].bitcast(I32).rearrange("p (a b) -> p a b", a=2), w2_words.bitcast(I32).rearrange("a p b -> p a b")
+        )
+        nc.sync.dma_start(
+            w3_raw[:].bitcast(I32).rearrange("p (a c) -> p a c", a=2),
+            w3_words.rearrange("a p c i -> a p (c i)").bitcast(I32).rearrange("a p c -> p a c"),
+        )
+        nc.sync.dma_start(lists[2][:], offs2)
+        scale_rows = tab_scales.rearrange("a q t -> (a q) t").bitcast(I32)
+        runs = [(0, 4, 16), (116, 4, 0), (120, 8, 0)]
+        for q in range(4):
+            runs.append((32 * q + 4, 16, 4 * q))
+            if q < 3:
+                runs.append((32 * q + 20, 16, 4 * q + 8))
+        for part, count, row in runs:
+            nc.sync.dma_start(scale_win[part : part + count, :].bitcast(I32), scale_rows[row : row + count, :])
+        nc.scalar.activation(out=warm[:, 8:9], in_=warm[:, 0:1], func=ACT.Abs_reciprocal_sqrt)
+        for w, src in enumerate((w2_scales, w3_scales)):
+            for q in range(4):
+                nc.gpsimd.dma_start(
+                    ws_raw[32 * q : 32 * q + 4, 2 * H * w : 2 * H * (w + 1)].bitcast(I32).rearrange("r (a c) -> r a c", a=2),
+                    src[:, 4 * q : 4 * q + 4, :].bitcast(I32).rearrange("a r c -> r a c"),
+                )
+
+        def load_words(a):
+            nc.sync.dma_start(word_win[a][:].bitcast(I32), tab_words[a].rearrange("p t i -> p (t i)").bitcast(I32))
+
+        w1_raw = [sb("w1_raw%d" % a, 4 * H, F32) for a in range(2)]
+
+        def load_w1(a):
+            nc.sync.dma_start(w1_raw[a][:], w1[512 * a : 512 * (a + 1), :].rearrange("(p j) c -> p (j c)", j=4))
+
+        nc.sync.dma_start(lists[3][:], offs3)
+        load_words(0)
+        load_words(1)
+        nc.sync.dma_start(lists[1][:], offs)
+        load_w1(0)
+        load_w1(1)
+        w4_rows = w4.rearrange("(g t i) n -> t g i n", t=4, i=8)
+        for t in range(4):
+            nc.sync.dma_start(w4_raw[:, N * t : N * (t + 1)], w4_rows[t])
+        nc.sync.dma_start(fs[:], fscale.rearrange("(p c) -> p c", c=2))
+        nc.sync.dma_start(fb[:], fbase.rearrange("(p c) -> p c", c=2))
+
+        g_scale = {j: sb("g_scale%d" % j, S, U8) for j in (1, 2, 3)}
+        g_word = {(j, a): sb("g_word%d_%d" % (j, a), S, U32) for j in (1, 2, 3) for a in range(2)}
+
+        def gather(dst, window, j, lo, hi):
+            nc.vector.tensor_copy(dst[:, lo:hi], window[:].indirect(lists[j][:, lo // 16 : hi // 16]))
+
+        w2_ord = sb("w2_ord", 4 * H, U8)
+        w3_ord = sb("w3_ord", 2 * H, U32)
+        ws_ord = sb("ws_ord", 4 * H, U8)
+
+        def reorder(engine, dst, src, planes):
+            engine.tensor_copy(
+                dst[:].bitcast(I32).rearrange("p (a t g e) -> p a t g e", a=planes, t=4, g=16),
+                src[:].bitcast(I32).rearrange("p (a g t e) -> p a t g e", a=planes, t=4, g=16),
+            )
+
+        reorder(nc.vector, w2_ord, w2_raw, 2)
+        reorder(nc.vector, w3_ord, w3_raw, 2)
+        reorder(nc.gpsimd, ws_ord, ws_raw, 4)
+        gather(g_scale[2], scale_win, 2, 0, S)
+        nc.gpsimd.dma_start(g2_pass0[0:100, :].bitcast(I32), g_scale[2][4:104, :].bitcast(I32))
+        gather(g_scale[3], scale_win, 3, 0, S)
+        gather(g_word[2, 0], word_win[0], 2, 0, S)
+        gather(g_word[3, 0], word_win[0], 3, 0, S)
+
+        w1_bf = [sb("w1_bf%d" % a, 4 * H, BF16) for a in range(2)]
+        w1_codes = sb("w1_codes", 2 * H, U32)
+        w1_scale = sb("w1_scale", 2 * H, U8)
+        src = w1_raw[0][:].rearrange("p (j g t i) -> p t g i j", j=4, g=16, t=4)
+        dst = w1_bf[0][:].rearrange("p (t g i j) -> p t g i j", j=4, g=16, t=4)
+        for t in range(4):
+            nc.scalar.copy(dst[:, t], src[:, t])
+
+        def table_scale(j, a, lo, hi):
+            if j == 2 and a == 0:
+                return g2_pass0[:, lo:hi]
+            return g_scale[j][4 * (1 - a) : P, lo:hi]
+
+        damp = [sb("damp%d" % c, 4 * CHUNK, F32) for c in range(S // CHUNK)]
+        for half in range(2):
+            lo, hi = HALF * half, HALF * (half + 1)
+            gather(g_word[3, 1], word_win[1], 3, lo, hi)
+            gather(g_word[2, 1], word_win[1], 2, lo, hi)
+            m_banks = [bank(4 * half + t) for t in range(4)]
+            for a in range(2):
+                for j in (3, 2):
+                    for t in range(4):
+                        col = H * a + P * t
+                        if j == 2:
+                            lhsT = w2_ord[:, 2 * col : 2 * (col + P)].bitcast(FP4X4)
+                        else:
+                            lhsT = w3_ord[:, col : col + P].bitcast(FP8X4)
+                        scol = 2 * H * (j - 2) + col
+                        nc.tensor.matmul_mx(
+                            out=m_banks[t][:],
+                            lhsT=lhsT,
+                            lhsT_scale=ws_ord[:, scol : scol + P],
+                            rhs=g_word[j, a][:, lo:hi].bitcast(FP8X4),
+                            rhs_scale=table_scale(j, a, lo, hi),
+                            start=(a == 0 and j == 3),
+                            stop=(a == 1 and j == 2),
+                        )
+            m_abs = sb("m_abs%d" % half, 4 * HALF, F32)
+            for t in range(4):
+                nc.scalar.activation(out=m_abs[:, HALF * t : HALF * (t + 1)], in_=m_banks[t][:], func=ACT.Abs)
+            by_token = m_abs[:].rearrange("p (t n) -> p n t", t=4)
+            for c in range(4):
+                root = sb("root%d" % (c % 2), 4 * CHUNK, F32)
+                nc.scalar.activation(
+                    out=root[:].rearrange("p (n t) -> p n t", t=4),
+                    in_=by_token[:, CHUNK * c : CHUNK * (c + 1), :],
+                    func=ACT.Abs_reciprocal_sqrt,
+                    bias=1.0,
+                )
+                nc.scalar.activation(out=damp[4 * half + c][:], in_=root[:], func=ACT.Square)
+
+        gather(g_scale[1], scale_win, 1, 0, S)
+        gather(g_word[1, 0], word_win[0], 1, 0, S)
+
+        def quantize(codes, scales, values):
+            nc.vector.quantize_mx(out=codes.bitcast(FP8X4), scales=scales, in_=values)
+
+        quantize(w1_codes[:, 0:H], w1_scale[:, 0:H], w1_bf[0][:])
+        nc.vector.tensor_copy(
+            w1_bf[1][:].rearrange("p (t g i j) -> p t g i j", j=4, g=16, t=4),
+            w1_raw[1][:].rearrange("p (j g t i) -> p t g i j", j=4, g=16, t=4),
+        )
+        gather(g_word[1, 1], word_win[1], 1, 0, HALF)
+        quantize(w1_codes[:, H : 2 * H], w1_scale[:, H : 2 * H], w1_bf[1][:])
+        w4_bf = sb("w4_bf", 4 * N, BF16)
+        w4_codes = sb("w4_codes", N, U32)
+        w4_scale = sb("w4_scale", N, U8)
+        nc.vector.tensor_copy(
+            w4_bf[:].rearrange("p (c m t) -> p c m t", c=2, t=4), w4_raw[:].rearrange("p (t m c) -> p c m t", c=2, t=4)
+        )
+        gather(g_word[1, 1], word_win[1], 1, HALF, S)
+        quantize(w4_codes[:], w4_scale[:], w4_bf[:])
+
+        a_banks = []
+        for c in range(S // CHUNK):
+            lo, hi = CHUNK * c, CHUNK * (c + 1)
+            acc = bank(c)
+            a_banks.append(acc)
+            for t in range(4):
+                for a in range(2):
+                    col = H * a + P * t
+                    nc.tensor.matmul_mx(
+                        out=acc[:, CHUNK * t : CHUNK * (t + 1)],
+                        lhsT=w1_codes[:, col : col + P].bitcast(FP8X4),
+                        lhsT_scale=w1_scale[:, col : col + P],
+                        rhs=g_word[1, a][:, lo:hi].bitcast(FP8X4),
+                        rhs_scale=table_scale(1, a, lo, hi),
+                        start=(a == 0),
+                        stop=(a == 1),
+                    )
+
+        h_bf = [sb("h_bf%d" % c, 4 * CHUNK, BF16) for c in range(S // CHUNK)]
+        h_codes = sb("h_codes", S, U32)
+        h_scale = sb("h_scale", S, U8)
+        out_rows = out.rearrange("(p c) j -> p c j", c=2)
+
+        def damped(c):
+            nc.vector.tensor_tensor(
+                h_bf[c][:].rearrange("p (n t) -> p n t", t=4),
+                a_banks[c][:].rearrange("p (t n) -> p n t", t=4),
+                damp[c][:].rearrange("p (n t) -> p n t", t=4),
+                MULT,
+            )
+
+        def exposures(lo, hi, banks):
+            width = hi - lo
+            result = sb("result%d" % lo, 2 * width, F32)
+            tiles = {b: bank(b) for b in sorted(set(banks))}
+            for c in range(2):
+                start = 0 if banks[0] != banks[1] else width * c
+                acc = tiles[banks[c]][:, start : start + width]
+                nc.tensor.matmul_mx(
+                    out=acc,
+                    lhsT=w4_codes[:, P * c : P * (c + 1)].bitcast(FP8X4),
+                    lhsT_scale=w4_scale[:, P * c : P * (c + 1)],
+                    rhs=h_codes[:, lo:hi].bitcast(FP8X4),
+                    rhs_scale=h_scale[:, lo:hi],
+                    start=True,
+                    stop=True,
+                )
+            for c in range(2):
+                start = 0 if banks[0] != banks[1] else width * c
+                nc.scalar.activation(
+                    out=result[:, width * c : width * (c + 1)],
+                    in_=tiles[banks[c]][:, start : start + width],
+                    func=ACT.Identity,
+                    scale=fs[:, c : c + 1],
+                    bias=fb[:, c : c + 1],
+                )
+            nc.sync.dma_start(out_rows[:, :, lo:hi], result[:].rearrange("p (c j) -> p c j", c=2))
+
+        groups = {3: (0, 512, (0, 1)), 5: (512, 768, (2, 2)), 6: (768, 896, (3, 3)), 7: (896, 1024, (4, 4))}
+        damped(0)
+        for c in range(S // CHUNK):
+            if c + 1 < S // CHUNK:
+                damped(c + 1)
+            lo, hi = CHUNK * c, CHUNK * (c + 1)
+            quantize(h_codes[:, lo:hi], h_scale[:, lo:hi], h_bf[c][:])
+            if c in groups:
+                exposures(*groups[c])

@@ -44,13 +44,35 @@ def tile_list_equity_factor_exposures_kernel(
         fs = sb("fs", 2, F32)
         fb = sb("fb", 2, F32)
 
-        nc.gpsimd.memset(ws_raw[:].bitcast(I32), 0)
+        nc.vector.memset(scale_win[:, 0 : T // 2].bitcast(I32), 0)
+        nc.gpsimd.memset(scale_win[:, T // 2 : T].bitcast(I32), 0)
         nc.gpsimd.memset(warm[:, 0:8], 1.0)
+        nc.gpsimd.memset(ws_raw[:].bitcast(I32), 0)
         nc.gpsimd.memset(g2_pass0[:].bitcast(I32), 0)
 
         w2_raw = sb("w2_raw", 4 * H, U8)
         w3_raw = sb("w3_raw", 2 * H, U32)
         w4_raw = sb("w4_raw", 4 * N, F32)
+        scale_rows = tab_scales.rearrange("a q t -> (a q) t").bitcast(I32)
+
+        def load_scale_rows(queue, part, count, row):
+            queue.dma_start(scale_win[part : part + count, :].bitcast(I32), scale_rows[row : row + count, :])
+
+        nc.sync.dma_start(lists[2][:], offs2)
+        nc.sync.dma_start(lists[3][:], offs3)
+        for part, count, row in ((0, 4, 16), (108, 4, 12), (12, 32, 0), (68, 32, 0), (44, 4, 4), (64, 4, 24)):
+            load_scale_rows(nc.sync, part, count, row)
+        nc.scalar.activation(out=warm[:, 8:9], in_=warm[:, 0:1], func=ACT.Abs_reciprocal_sqrt)
+        for w, src in enumerate((w2_scales, w3_scales)):
+            nc.sync.dma_start(
+                ws_raw[0:16, 2 * H * w : 2 * H * (w + 1)].bitcast(I32).rearrange("q (a c) -> q a c", a=2),
+                src.bitcast(I32).rearrange("a q c -> q a c"),
+            )
+
+        def load_words(a):
+            nc.sync.dma_start(word_win[a][:].bitcast(I32), tab_words[a].rearrange("p t i -> p (t i)").bitcast(I32))
+
+        load_words(0)
         nc.sync.dma_start(
             w2_raw[:].bitcast(I32).rearrange("p (a b) -> p a b", a=2), w2_words.bitcast(I32).rearrange("a p b -> p a b")
         )
@@ -58,37 +80,17 @@ def tile_list_equity_factor_exposures_kernel(
             w3_raw[:].bitcast(I32).rearrange("p (a c) -> p a c", a=2),
             w3_words.rearrange("a p c i -> a p (c i)").bitcast(I32).rearrange("a p c -> p a c"),
         )
-        nc.sync.dma_start(lists[2][:], offs2)
-        scale_rows = tab_scales.rearrange("a q t -> (a q) t").bitcast(I32)
-        runs = [(0, 4, 16), (116, 4, 0), (120, 8, 0)]
-        for q in range(4):
-            runs.append((32 * q + 4, 16, 4 * q))
-            if q < 3:
-                runs.append((32 * q + 20, 16, 4 * q + 8))
-        for part, count, row in runs:
-            nc.sync.dma_start(scale_win[part : part + count, :].bitcast(I32), scale_rows[row : row + count, :])
-        nc.scalar.activation(out=warm[:, 8:9], in_=warm[:, 0:1], func=ACT.Abs_reciprocal_sqrt)
-        for w, src in enumerate((w2_scales, w3_scales)):
-            for q in range(4):
-                nc.gpsimd.dma_start(
-                    ws_raw[32 * q : 32 * q + 4, 2 * H * w : 2 * H * (w + 1)].bitcast(I32).rearrange("r (a c) -> r a c", a=2),
-                    src[:, 4 * q : 4 * q + 4, :].bitcast(I32).rearrange("a r c -> r a c"),
-                )
-
-        def load_words(a):
-            nc.sync.dma_start(word_win[a][:].bitcast(I32), tab_words[a].rearrange("p t i -> p (t i)").bitcast(I32))
-
-        w1_raw = [sb("w1_raw%d" % a, 4 * H, F32) for a in range(2)]
-
-        def load_w1(a):
-            nc.sync.dma_start(w1_raw[a][:], w1[512 * a : 512 * (a + 1), :].rearrange("(p j) c -> p (j c)", j=4))
-
-        nc.sync.dma_start(lists[3][:], offs3)
-        load_words(0)
         load_words(1)
+
+        w1_rows = w1.rearrange("(a p j) c -> a p j c", a=2, j=4)
+        w1_first = [sb("w1_first%d" % u, 2 * H, F32) for u in range(2)]
+        w1_second = sb("w1_second", 4 * H, F32)
+        for u in range(2):
+            nc.sync.dma_start(
+                w1_first[u][:].rearrange("p (j c) -> p j c", j=4), w1_rows[0][:, :, 256 * u : 256 * (u + 1)]
+            )
         nc.sync.dma_start(lists[1][:], offs)
-        load_w1(0)
-        load_w1(1)
+        nc.sync.dma_start(w1_second[:].rearrange("p (j c) -> p j c", j=4), w1_rows[1])
         w4_rows = w4.rearrange("(g t i) n -> t g i n", t=4, i=8)
         for t in range(4):
             nc.sync.dma_start(w4_raw[:, N * t : N * (t + 1)], w4_rows[t])
@@ -111,28 +113,32 @@ def tile_list_equity_factor_exposures_kernel(
                 src[:].bitcast(I32).rearrange("p (a g t e) -> p a t g e", a=planes, t=4, g=16),
             )
 
-        reorder(nc.vector, w2_ord, w2_raw, 2)
-        reorder(nc.vector, w3_ord, w3_raw, 2)
-        reorder(nc.gpsimd, ws_ord, ws_raw, 4)
         gather(g_scale[2], scale_win, 2, 0, S)
-        nc.gpsimd.dma_start(g2_pass0[0:100, :].bitcast(I32), g_scale[2][4:104, :].bitcast(I32))
+        nc.scalar.dma_start(g2_pass0[0:112, :].bitcast(I32), g_scale[2][12:124, :].bitcast(I32))
+        reorder(nc.vector, ws_ord, ws_raw, 4)
+        for q in range(1, 4):
+            nc.scalar.dma_start(ws_ord[32 * q : 32 * q + 4, :].bitcast(I32), ws_ord[4 * q : 4 * q + 4, :].bitcast(I32))
         gather(g_scale[3], scale_win, 3, 0, S)
-        gather(g_word[2, 0], word_win[0], 2, 0, S)
         gather(g_word[3, 0], word_win[0], 3, 0, S)
+        reorder(nc.vector, w3_ord, w3_raw, 2)
+        reorder(nc.vector, w2_ord, w2_raw, 2)
+        gather(g_word[2, 0], word_win[0], 2, 0, S)
 
         w1_bf = [sb("w1_bf%d" % a, 4 * H, BF16) for a in range(2)]
         w1_codes = sb("w1_codes", 2 * H, U32)
         w1_scale = sb("w1_scale", 2 * H, U8)
-        src = w1_raw[0][:].rearrange("p (j g t i) -> p t g i j", j=4, g=16, t=4)
         dst = w1_bf[0][:].rearrange("p (t g i j) -> p t g i j", j=4, g=16, t=4)
-        for t in range(4):
-            nc.scalar.copy(dst[:, t], src[:, t])
+        for u in range(2):
+            src = w1_first[u][:].rearrange("p (j g t i) -> p t g i j", j=4, g=8, t=4)
+            for t in range(4):
+                nc.scalar.copy(dst[:, t, 8 * u : 8 * (u + 1)], src[:, t])
 
         def table_scale(j, a, lo, hi):
             if j == 2 and a == 0:
                 return g2_pass0[:, lo:hi]
-            return g_scale[j][4 * (1 - a) : P, lo:hi]
+            return g_scale[j][12 * (1 - a) : P, lo:hi]
 
+        w4_bf = sb("w4_bf", 4 * N, BF16)
         damp = [sb("damp%d" % c, 4 * CHUNK, F32) for c in range(S // CHUNK)]
         for half in range(2):
             lo, hi = HALF * half, HALF * (half + 1)
@@ -161,15 +167,22 @@ def tile_list_equity_factor_exposures_kernel(
             for t in range(4):
                 nc.scalar.activation(out=m_abs[:, HALF * t : HALF * (t + 1)], in_=m_banks[t][:], func=ACT.Abs)
             by_token = m_abs[:].rearrange("p (t n) -> p n t", t=4)
-            for c in range(4):
-                root = sb("root%d" % (c % 2), 4 * CHUNK, F32)
-                nc.scalar.activation(
-                    out=root[:].rearrange("p (n t) -> p n t", t=4),
-                    in_=by_token[:, CHUNK * c : CHUNK * (c + 1), :],
-                    func=ACT.Abs_reciprocal_sqrt,
-                    bias=1.0,
+            if half == 1:
+                nc.scalar.copy(
+                    w4_bf[:].rearrange("p (c m t) -> p c m t", c=2, t=4),
+                    w4_raw[:].rearrange("p (t m c) -> p c m t", c=2, t=4),
                 )
-                nc.scalar.activation(out=damp[4 * half + c][:], in_=root[:], func=ACT.Square)
+            roots = [sb("root%d_%d" % (half, c), 4 * CHUNK, F32) for c in range(4)]
+            for c in range(5):
+                if c < 4:
+                    nc.scalar.activation(
+                        out=roots[c][:].rearrange("p (n t) -> p n t", t=4),
+                        in_=by_token[:, CHUNK * c : CHUNK * (c + 1), :],
+                        func=ACT.Abs_reciprocal_sqrt,
+                        bias=1.0,
+                    )
+                if c > 0:
+                    nc.scalar.activation(out=damp[4 * half + c - 1][:], in_=roots[c - 1][:], func=ACT.Square)
 
         gather(g_scale[1], scale_win, 1, 0, S)
         gather(g_word[1, 0], word_win[0], 1, 0, S)
@@ -180,16 +193,12 @@ def tile_list_equity_factor_exposures_kernel(
         quantize(w1_codes[:, 0:H], w1_scale[:, 0:H], w1_bf[0][:])
         nc.vector.tensor_copy(
             w1_bf[1][:].rearrange("p (t g i j) -> p t g i j", j=4, g=16, t=4),
-            w1_raw[1][:].rearrange("p (j g t i) -> p t g i j", j=4, g=16, t=4),
+            w1_second[:].rearrange("p (j g t i) -> p t g i j", j=4, g=16, t=4),
         )
         gather(g_word[1, 1], word_win[1], 1, 0, HALF)
         quantize(w1_codes[:, H : 2 * H], w1_scale[:, H : 2 * H], w1_bf[1][:])
-        w4_bf = sb("w4_bf", 4 * N, BF16)
         w4_codes = sb("w4_codes", N, U32)
         w4_scale = sb("w4_scale", N, U8)
-        nc.vector.tensor_copy(
-            w4_bf[:].rearrange("p (c m t) -> p c m t", c=2, t=4), w4_raw[:].rearrange("p (t m c) -> p c m t", c=2, t=4)
-        )
         gather(g_word[1, 1], word_win[1], 1, HALF, S)
         quantize(w4_codes[:], w4_scale[:], w4_bf[:])
 

@@ -15,6 +15,7 @@ FP8X4 = mybir.dt.float8_e4m3fn_x4
 FP4X4 = mybir.dt.float4_e2m1fn_x4
 ACT = mybir.ActivationFunctionType
 MULT = mybir.AluOpType.mult
+ADD = mybir.AluOpType.add
 
 P = 128
 HALF = 512
@@ -39,6 +40,7 @@ def tile_list_equity_factor_exposures_kernel(
         scale_win = sb("scale_win", T, U8)
         word_win = [sb("word_win%d" % a, T, U32) for a in range(2)]
         ws_raw = sb("ws_raw", 4 * H, U8)
+        ws_ord = sb("ws_ord", 4 * H, U8)
         g2_pass0 = sb("g2_pass0", S, U8)
         warm = sb("warm", 16, F32)
         fs = sb("fs", 2, F32)
@@ -47,7 +49,7 @@ def tile_list_equity_factor_exposures_kernel(
         nc.vector.memset(scale_win[:, 0 : T // 2].bitcast(I32), 0)
         nc.gpsimd.memset(scale_win[:, T // 2 : T].bitcast(I32), 0)
         nc.gpsimd.memset(warm[:, 0:8], 1.0)
-        nc.gpsimd.memset(ws_raw[:].bitcast(I32), 0)
+        nc.gpsimd.memset(ws_ord[:].bitcast(I32), 0)
         nc.gpsimd.memset(g2_pass0[:].bitcast(I32), 0)
 
         w2_raw = sb("w2_raw", 4 * H, U8)
@@ -58,12 +60,7 @@ def tile_list_equity_factor_exposures_kernel(
         def load_scale_rows(queue, part, count, row):
             queue.dma_start(scale_win[part : part + count, :].bitcast(I32), scale_rows[row : row + count, :])
 
-        nc.sync.dma_start(lists[2][:], offs2)
-        nc.sync.dma_start(lists[3][:], offs3)
-        for part, count, row in ((0, 4, 16), (108, 4, 12), (12, 32, 0), (68, 32, 0), (44, 4, 4), (64, 4, 24)):
-            load_scale_rows(nc.sync, part, count, row)
-        nc.scalar.activation(out=warm[:, 8:9], in_=warm[:, 0:1], func=ACT.Abs_reciprocal_sqrt)
-        for w, src in enumerate((w2_scales, w3_scales)):
+        def load_weight_scales(w, src):
             nc.sync.dma_start(
                 ws_raw[0:16, 2 * H * w : 2 * H * (w + 1)].bitcast(I32).rearrange("q (a c) -> q a c", a=2),
                 src.bitcast(I32).rearrange("a q c -> q a c"),
@@ -72,16 +69,47 @@ def tile_list_equity_factor_exposures_kernel(
         def load_words(a):
             nc.sync.dma_start(word_win[a][:].bitcast(I32), tab_words[a].rearrange("p t i -> p (t i)").bitcast(I32))
 
-        load_words(0)
-        nc.sync.dma_start(
-            w2_raw[:].bitcast(I32).rearrange("p (a b) -> p a b", a=2), w2_words.bitcast(I32).rearrange("a p b -> p a b")
-        )
+        nc.sync.dma_start(lists[2][:], offs2)
+        load_weight_scales(0, w2_scales)
+        for part, count, row in ((0, 4, 16), (108, 4, 12), (12, 32, 0), (68, 32, 0), (44, 4, 4), (64, 4, 24)):
+            load_scale_rows(nc.sync, part, count, row)
+        nc.scalar.activation(out=warm[:, 8:9], in_=warm[:, 0:1], func=ACT.Abs_reciprocal_sqrt)
+        load_weight_scales(1, w3_scales)
         nc.sync.dma_start(
             w3_raw[:].bitcast(I32).rearrange("p (a c) -> p a c", a=2),
             w3_words.rearrange("a p c i -> a p (c i)").bitcast(I32).rearrange("a p c -> p a c"),
         )
-        load_words(1)
+        nc.sync.dma_start(
+            w2_raw[:].bitcast(I32).rearrange("p (a b) -> p a b", a=2), w2_words.bitcast(I32).rearrange("a p b -> p a b")
+        )
+        nc.sync.dma_start(lists[3][:], offs3)
+        load_words(0)
 
+        g_scale = {j: sb("g_scale%d" % j, S, U8) for j in (1, 2, 3)}
+        g_word = {(j, a): sb("g_word%d_%d" % (j, a), S, U32) for j in (1, 2, 3) for a in range(2)}
+
+        def gather(dst, window, j, lo, hi):
+            nc.vector.tensor_copy(dst[:, lo:hi], window[:].indirect(lists[j][:, lo // 16 : hi // 16]))
+
+        w2_ord = sb("w2_ord", 4 * H, U8)
+        w3_ord = sb("w3_ord", 2 * H, U32)
+
+        def reorder(dst, src, planes):
+            nc.vector.tensor_copy(
+                dst.bitcast(I32).rearrange("p (a t g e) -> p a t g e", a=planes, t=4, g=16),
+                src.bitcast(I32).rearrange("p (a g t e) -> p a t g e", a=planes, t=4, g=16),
+            )
+
+        gather(g_scale[2], scale_win, 2, 0, S)
+        nc.sync.dma_start(g2_pass0[0:112, :].bitcast(I32), g_scale[2][12:124, :].bitcast(I32))
+        reorder(ws_ord[0:16, :], ws_raw[0:16, :], 4)
+        for q in range(1, 4):
+            nc.sync.dma_start(ws_ord[32 * q : 32 * q + 4, :].bitcast(I32), ws_ord[4 * q : 4 * q + 4, :].bitcast(I32))
+        reorder(w3_ord[:], w3_raw[:], 2)
+        reorder(w2_ord[:], w2_raw[:], 2)
+        gather(g_scale[3], scale_win, 3, 0, S)
+
+        load_words(1)
         w1_rows = w1.rearrange("(a p j) c -> a p j c", a=2, j=4)
         w1_first = [sb("w1_first%d" % u, 2 * H, F32) for u in range(2)]
         w1_second = sb("w1_second", 4 * H, F32)
@@ -97,31 +125,7 @@ def tile_list_equity_factor_exposures_kernel(
         nc.sync.dma_start(fs[:], fscale.rearrange("(p c) -> p c", c=2))
         nc.sync.dma_start(fb[:], fbase.rearrange("(p c) -> p c", c=2))
 
-        g_scale = {j: sb("g_scale%d" % j, S, U8) for j in (1, 2, 3)}
-        g_word = {(j, a): sb("g_word%d_%d" % (j, a), S, U32) for j in (1, 2, 3) for a in range(2)}
-
-        def gather(dst, window, j, lo, hi):
-            nc.vector.tensor_copy(dst[:, lo:hi], window[:].indirect(lists[j][:, lo // 16 : hi // 16]))
-
-        w2_ord = sb("w2_ord", 4 * H, U8)
-        w3_ord = sb("w3_ord", 2 * H, U32)
-        ws_ord = sb("ws_ord", 4 * H, U8)
-
-        def reorder(engine, dst, src, planes):
-            engine.tensor_copy(
-                dst[:].bitcast(I32).rearrange("p (a t g e) -> p a t g e", a=planes, t=4, g=16),
-                src[:].bitcast(I32).rearrange("p (a g t e) -> p a t g e", a=planes, t=4, g=16),
-            )
-
-        gather(g_scale[2], scale_win, 2, 0, S)
-        nc.scalar.dma_start(g2_pass0[0:112, :].bitcast(I32), g_scale[2][12:124, :].bitcast(I32))
-        reorder(nc.vector, ws_ord, ws_raw, 4)
-        for q in range(1, 4):
-            nc.scalar.dma_start(ws_ord[32 * q : 32 * q + 4, :].bitcast(I32), ws_ord[4 * q : 4 * q + 4, :].bitcast(I32))
-        gather(g_scale[3], scale_win, 3, 0, S)
         gather(g_word[3, 0], word_win[0], 3, 0, S)
-        reorder(nc.vector, w3_ord, w3_raw, 2)
-        reorder(nc.vector, w2_ord, w2_raw, 2)
         gather(g_word[2, 0], word_win[0], 2, 0, S)
 
         w1_bf = [sb("w1_bf%d" % a, 4 * H, BF16) for a in range(2)]
@@ -138,51 +142,75 @@ def tile_list_equity_factor_exposures_kernel(
                 return g2_pass0[:, lo:hi]
             return g_scale[j][12 * (1 - a) : P, lo:hi]
 
-        w4_bf = sb("w4_bf", 4 * N, BF16)
+        def m_pass(acc, j, a, t, lo, hi):
+            col = H * a + P * t
+            if j == 2:
+                lhsT = w2_ord[:, 2 * col : 2 * (col + P)].bitcast(FP4X4)
+            else:
+                lhsT = w3_ord[:, col : col + P].bitcast(FP8X4)
+            scol = 2 * H * (j - 2) + col
+            nc.tensor.matmul_mx(
+                out=acc,
+                lhsT=lhsT,
+                lhsT_scale=ws_ord[:, scol : scol + P],
+                rhs=g_word[j, a][:, lo:hi].bitcast(FP8X4),
+                rhs_scale=table_scale(j, a, lo, hi),
+                start=(a == 0 and j == 3),
+                stop=(a == 1 and j == 2),
+            )
+
+        roots = [sb("root%d" % c, 4 * CHUNK, F32) for c in range(S // CHUNK)]
         damp = [sb("damp%d" % c, 4 * CHUNK, F32) for c in range(S // CHUNK)]
-        for half in range(2):
-            lo, hi = HALF * half, HALF * (half + 1)
-            gather(g_word[3, 1], word_win[1], 3, lo, hi)
-            gather(g_word[2, 1], word_win[1], 2, lo, hi)
-            m_banks = [bank(4 * half + t) for t in range(4)]
-            for a in range(2):
-                for j in (3, 2):
-                    for t in range(4):
-                        col = H * a + P * t
-                        if j == 2:
-                            lhsT = w2_ord[:, 2 * col : 2 * (col + P)].bitcast(FP4X4)
-                        else:
-                            lhsT = w3_ord[:, col : col + P].bitcast(FP8X4)
-                        scol = 2 * H * (j - 2) + col
-                        nc.tensor.matmul_mx(
-                            out=m_banks[t][:],
-                            lhsT=lhsT,
-                            lhsT_scale=ws_ord[:, scol : scol + P],
-                            rhs=g_word[j, a][:, lo:hi].bitcast(FP8X4),
-                            rhs_scale=table_scale(j, a, lo, hi),
-                            start=(a == 0 and j == 3),
-                            stop=(a == 1 and j == 2),
-                        )
-            m_abs = sb("m_abs%d" % half, 4 * HALF, F32)
-            for t in range(4):
-                nc.scalar.activation(out=m_abs[:, HALF * t : HALF * (t + 1)], in_=m_banks[t][:], func=ACT.Abs)
-            by_token = m_abs[:].rearrange("p (t n) -> p n t", t=4)
-            if half == 1:
-                nc.scalar.copy(
-                    w4_bf[:].rearrange("p (c m t) -> p c m t", c=2, t=4),
-                    w4_raw[:].rearrange("p (t m c) -> p c m t", c=2, t=4),
+        m_abs = [sb("m_abs%d" % half, 4 * HALF, F32) for half in range(2)]
+
+        gather(g_word[3, 1], word_win[1], 3, 0, HALF)
+        gather(g_word[2, 1], word_win[1], 2, 0, HALF)
+        m_banks = [bank(t) for t in range(4)]
+        for a in range(2):
+            for j in (3, 2):
+                for t in range(4):
+                    m_pass(m_banks[t][:], j, a, t, 0, HALF)
+        for t in range(4):
+            nc.scalar.activation(out=m_abs[0][:, HALF * t : HALF * (t + 1)], in_=m_banks[t][:], func=ACT.Abs)
+        dst = w1_bf[1][:].rearrange("p (t g i j) -> p t g i j", j=4, g=16, t=4)
+        src = w1_second[:].rearrange("p (j g t i) -> p t g i j", j=4, g=16, t=4)
+        for t in range(4):
+            nc.scalar.copy(dst[:, t], src[:, t])
+        by_token = m_abs[0][:].rearrange("p (t q n) -> p q t n", t=4, n=4)
+        for c in range(4):
+            nc.scalar.activation(
+                out=roots[c][:].rearrange("p (q n t) -> p q t n", t=4, n=4),
+                in_=by_token[:, 32 * c : 32 * (c + 1)],
+                func=ACT.Abs_reciprocal_sqrt,
+                bias=1.0,
+            )
+            nc.gpsimd.tensor_tensor(damp[c][:], roots[c][:], roots[c][:], MULT)
+
+        gather(g_word[3, 1], word_win[1], 3, HALF, S)
+        gather(g_word[2, 1], word_win[1], 2, HALF, S)
+        for c in range(4, 9):
+            if c < 8:
+                acc = bank(c)
+                for t in range(4):
+                    for a in range(2):
+                        for j in (3, 2):
+                            m_pass(acc[:, CHUNK * t : CHUNK * (t + 1)], j, a, t, CHUNK * c, CHUNK * (c + 1))
+                nc.scalar.activation(
+                    out=m_abs[1][:, HALF * (c - 4) : HALF * (c - 3)].rearrange("p (n t) -> p n t", t=4),
+                    in_=acc[:].rearrange("p (t n) -> p n t", t=4),
+                    func=ACT.Abs,
                 )
-            roots = [sb("root%d_%d" % (half, c), 4 * CHUNK, F32) for c in range(4)]
-            for c in range(5):
-                if c < 4:
-                    nc.scalar.activation(
-                        out=roots[c][:].rearrange("p (n t) -> p n t", t=4),
-                        in_=by_token[:, CHUNK * c : CHUNK * (c + 1), :],
-                        func=ACT.Abs_reciprocal_sqrt,
-                        bias=1.0,
-                    )
-                if c > 0:
-                    nc.scalar.activation(out=damp[4 * half + c - 1][:], in_=roots[c - 1][:], func=ACT.Square)
+            if c > 4:
+                nc.scalar.activation(
+                    out=roots[c - 1][:],
+                    in_=m_abs[1][:, HALF * (c - 5) : HALF * (c - 4)],
+                    func=ACT.Abs_reciprocal_sqrt,
+                    bias=1.0,
+                )
+                if c < 8:
+                    nc.gpsimd.tensor_tensor(damp[c - 1][:], roots[c - 1][:], roots[c - 1][:], MULT)
+                else:
+                    nc.scalar.activation(out=damp[c - 1][:], in_=roots[c - 1][:], func=ACT.Square)
 
         gather(g_scale[1], scale_win, 1, 0, S)
         gather(g_word[1, 0], word_win[0], 1, 0, S)
@@ -190,15 +218,20 @@ def tile_list_equity_factor_exposures_kernel(
         def quantize(codes, scales, values):
             nc.vector.quantize_mx(out=codes.bitcast(FP8X4), scales=scales, in_=values)
 
-        quantize(w1_codes[:, 0:H], w1_scale[:, 0:H], w1_bf[0][:])
-        nc.vector.tensor_copy(
-            w1_bf[1][:].rearrange("p (t g i j) -> p t g i j", j=4, g=16, t=4),
-            w1_second[:].rearrange("p (j g t i) -> p t g i j", j=4, g=16, t=4),
-        )
-        gather(g_word[1, 1], word_win[1], 1, 0, HALF)
-        quantize(w1_codes[:, H : 2 * H], w1_scale[:, H : 2 * H], w1_bf[1][:])
+        w4_bf = sb("w4_bf", 4 * N, BF16)
         w4_codes = sb("w4_codes", N, U32)
         w4_scale = sb("w4_scale", N, U8)
+        nc.gpsimd.tensor_scalar(
+            w4_bf[:].rearrange("p (c m t) -> p c m t", c=2, t=4),
+            w4_raw[:].rearrange("p (t m c) -> p c m t", c=2, t=4),
+            1.0,
+            0.0,
+            MULT,
+            ADD,
+        )
+        quantize(w1_codes[:, 0:H], w1_scale[:, 0:H], w1_bf[0][:])
+        quantize(w1_codes[:, H : 2 * H], w1_scale[:, H : 2 * H], w1_bf[1][:])
+        gather(g_word[1, 1], word_win[1], 1, 0, HALF)
         gather(g_word[1, 1], word_win[1], 1, HALF, S)
         quantize(w4_codes[:], w4_scale[:], w4_bf[:])
 
@@ -220,14 +253,14 @@ def tile_list_equity_factor_exposures_kernel(
                         stop=(a == 1),
                     )
 
-        h_bf = [sb("h_bf%d" % c, 4 * CHUNK, BF16) for c in range(S // CHUNK)]
+        h_bf = sb("h_bf", 4 * S, BF16)
         h_codes = sb("h_codes", S, U32)
         h_scale = sb("h_scale", S, U8)
         out_rows = out.rearrange("(p c) j -> p c j", c=2)
 
         def damped(c):
             nc.vector.tensor_tensor(
-                h_bf[c][:].rearrange("p (n t) -> p n t", t=4),
+                h_bf[:, HALF * c : HALF * (c + 1)].rearrange("p (n t) -> p n t", t=4),
                 a_banks[c][:].rearrange("p (t n) -> p n t", t=4),
                 damp[c][:].rearrange("p (n t) -> p n t", t=4),
                 MULT,
@@ -260,12 +293,11 @@ def tile_list_equity_factor_exposures_kernel(
                 )
             nc.sync.dma_start(out_rows[:, :, lo:hi], result[:].rearrange("p (c j) -> p c j", c=2))
 
-        groups = {3: (0, 512, (0, 1)), 5: (512, 768, (2, 2)), 6: (768, 896, (3, 3)), 7: (896, 1024, (4, 4))}
-        damped(0)
-        for c in range(S // CHUNK):
-            if c + 1 < S // CHUNK:
-                damped(c + 1)
-            lo, hi = CHUNK * c, CHUNK * (c + 1)
-            quantize(h_codes[:, lo:hi], h_scale[:, lo:hi], h_bf[c][:])
+        groups = {4: (0, 512, (0, 1)), 6: (512, 768, (2, 2)), 7: (768, 896, (3, 3)), 8: (896, 1024, (4, 4))}
+        for c in range(S // CHUNK + 1):
+            if c < S // CHUNK:
+                damped(c)
             if c in groups:
-                exposures(*groups[c])
+                lo, hi, banks = groups[c]
+                quantize(h_codes[:, lo:hi], h_scale[:, lo:hi], h_bf[:, 4 * lo : 4 * hi])
+                exposures(lo, hi, banks)

@@ -20,6 +20,7 @@ ADD = mybir.AluOpType.add
 P = 128
 HALF = 512
 CHUNK = 128
+ON_GPSIMD = (0, 1, 2, 3, 4, 5)
 
 
 def tile_list_equity_factor_exposures_kernel(
@@ -83,31 +84,42 @@ def tile_list_equity_factor_exposures_kernel(
             w2_raw[:].bitcast(I32).rearrange("p (a b) -> p a b", a=2), w2_words.bitcast(I32).rearrange("a p b -> p a b")
         )
         nc.sync.dma_start(lists[3][:], offs3)
+        nc.sync.dma_start(lists[1][:], offs)
         load_words(0)
 
         g_scale = {j: sb("g_scale%d" % j, S, U8) for j in (1, 2, 3)}
-        g_word = {(j, a): sb("g_word%d_%d" % (j, a), S, U32) for j in (1, 2, 3) for a in range(2)}
+        g_word = {}
 
         def gather(dst, window, j, lo, hi):
-            nc.vector.tensor_copy(dst[:, lo:hi], window[:].indirect(lists[j][:, lo // 16 : hi // 16]))
+            nc.vector.tensor_copy(dst, window[:].indirect(lists[j][:, lo // 16 : hi // 16]))
+
+        def gather_words(j, a, lo, hi, slot):
+            dst = sb(slot, hi - lo, U32)
+            gather(dst[:], word_win[a], j, lo, hi)
+            for half in range(lo // HALF, hi // HALF):
+                g_word[j, a, half] = dst[:, HALF * half - lo : HALF * (half + 1) - lo]
+
+        def table_words(j, a, lo, hi):
+            return g_word[j, a, lo // HALF][:, lo % HALF : lo % HALF + hi - lo].bitcast(FP8X4)
 
         w2_ord = sb("w2_ord", 4 * H, U8)
         w3_ord = sb("w3_ord", 2 * H, U32)
 
         def reorder(dst, src, planes):
-            nc.vector.tensor_copy(
+            nc.gpsimd.tensor_copy(
                 dst.bitcast(I32).rearrange("p (a t g e) -> p a t g e", a=planes, t=4, g=16),
                 src.bitcast(I32).rearrange("p (a g t e) -> p a t g e", a=planes, t=4, g=16),
             )
 
-        gather(g_scale[2], scale_win, 2, 0, S)
-        nc.sync.dma_start(g2_pass0[0:112, :].bitcast(I32), g_scale[2][12:124, :].bitcast(I32))
+        gather(g_scale[2][:], scale_win, 2, 0, S)
         reorder(ws_ord[0:16, :], ws_raw[0:16, :], 4)
         for q in range(1, 4):
             nc.sync.dma_start(ws_ord[32 * q : 32 * q + 4, :].bitcast(I32), ws_ord[4 * q : 4 * q + 4, :].bitcast(I32))
+        nc.sync.dma_start(g2_pass0[0:112, :].bitcast(I32), g_scale[2][12:124, :].bitcast(I32))
         reorder(w3_ord[:], w3_raw[:], 2)
         reorder(w2_ord[:], w2_raw[:], 2)
-        gather(g_scale[3], scale_win, 3, 0, S)
+        gather(g_scale[3][:], scale_win, 3, 0, S)
+        gather(g_scale[1][:], scale_win, 1, 0, S)
 
         load_words(1)
         w1_rows = w1.rearrange("(a p j) c -> a p j c", a=2, j=4)
@@ -117,7 +129,6 @@ def tile_list_equity_factor_exposures_kernel(
             nc.sync.dma_start(
                 w1_first[u][:].rearrange("p (j c) -> p j c", j=4), w1_rows[0][:, :, 256 * u : 256 * (u + 1)]
             )
-        nc.sync.dma_start(lists[1][:], offs)
         nc.sync.dma_start(w1_second[:].rearrange("p (j c) -> p j c", j=4), w1_rows[1])
         w4_rows = w4.rearrange("(g t i) n -> t g i n", t=4, i=8)
         for t in range(4):
@@ -125,8 +136,8 @@ def tile_list_equity_factor_exposures_kernel(
         nc.sync.dma_start(fs[:], fscale.rearrange("(p c) -> p c", c=2))
         nc.sync.dma_start(fb[:], fbase.rearrange("(p c) -> p c", c=2))
 
-        gather(g_word[3, 0], word_win[0], 3, 0, S)
-        gather(g_word[2, 0], word_win[0], 2, 0, S)
+        gather_words(3, 0, 0, S, "words30")
+        gather_words(2, 0, 0, S, "words20")
 
         w1_bf = [sb("w1_bf%d" % a, 4 * H, BF16) for a in range(2)]
         w1_codes = sb("w1_codes", 2 * H, U32)
@@ -153,7 +164,7 @@ def tile_list_equity_factor_exposures_kernel(
                 out=acc,
                 lhsT=lhsT,
                 lhsT_scale=ws_ord[:, scol : scol + P],
-                rhs=g_word[j, a][:, lo:hi].bitcast(FP8X4),
+                rhs=table_words(j, a, lo, hi),
                 rhs_scale=table_scale(j, a, lo, hi),
                 start=(a == 0 and j == 3),
                 stop=(a == 1 and j == 2),
@@ -163,82 +174,58 @@ def tile_list_equity_factor_exposures_kernel(
         damp = [sb("damp%d" % c, 4 * CHUNK, F32) for c in range(S // CHUNK)]
         m_abs = [sb("m_abs%d" % half, 4 * HALF, F32) for half in range(2)]
 
-        gather(g_word[3, 1], word_win[1], 3, 0, HALF)
-        gather(g_word[2, 1], word_win[1], 2, 0, HALF)
-        m_banks = [bank(t) for t in range(4)]
-        for a in range(2):
-            for j in (3, 2):
+        w4_bf = sb("w4_bf", 4 * N, BF16)
+        for half in range(2):
+            lo, hi = HALF * half, HALF * (half + 1)
+            gather_words(3, 1, lo, hi, ("slot_a", "words31")[half])
+            gather_words(2, 1, lo, hi, ("slot_b", "words21")[half])
+            m_banks = [bank(t) for t in range(4)]
+            for a in range(2):
+                for j in (3, 2):
+                    for t in range(4):
+                        m_pass(m_banks[t][:], j, a, t, lo, hi)
+            for t in range(4):
+                nc.scalar.activation(out=m_abs[half][:, HALF * t : HALF * (t + 1)], in_=m_banks[t][:], func=ACT.Abs)
+            if half == 0:
+                dst = w1_bf[1][:].rearrange("p (t g i j) -> p t g i j", j=4, g=16, t=4)
+                src = w1_second[:].rearrange("p (j g t i) -> p t g i j", j=4, g=16, t=4)
                 for t in range(4):
-                    m_pass(m_banks[t][:], j, a, t, 0, HALF)
-        for t in range(4):
-            nc.scalar.activation(out=m_abs[0][:, HALF * t : HALF * (t + 1)], in_=m_banks[t][:], func=ACT.Abs)
-        dst = w1_bf[1][:].rearrange("p (t g i j) -> p t g i j", j=4, g=16, t=4)
-        src = w1_second[:].rearrange("p (j g t i) -> p t g i j", j=4, g=16, t=4)
-        for t in range(4):
-            nc.scalar.copy(dst[:, t], src[:, t])
-        by_token = m_abs[0][:].rearrange("p (t q n) -> p q t n", t=4, n=4)
-        for c in range(4):
-            nc.scalar.activation(
-                out=roots[c][:].rearrange("p (q n t) -> p q t n", t=4, n=4),
-                in_=by_token[:, 32 * c : 32 * (c + 1)],
-                func=ACT.Abs_reciprocal_sqrt,
-                bias=1.0,
-            )
-            nc.gpsimd.tensor_tensor(damp[c][:], roots[c][:], roots[c][:], MULT)
-
-        gather(g_word[3, 1], word_win[1], 3, HALF, S)
-        gather(g_word[2, 1], word_win[1], 2, HALF, S)
-        for c in range(4, 9):
-            if c < 8:
-                acc = bank(c)
-                for t in range(4):
-                    for a in range(2):
-                        for j in (3, 2):
-                            m_pass(acc[:, CHUNK * t : CHUNK * (t + 1)], j, a, t, CHUNK * c, CHUNK * (c + 1))
-                nc.scalar.activation(
-                    out=m_abs[1][:, HALF * (c - 4) : HALF * (c - 3)].rearrange("p (n t) -> p n t", t=4),
-                    in_=acc[:].rearrange("p (t n) -> p n t", t=4),
-                    func=ACT.Abs,
-                )
-            if c > 4:
-                nc.scalar.activation(
-                    out=roots[c - 1][:],
-                    in_=m_abs[1][:, HALF * (c - 5) : HALF * (c - 4)],
-                    func=ACT.Abs_reciprocal_sqrt,
-                    bias=1.0,
-                )
-                if c < 8:
-                    nc.gpsimd.tensor_tensor(damp[c - 1][:], roots[c - 1][:], roots[c - 1][:], MULT)
-                else:
+                    nc.gpsimd.tensor_scalar(dst[:, t], src[:, t], 1.0, 0.0, MULT, ADD)
+            by_token = m_abs[half][:].rearrange("p (t q n) -> p q t n", t=4, n=4)
+            for c in range(4 * half, 4 * half + 5):
+                if c < 4 * half + 4:
+                    nc.scalar.activation(
+                        out=roots[c][:].rearrange("p (q n t) -> p q t n", t=4, n=4),
+                        in_=by_token[:, 32 * (c % 4) : 32 * (c % 4 + 1)],
+                        func=ACT.Abs_reciprocal_sqrt,
+                        bias=1.0,
+                    )
+                    if c in ON_GPSIMD:
+                        nc.gpsimd.tensor_tensor(damp[c][:], roots[c][:], roots[c][:], MULT)
+                if c > 4 * half and c - 1 not in ON_GPSIMD:
                     nc.scalar.activation(out=damp[c - 1][:], in_=roots[c - 1][:], func=ACT.Square)
 
-        gather(g_scale[1], scale_win, 1, 0, S)
-        gather(g_word[1, 0], word_win[0], 1, 0, S)
+        gather_words(1, 0, 0, HALF, "slot_a")
+        gather_words(1, 0, HALF, S, "slot_b")
 
         def quantize(codes, scales, values):
             nc.vector.quantize_mx(out=codes.bitcast(FP8X4), scales=scales, in_=values)
 
-        w4_bf = sb("w4_bf", 4 * N, BF16)
         w4_codes = sb("w4_codes", N, U32)
         w4_scale = sb("w4_scale", N, U8)
-        nc.gpsimd.tensor_scalar(
-            w4_bf[:].rearrange("p (c m t) -> p c m t", c=2, t=4),
-            w4_raw[:].rearrange("p (t m c) -> p c m t", c=2, t=4),
-            1.0,
-            0.0,
-            MULT,
-            ADD,
-        )
         quantize(w1_codes[:, 0:H], w1_scale[:, 0:H], w1_bf[0][:])
         quantize(w1_codes[:, H : 2 * H], w1_scale[:, H : 2 * H], w1_bf[1][:])
-        gather(g_word[1, 1], word_win[1], 1, 0, HALF)
-        gather(g_word[1, 1], word_win[1], 1, HALF, S)
+        gather_words(1, 1, 0, HALF, "words11a")
+        nc.vector.tensor_copy(
+            w4_bf[:].rearrange("p (c m t) -> p c m t", c=2, t=4), w4_raw[:].rearrange("p (t m c) -> p c m t", c=2, t=4)
+        )
+        gather_words(1, 1, HALF, S, "words11b")
         quantize(w4_codes[:], w4_scale[:], w4_bf[:])
 
         a_banks = []
         for c in range(S // CHUNK):
             lo, hi = CHUNK * c, CHUNK * (c + 1)
-            acc = bank(c)
+            acc = bank((c + 4) % 8)
             a_banks.append(acc)
             for t in range(4):
                 for a in range(2):
@@ -247,7 +234,7 @@ def tile_list_equity_factor_exposures_kernel(
                         out=acc[:, CHUNK * t : CHUNK * (t + 1)],
                         lhsT=w1_codes[:, col : col + P].bitcast(FP8X4),
                         lhsT_scale=w1_scale[:, col : col + P],
-                        rhs=g_word[1, a][:, lo:hi].bitcast(FP8X4),
+                        rhs=table_words(1, a, lo, hi),
                         rhs_scale=table_scale(1, a, lo, hi),
                         start=(a == 0),
                         stop=(a == 1),
@@ -293,7 +280,7 @@ def tile_list_equity_factor_exposures_kernel(
                 )
             nc.sync.dma_start(out_rows[:, :, lo:hi], result[:].rearrange("p (c j) -> p c j", c=2))
 
-        groups = {4: (0, 512, (0, 1)), 6: (512, 768, (2, 2)), 7: (768, 896, (3, 3)), 8: (896, 1024, (4, 4))}
+        groups = {4: (0, 512, (4, 5)), 6: (512, 768, (6, 6)), 7: (768, 896, (7, 7)), 8: (896, 1024, (0, 0))}
         for c in range(S // CHUNK + 1):
             if c < S // CHUNK:
                 damped(c)

@@ -20,7 +20,7 @@ ADD = mybir.AluOpType.add
 P = 128
 HALF = 512
 CHUNK = 128
-ON_GPSIMD = (0, 1, 2, 3, 4, 5)
+CHUNKS = S // CHUNK
 
 
 def tile_list_equity_factor_exposures_kernel(
@@ -42,24 +42,21 @@ def tile_list_equity_factor_exposures_kernel(
         word_win = [sb("word_win%d" % a, T, U32) for a in range(2)]
         ws_raw = sb("ws_raw", 4 * H, U8)
         ws_ord = sb("ws_ord", 4 * H, U8)
-        g2_pass0 = sb("g2_pass0", S, U8)
+        planes23 = sb("planes23", 4 * S, U8)
         warm = sb("warm", 16, F32)
         fs = sb("fs", 2, F32)
         fb = sb("fb", 2, F32)
 
-        nc.vector.memset(scale_win[:, 0 : T // 2].bitcast(I32), 0)
-        nc.gpsimd.memset(scale_win[:, T // 2 : T].bitcast(I32), 0)
+        nc.vector.memset(scale_win[64:128, :].bitcast(I32), 0)
+        nc.vector.memset(scale_win[32:64, :].bitcast(I32), 0)
         nc.gpsimd.memset(warm[:, 0:8], 1.0)
-        nc.gpsimd.memset(ws_ord[:].bitcast(I32), 0)
-        nc.gpsimd.memset(g2_pass0[:].bitcast(I32), 0)
+        nc.vector.memset(planes23[:].bitcast(I32), 0)
+        nc.vector.memset(ws_ord[:].bitcast(I32), 0)
+        nc.scalar.activation(out=warm[:, 8:9], in_=warm[:, 0:1], func=ACT.Abs_reciprocal_sqrt)
 
         w2_raw = sb("w2_raw", 4 * H, U8)
         w3_raw = sb("w3_raw", 2 * H, U32)
         w4_raw = sb("w4_raw", 4 * N, F32)
-        scale_rows = tab_scales.rearrange("a q t -> (a q) t").bitcast(I32)
-
-        def load_scale_rows(queue, part, count, row):
-            queue.dma_start(scale_win[part : part + count, :].bitcast(I32), scale_rows[row : row + count, :])
 
         def load_weight_scales(w, src):
             nc.sync.dma_start(
@@ -71,11 +68,7 @@ def tile_list_equity_factor_exposures_kernel(
             nc.sync.dma_start(word_win[a][:].bitcast(I32), tab_words[a].rearrange("p t i -> p (t i)").bitcast(I32))
 
         nc.sync.dma_start(lists[2][:], offs2)
-        load_weight_scales(0, w2_scales)
-        for part, count, row in ((0, 4, 16), (108, 4, 12), (12, 32, 0), (68, 32, 0), (44, 4, 4), (64, 4, 24)):
-            load_scale_rows(nc.sync, part, count, row)
-        nc.scalar.activation(out=warm[:, 8:9], in_=warm[:, 0:1], func=ACT.Abs_reciprocal_sqrt)
-        load_weight_scales(1, w3_scales)
+        nc.sync.dma_start(scale_win[0:32, :].bitcast(I32), tab_scales.bitcast(I32).rearrange("a q t -> q a t"))
         nc.sync.dma_start(
             w3_raw[:].bitcast(I32).rearrange("p (a c) -> p a c", a=2),
             w3_words.rearrange("a p c i -> a p (c i)").bitcast(I32).rearrange("a p c -> p a c"),
@@ -83,11 +76,24 @@ def tile_list_equity_factor_exposures_kernel(
         nc.sync.dma_start(
             w2_raw[:].bitcast(I32).rearrange("p (a b) -> p a b", a=2), w2_words.bitcast(I32).rearrange("a p b -> p a b")
         )
+        load_weight_scales(0, w2_scales)
         nc.sync.dma_start(lists[3][:], offs3)
-        nc.sync.dma_start(lists[1][:], offs)
+        load_weight_scales(1, w3_scales)
         load_words(0)
+        load_words(1)
+        nc.sync.dma_start(lists[1][:], offs)
+        w1_rows = w1.rearrange("(a p j) c -> a p j c", a=2, j=4)
+        w1_raw = [sb("w1_raw%d" % a, 4 * H, F32) for a in range(2)]
+        nc.sync.dma_start(w1_raw[0][:].rearrange("p (j c) -> p j c", j=4), w1_rows[0])
+        w4_rows = w4.rearrange("(g t i) n -> t g i n", t=4, i=8)
+        for t in range(4):
+            nc.sync.dma_start(w4_raw[:, N * t : N * (t + 1)], w4_rows[t])
+        nc.sync.dma_start(w1_raw[1][:].rearrange("p (j c) -> p j c", j=4), w1_rows[1])
+        nc.sync.dma_start(fs[:], fscale.rearrange("(p c) -> p c", c=2))
+        nc.sync.dma_start(fb[:], fbase.rearrange("(p c) -> p c", c=2))
 
-        g_scale = {j: sb("g_scale%d" % j, S, U8) for j in (1, 2, 3)}
+        picked23 = sb("picked23", 2 * S, U8)
+        picked1 = sb("picked1", S, U8)
         g_word = {}
 
         def gather(dst, window, j, lo, hi):
@@ -99,145 +105,128 @@ def tile_list_equity_factor_exposures_kernel(
             for half in range(lo // HALF, hi // HALF):
                 g_word[j, a, half] = dst[:, HALF * half - lo : HALF * (half + 1) - lo]
 
-        def table_words(j, a, lo, hi):
-            return g_word[j, a, lo // HALF][:, lo % HALF : lo % HALF + hi - lo].bitcast(FP8X4)
+        def table_words(j, a, c):
+            lo = CHUNK * c
+            return g_word[j, a, lo // HALF][:, lo % HALF : lo % HALF + CHUNK].bitcast(FP8X4)
+
+        def spread(queue, planes, picked):
+            for q in range(4):
+                queue.dma_start(
+                    planes[32 * q : 32 * q + 4].bitcast(I32).rearrange("r (a n) -> r a n", a=2),
+                    picked[8 * q : 8 * q + 8, :].bitcast(I32),
+                )
+
+        def table_scale(j, a, c):
+            lo = CHUNK * c
+            if j == 1:
+                return planes23[:, S * a + lo : S * a + lo + CHUNK]
+            col = 2 * S * a + S * (j - 2) + lo
+            return planes23[:, col : col + CHUNK]
 
         w2_ord = sb("w2_ord", 4 * H, U8)
         w3_ord = sb("w3_ord", 2 * H, U32)
 
         def reorder(dst, src, planes):
-            nc.gpsimd.tensor_copy(
+            nc.vector.tensor_copy(
                 dst.bitcast(I32).rearrange("p (a t g e) -> p a t g e", a=planes, t=4, g=16),
                 src.bitcast(I32).rearrange("p (a g t e) -> p a t g e", a=planes, t=4, g=16),
             )
 
-        gather(g_scale[2][:], scale_win, 2, 0, S)
+        gather(picked23[:, 0:S], scale_win, 2, 0, S)
+        gather(picked23[:, S : 2 * S], scale_win, 3, 0, S)
+        spread(nc.scalar, planes23[:], picked23)
         reorder(ws_ord[0:16, :], ws_raw[0:16, :], 4)
         for q in range(1, 4):
-            nc.sync.dma_start(ws_ord[32 * q : 32 * q + 4, :].bitcast(I32), ws_ord[4 * q : 4 * q + 4, :].bitcast(I32))
-        nc.sync.dma_start(g2_pass0[0:112, :].bitcast(I32), g_scale[2][12:124, :].bitcast(I32))
+            nc.scalar.dma_start(ws_ord[32 * q : 32 * q + 4, :].bitcast(I32), ws_ord[4 * q : 4 * q + 4, :].bitcast(I32))
         reorder(w3_ord[:], w3_raw[:], 2)
         reorder(w2_ord[:], w2_raw[:], 2)
-        gather(g_scale[3][:], scale_win, 3, 0, S)
-        gather(g_scale[1][:], scale_win, 1, 0, S)
 
-        load_words(1)
-        w1_rows = w1.rearrange("(a p j) c -> a p j c", a=2, j=4)
-        w1_first = [sb("w1_first%d" % u, 2 * H, F32) for u in range(2)]
-        w1_second = sb("w1_second", 4 * H, F32)
-        for u in range(2):
-            nc.sync.dma_start(
-                w1_first[u][:].rearrange("p (j c) -> p j c", j=4), w1_rows[0][:, :, 256 * u : 256 * (u + 1)]
-            )
-        nc.sync.dma_start(w1_second[:].rearrange("p (j c) -> p j c", j=4), w1_rows[1])
-        w4_rows = w4.rearrange("(g t i) n -> t g i n", t=4, i=8)
-        for t in range(4):
-            nc.sync.dma_start(w4_raw[:, N * t : N * (t + 1)], w4_rows[t])
-        nc.sync.dma_start(fs[:], fscale.rearrange("(p c) -> p c", c=2))
-        nc.sync.dma_start(fb[:], fbase.rearrange("(p c) -> p c", c=2))
+        def m_passes(acc, j, a, c):
+            for t in range(4):
+                col = H * a + P * t
+                if j == 2:
+                    lhsT = w2_ord[:, 2 * col : 2 * (col + P)].bitcast(FP4X4)
+                else:
+                    lhsT = w3_ord[:, col : col + P].bitcast(FP8X4)
+                scol = 2 * H * (j - 2) + col
+                nc.tensor.matmul_mx(
+                    out=acc[:, CHUNK * t : CHUNK * (t + 1)],
+                    lhsT=lhsT,
+                    lhsT_scale=ws_ord[:, scol : scol + P],
+                    rhs=table_words(j, a, c),
+                    rhs_scale=table_scale(j, a, c),
+                    start=(a == 0 and j == 3 and t == 0),
+                    stop=(a == 1 and j == 2 and t == 3),
+                )
 
-        gather_words(3, 0, 0, S, "words30")
-        gather_words(2, 0, 0, S, "words20")
+        m_banks = [bank(c) for c in range(CHUNKS)]
+        for a in range(2):
+            for half in range(2):
+                for j in (3, 2):
+                    gather_words(j, a, HALF * half, HALF * (half + 1), "words%d%d%d" % (j, a, half))
+                    for c in range(4 * half, 4 * half + 4):
+                        m_passes(m_banks[c], j, a, c)
+
+        gather(picked1[:], scale_win, 1, 0, S)
+        spread(nc.sync, planes23[:, 0 : 2 * S], picked1)
+        gather_words(1, 0, 0, S, "words10")
+        gather_words(1, 1, 0, HALF, "words110")
 
         w1_bf = [sb("w1_bf%d" % a, 4 * H, BF16) for a in range(2)]
         w1_codes = sb("w1_codes", 2 * H, U32)
         w1_scale = sb("w1_scale", 2 * H, U8)
-        dst = w1_bf[0][:].rearrange("p (t g i j) -> p t g i j", j=4, g=16, t=4)
-        for u in range(2):
-            src = w1_first[u][:].rearrange("p (j g t i) -> p t g i j", j=4, g=8, t=4)
+
+        def round_w1(copy, a):
+            dst = w1_bf[a][:].rearrange("p (t g u i j) -> p t g u j i", t=4, g=16, u=2, j=4)
+            src = w1_raw[a][:].rearrange("p (j g t u i) -> p t g u j i", t=4, g=16, u=2, j=4)
             for t in range(4):
-                nc.scalar.copy(dst[:, t, 8 * u : 8 * (u + 1)], src[:, t])
-
-        def table_scale(j, a, lo, hi):
-            if j == 2 and a == 0:
-                return g2_pass0[:, lo:hi]
-            return g_scale[j][12 * (1 - a) : P, lo:hi]
-
-        def m_pass(acc, j, a, t, lo, hi):
-            col = H * a + P * t
-            if j == 2:
-                lhsT = w2_ord[:, 2 * col : 2 * (col + P)].bitcast(FP4X4)
-            else:
-                lhsT = w3_ord[:, col : col + P].bitcast(FP8X4)
-            scol = 2 * H * (j - 2) + col
-            nc.tensor.matmul_mx(
-                out=acc,
-                lhsT=lhsT,
-                lhsT_scale=ws_ord[:, scol : scol + P],
-                rhs=table_words(j, a, lo, hi),
-                rhs_scale=table_scale(j, a, lo, hi),
-                start=(a == 0 and j == 3),
-                stop=(a == 1 and j == 2),
-            )
-
-        roots = [sb("root%d" % c, 4 * CHUNK, F32) for c in range(S // CHUNK)]
-        damp = [sb("damp%d" % c, 4 * CHUNK, F32) for c in range(S // CHUNK)]
-        m_abs = [sb("m_abs%d" % half, 4 * HALF, F32) for half in range(2)]
-
-        w4_bf = sb("w4_bf", 4 * N, BF16)
-        for half in range(2):
-            lo, hi = HALF * half, HALF * (half + 1)
-            gather_words(3, 1, lo, hi, ("slot_a", "words31")[half])
-            gather_words(2, 1, lo, hi, ("slot_b", "words21")[half])
-            m_banks = [bank(t) for t in range(4)]
-            for a in range(2):
-                for j in (3, 2):
-                    for t in range(4):
-                        m_pass(m_banks[t][:], j, a, t, lo, hi)
-            for t in range(4):
-                nc.scalar.activation(out=m_abs[half][:, HALF * t : HALF * (t + 1)], in_=m_banks[t][:], func=ACT.Abs)
-            if half == 0:
-                dst = w1_bf[1][:].rearrange("p (t g i j) -> p t g i j", j=4, g=16, t=4)
-                src = w1_second[:].rearrange("p (j g t i) -> p t g i j", j=4, g=16, t=4)
-                for t in range(4):
-                    nc.gpsimd.tensor_scalar(dst[:, t], src[:, t], 1.0, 0.0, MULT, ADD)
-            by_token = m_abs[half][:].rearrange("p (t q n) -> p q t n", t=4, n=4)
-            for c in range(4 * half, 4 * half + 5):
-                if c < 4 * half + 4:
-                    nc.scalar.activation(
-                        out=roots[c][:].rearrange("p (q n t) -> p q t n", t=4, n=4),
-                        in_=by_token[:, 32 * (c % 4) : 32 * (c % 4 + 1)],
-                        func=ACT.Abs_reciprocal_sqrt,
-                        bias=1.0,
-                    )
-                    if c in ON_GPSIMD:
-                        nc.gpsimd.tensor_tensor(damp[c][:], roots[c][:], roots[c][:], MULT)
-                if c > 4 * half and c - 1 not in ON_GPSIMD:
-                    nc.scalar.activation(out=damp[c - 1][:], in_=roots[c - 1][:], func=ACT.Square)
-
-        gather_words(1, 0, 0, HALF, "slot_a")
-        gather_words(1, 0, HALF, S, "slot_b")
+                copy(dst[:, t], src[:, t])
 
         def quantize(codes, scales, values):
             nc.vector.quantize_mx(out=codes.bitcast(FP8X4), scales=scales, in_=values)
 
+        round_w1(nc.scalar.copy, 0)
+        w4_bf = sb("w4_bf", 4 * N, BF16)
         w4_codes = sb("w4_codes", N, U32)
         w4_scale = sb("w4_scale", N, U8)
+        nc.vector.tensor_copy(
+            w4_bf[:].rearrange("p (c u i t) -> p u t i c", c=2, i=2, t=4),
+            w4_raw[:].rearrange("p (t u i c) -> p u t i c", c=2, i=2, t=4),
+        )
+        round_w1(nc.vector.tensor_copy, 1)
+        quantize(w4_codes[:], w4_scale[:], w4_bf[:])
         quantize(w1_codes[:, 0:H], w1_scale[:, 0:H], w1_bf[0][:])
         quantize(w1_codes[:, H : 2 * H], w1_scale[:, H : 2 * H], w1_bf[1][:])
-        gather_words(1, 1, 0, HALF, "words11a")
-        nc.vector.tensor_copy(
-            w4_bf[:].rearrange("p (c m t) -> p c m t", c=2, t=4), w4_raw[:].rearrange("p (t m c) -> p c m t", c=2, t=4)
-        )
-        gather_words(1, 1, HALF, S, "words11b")
-        quantize(w4_codes[:], w4_scale[:], w4_bf[:])
+        gather_words(1, 1, HALF, S, "w1_bf1")
+
+        damp = []
+        for c in range(CHUNKS):
+            m_abs = sb("m_abs%d" % c, HALF, F32)
+            root = sb("root%d" % c, HALF, F32)
+            damp.append(sb("damp%d" % c, HALF, F32))
+            nc.scalar.activation(
+                out=m_abs[:].rearrange("p (n t) -> p n t", t=4),
+                in_=m_banks[c][:].rearrange("p (t n) -> p n t", t=4),
+                func=ACT.Abs,
+            )
+            nc.scalar.activation(out=root[:], in_=m_abs[:], func=ACT.Abs_reciprocal_sqrt, bias=1.0)
+            nc.scalar.activation(out=damp[c][:], in_=root[:], func=ACT.Square)
 
         a_banks = []
-        for c in range(S // CHUNK):
-            lo, hi = CHUNK * c, CHUNK * (c + 1)
-            acc = bank((c + 4) % 8)
+        for c in range(CHUNKS):
+            acc = bank(c)
             a_banks.append(acc)
-            for t in range(4):
-                for a in range(2):
+            for a in range(2):
+                for t in range(4):
                     col = H * a + P * t
                     nc.tensor.matmul_mx(
                         out=acc[:, CHUNK * t : CHUNK * (t + 1)],
                         lhsT=w1_codes[:, col : col + P].bitcast(FP8X4),
                         lhsT_scale=w1_scale[:, col : col + P],
-                        rhs=table_words(1, a, lo, hi),
-                        rhs_scale=table_scale(1, a, lo, hi),
-                        start=(a == 0),
-                        stop=(a == 1),
+                        rhs=table_words(1, a, c),
+                        rhs_scale=table_scale(1, a, c),
+                        start=(a == 0 and t == 0),
+                        stop=(a == 1 and t == 3),
                     )
 
         h_bf = sb("h_bf", 4 * S, BF16)
@@ -280,9 +269,9 @@ def tile_list_equity_factor_exposures_kernel(
                 )
             nc.sync.dma_start(out_rows[:, :, lo:hi], result[:].rearrange("p (c j) -> p c j", c=2))
 
-        groups = {4: (0, 512, (4, 5)), 6: (512, 768, (6, 6)), 7: (768, 896, (7, 7)), 8: (896, 1024, (0, 0))}
-        for c in range(S // CHUNK + 1):
-            if c < S // CHUNK:
+        groups = {4: (0, 512, (0, 1)), 6: (512, 768, (2, 2)), 7: (768, 896, (3, 3)), 8: (896, 1024, (4, 4))}
+        for c in range(CHUNKS + 1):
+            if c < CHUNKS:
                 damped(c)
             if c in groups:
                 lo, hi, banks = groups[c]

@@ -50,8 +50,8 @@ def tile_list_equity_factor_exposures_kernel(
         nc.vector.memset(scale_win[64:128, :].bitcast(I32), 0)
         nc.vector.memset(scale_win[32:64, :].bitcast(I32), 0)
         nc.gpsimd.memset(warm[:, 0:8], 1.0)
-        nc.vector.memset(planes23[:].bitcast(I32), 0)
         nc.vector.memset(ws_ord[:].bitcast(I32), 0)
+        nc.vector.memset(planes23[:].bitcast(I32), 0)
         nc.scalar.activation(out=warm[:, 8:9], in_=warm[:, 0:1], func=ACT.Abs_reciprocal_sqrt)
 
         w2_raw = sb("w2_raw", 4 * H, U8)
@@ -59,7 +59,7 @@ def tile_list_equity_factor_exposures_kernel(
         w4_raw = sb("w4_raw", 4 * N, F32)
 
         def load_weight_scales(w, src):
-            nc.sync.dma_start(
+            nc.scalar.dma_start(
                 ws_raw[0:16, 2 * H * w : 2 * H * (w + 1)].bitcast(I32).rearrange("q (a c) -> q a c", a=2),
                 src.bitcast(I32).rearrange("a q c -> q a c"),
             )
@@ -69,6 +69,9 @@ def tile_list_equity_factor_exposures_kernel(
 
         nc.sync.dma_start(lists[2][:], offs2)
         nc.sync.dma_start(scale_win[0:32, :].bitcast(I32), tab_scales.bitcast(I32).rearrange("a q t -> q a t"))
+        nc.sync.dma_start(lists[3][:], offs3)
+        load_weight_scales(0, w2_scales)
+        load_weight_scales(1, w3_scales)
         nc.sync.dma_start(
             w3_raw[:].bitcast(I32).rearrange("p (a c) -> p a c", a=2),
             w3_words.rearrange("a p c i -> a p (c i)").bitcast(I32).rearrange("a p c -> p a c"),
@@ -76,9 +79,6 @@ def tile_list_equity_factor_exposures_kernel(
         nc.sync.dma_start(
             w2_raw[:].bitcast(I32).rearrange("p (a b) -> p a b", a=2), w2_words.bitcast(I32).rearrange("a p b -> p a b")
         )
-        load_weight_scales(0, w2_scales)
-        nc.sync.dma_start(lists[3][:], offs3)
-        load_weight_scales(1, w3_scales)
         load_words(0)
         load_words(1)
         nc.sync.dma_start(lists[1][:], offs)
@@ -132,12 +132,12 @@ def tile_list_equity_factor_exposures_kernel(
                 src.bitcast(I32).rearrange("p (a g t e) -> p a t g e", a=planes, t=4, g=16),
             )
 
-        gather(picked23[:, 0:S], scale_win, 2, 0, S)
-        gather(picked23[:, S : 2 * S], scale_win, 3, 0, S)
-        spread(nc.scalar, planes23[:], picked23)
         reorder(ws_ord[0:16, :], ws_raw[0:16, :], 4)
         for q in range(1, 4):
             nc.scalar.dma_start(ws_ord[32 * q : 32 * q + 4, :].bitcast(I32), ws_ord[4 * q : 4 * q + 4, :].bitcast(I32))
+        gather(picked23[:, 0:S], scale_win, 2, 0, S)
+        gather(picked23[:, S : 2 * S], scale_win, 3, 0, S)
+        spread(nc.scalar, planes23[:], picked23)
         reorder(w3_ord[:], w3_raw[:], 2)
         reorder(w2_ord[:], w2_raw[:], 2)
 
@@ -159,22 +159,31 @@ def tile_list_equity_factor_exposures_kernel(
                     stop=(a == 1 and j == 2 and t == 3),
                 )
 
-        m_banks = [bank(c) for c in range(CHUNKS)]
+        m_abs = [sb("m_abs%d" % c, HALF, F32) for c in range(CHUNKS)]
+        root = [sb("root%d" % c, HALF, F32) for c in range(CHUNKS)]
+        damp = [sb("damp%d" % c, HALF, F32) for c in range(CHUNKS)]
+
+        def damping_step(step, acc):
+            if step < CHUNKS:
+                nc.scalar.activation(
+                    out=m_abs[step][:].rearrange("p (n t) -> p n t", t=4),
+                    in_=acc[:].rearrange("p (t n) -> p n t", t=4),
+                    func=ACT.Abs,
+                )
+            if 1 <= step <= CHUNKS:
+                nc.scalar.activation(out=root[step - 1][:], in_=m_abs[step - 1][:], func=ACT.Abs_reciprocal_sqrt, bias=1.0)
+            if step >= 2:
+                nc.scalar.activation(out=damp[step - 2][:], in_=root[step - 2][:], func=ACT.Square)
+
+        first_banks = [bank(c) for c in range(4)]
         for a in range(2):
-            for half in range(2):
-                for j in (3, 2):
-                    gather_words(j, a, HALF * half, HALF * (half + 1), "words%d%d%d" % (j, a, half))
-                    for c in range(4 * half, 4 * half + 4):
-                        m_passes(m_banks[c], j, a, c)
-
-        gather(picked1[:], scale_win, 1, 0, S)
-        spread(nc.sync, planes23[:, 0 : 2 * S], picked1)
-        gather_words(1, 0, 0, S, "words10")
-        gather_words(1, 1, 0, HALF, "words110")
-
+            for j in (3, 2):
+                gather_words(j, a, 0, HALF, "words%d%d0" % (j, a))
+                for c in range(4):
+                    m_passes(first_banks[c], j, a, c)
+            for j in (3, 2):
+                gather_words(j, a, HALF, S, "words%d%d1" % (j, a))
         w1_bf = [sb("w1_bf%d" % a, 4 * H, BF16) for a in range(2)]
-        w1_codes = sb("w1_codes", 2 * H, U32)
-        w1_scale = sb("w1_scale", 2 * H, U8)
 
         def round_w1(copy, a):
             dst = w1_bf[a][:].rearrange("p (t g u i j) -> p t g u j i", t=4, g=16, u=2, j=4)
@@ -182,39 +191,45 @@ def tile_list_equity_factor_exposures_kernel(
             for t in range(4):
                 copy(dst[:, t], src[:, t])
 
+        round_w1(nc.scalar.copy, 0)
+        for c in range(4):
+            damping_step(c, first_banks[c])
+        for c in range(4, CHUNKS):
+            acc = bank(c - 4)
+            for a in range(2):
+                for j in (3, 2):
+                    m_passes(acc, j, a, c)
+            damping_step(c, acc)
+        damping_step(CHUNKS, None)
+        damping_step(CHUNKS + 1, None)
+
+        gather(picked1[:], scale_win, 1, 0, S)
+        spread(nc.sync, planes23[:, 0 : 2 * S], picked1)
+        gather_words(1, 0, 0, S, "words10")
+
+        w1_codes = sb("w1_codes", 2 * H, U32)
+        w1_scale = sb("w1_scale", 2 * H, U8)
+
         def quantize(codes, scales, values):
             nc.vector.quantize_mx(out=codes.bitcast(FP8X4), scales=scales, in_=values)
 
-        round_w1(nc.scalar.copy, 0)
         w4_bf = sb("w4_bf", 4 * N, BF16)
         w4_codes = sb("w4_codes", N, U32)
         w4_scale = sb("w4_scale", N, U8)
+        quantize(w1_codes[:, 0:H], w1_scale[:, 0:H], w1_bf[0][:])
+        gather_words(1, 1, 0, HALF, "w1_bf0")
         nc.vector.tensor_copy(
             w4_bf[:].rearrange("p (c u i t) -> p u t i c", c=2, i=2, t=4),
             w4_raw[:].rearrange("p (t u i c) -> p u t i c", c=2, i=2, t=4),
         )
         round_w1(nc.vector.tensor_copy, 1)
         quantize(w4_codes[:], w4_scale[:], w4_bf[:])
-        quantize(w1_codes[:, 0:H], w1_scale[:, 0:H], w1_bf[0][:])
         quantize(w1_codes[:, H : 2 * H], w1_scale[:, H : 2 * H], w1_bf[1][:])
         gather_words(1, 1, HALF, S, "w1_bf1")
 
-        damp = []
-        for c in range(CHUNKS):
-            m_abs = sb("m_abs%d" % c, HALF, F32)
-            root = sb("root%d" % c, HALF, F32)
-            damp.append(sb("damp%d" % c, HALF, F32))
-            nc.scalar.activation(
-                out=m_abs[:].rearrange("p (n t) -> p n t", t=4),
-                in_=m_banks[c][:].rearrange("p (t n) -> p n t", t=4),
-                func=ACT.Abs,
-            )
-            nc.scalar.activation(out=root[:], in_=m_abs[:], func=ACT.Abs_reciprocal_sqrt, bias=1.0)
-            nc.scalar.activation(out=damp[c][:], in_=root[:], func=ACT.Square)
-
         a_banks = []
         for c in range(CHUNKS):
-            acc = bank(c)
+            acc = bank((c + 4) % 8)
             a_banks.append(acc)
             for a in range(2):
                 for t in range(4):
@@ -260,16 +275,26 @@ def tile_list_equity_factor_exposures_kernel(
                 )
             for c in range(2):
                 start = 0 if banks[0] != banks[1] else width * c
-                nc.scalar.activation(
-                    out=result[:, width * c : width * (c + 1)],
-                    in_=tiles[banks[c]][:, start : start + width],
-                    func=ACT.Identity,
-                    scale=fs[:, c : c + 1],
-                    bias=fb[:, c : c + 1],
-                )
+                if hi == S and c == 1:
+                    nc.vector.tensor_scalar(
+                        result[:, width * c : width * (c + 1)],
+                        tiles[banks[c]][:, start : start + width],
+                        fs[:, c : c + 1],
+                        fb[:, c : c + 1],
+                        MULT,
+                        ADD,
+                    )
+                else:
+                    nc.scalar.activation(
+                        out=result[:, width * c : width * (c + 1)],
+                        in_=tiles[banks[c]][:, start : start + width],
+                        func=ACT.Identity,
+                        scale=fs[:, c : c + 1],
+                        bias=fb[:, c : c + 1],
+                    )
             nc.sync.dma_start(out_rows[:, :, lo:hi], result[:].rearrange("p (c j) -> p c j", c=2))
 
-        groups = {4: (0, 512, (0, 1)), 6: (512, 768, (2, 2)), 7: (768, 896, (3, 3)), 8: (896, 1024, (4, 4))}
+        groups = {3: (0, 256, (4, 4)), 5: (256, 512, (5, 5)), 6: (512, 768, (6, 6)), 7: (768, 896, (7, 7)), 8: (896, 1024, (0, 1))}
         for c in range(CHUNKS + 1):
             if c < CHUNKS:
                 damped(c)

@@ -50,8 +50,8 @@ def tile_list_equity_factor_exposures_kernel(
         nc.vector.memset(scale_win[64:128, :].bitcast(I32), 0)
         nc.vector.memset(scale_win[32:64, :].bitcast(I32), 0)
         nc.gpsimd.memset(warm[:, 0:8], 1.0)
+        nc.gpsimd.memset(planes23[:].bitcast(I32), 0)
         nc.vector.memset(ws_ord[:].bitcast(I32), 0)
-        nc.vector.memset(planes23[:].bitcast(I32), 0)
         nc.scalar.activation(out=warm[:, 8:9], in_=warm[:, 0:1], func=ACT.Abs_reciprocal_sqrt)
 
         w2_raw = sb("w2_raw", 4 * H, U8)
@@ -81,14 +81,18 @@ def tile_list_equity_factor_exposures_kernel(
         )
         load_words(0)
         load_words(1)
-        nc.sync.dma_start(lists[1][:], offs)
         w1_rows = w1.rearrange("(a p j) c -> a p j c", a=2, j=4)
-        w1_raw = [sb("w1_raw%d" % a, 4 * H, F32) for a in range(2)]
-        nc.sync.dma_start(w1_raw[0][:].rearrange("p (j c) -> p j c", j=4), w1_rows[0])
+        w1_first = [sb("w1_first%d" % u, 2 * H, F32) for u in range(2)]
+        w1_second = sb("w1_second", 4 * H, F32)
+        for u in range(2):
+            nc.sync.dma_start(
+                w1_first[u][:].rearrange("p (j c) -> p j c", j=4), w1_rows[0][:, :, 256 * u : 256 * (u + 1)]
+            )
+        nc.sync.dma_start(lists[1][:], offs)
+        nc.sync.dma_start(w1_second[:].rearrange("p (j c) -> p j c", j=4), w1_rows[1])
         w4_rows = w4.rearrange("(g t i) n -> t g i n", t=4, i=8)
         for t in range(4):
             nc.sync.dma_start(w4_raw[:, N * t : N * (t + 1)], w4_rows[t])
-        nc.sync.dma_start(w1_raw[1][:].rearrange("p (j c) -> p j c", j=4), w1_rows[1])
         nc.sync.dma_start(fs[:], fscale.rearrange("(p c) -> p c", c=2))
         nc.sync.dma_start(fb[:], fbase.rearrange("(p c) -> p c", c=2))
 
@@ -159,7 +163,6 @@ def tile_list_equity_factor_exposures_kernel(
                     stop=(a == 1 and j == 2 and t == 3),
                 )
 
-        m_abs = [sb("m_abs%d" % c, HALF, F32) for c in range(CHUNKS)]
         root = [sb("root%d" % c, HALF, F32) for c in range(CHUNKS)]
         damp = [sb("damp%d" % c, HALF, F32) for c in range(CHUNKS)]
 
@@ -178,22 +181,29 @@ def tile_list_equity_factor_exposures_kernel(
         first_banks = [bank(c) for c in range(4)]
         for a in range(2):
             for j in (3, 2):
-                gather_words(j, a, 0, HALF, "words%d%d0" % (j, a))
+                gather_words(j, a, 0, (S, HALF)[a], "words%d%d0" % (j, a))
                 for c in range(4):
                     m_passes(first_banks[c], j, a, c)
-            for j in (3, 2):
-                gather_words(j, a, HALF, S, "words%d%d1" % (j, a))
+        for j in (3, 2):
+            gather_words(j, 1, HALF, S, "words%d11" % j)
         w1_bf = [sb("w1_bf%d" % a, 4 * H, BF16) for a in range(2)]
 
-        def round_w1(copy, a):
+        def round_w1(copy, a, raw, lo, hi):
             dst = w1_bf[a][:].rearrange("p (t g u i j) -> p t g u j i", t=4, g=16, u=2, j=4)
-            src = w1_raw[a][:].rearrange("p (j g t u i) -> p t g u j i", t=4, g=16, u=2, j=4)
+            src = raw[:].rearrange("p (j g t u i) -> p t g u j i", t=4, g=hi - lo, u=2, j=4)
             for t in range(4):
-                copy(dst[:, t], src[:, t])
+                copy(dst[:, t, lo:hi], src[:, t])
 
-        round_w1(nc.scalar.copy, 0)
+        for u in range(2):
+            round_w1(nc.scalar.copy, 0, w1_first[u], 8 * u, 8 * (u + 1))
+        m_abs = [sb("m_abs%d" % c if c else "w1_first1", HALF, F32) for c in range(CHUNKS)]
         for c in range(4):
             damping_step(c, first_banks[c])
+        w4_bf = sb("w4_bf", 4 * N, BF16)
+        nc.scalar.copy(
+            w4_bf[:].rearrange("p (c u i t) -> p u t i c", c=2, i=2, t=4),
+            w4_raw[:].rearrange("p (t u i c) -> p u t i c", c=2, i=2, t=4),
+        )
         for c in range(4, CHUNKS):
             acc = bank(c - 4)
             for a in range(2):
@@ -213,19 +223,14 @@ def tile_list_equity_factor_exposures_kernel(
         def quantize(codes, scales, values):
             nc.vector.quantize_mx(out=codes.bitcast(FP8X4), scales=scales, in_=values)
 
-        w4_bf = sb("w4_bf", 4 * N, BF16)
         w4_codes = sb("w4_codes", N, U32)
         w4_scale = sb("w4_scale", N, U8)
         quantize(w1_codes[:, 0:H], w1_scale[:, 0:H], w1_bf[0][:])
-        gather_words(1, 1, 0, HALF, "w1_bf0")
-        nc.vector.tensor_copy(
-            w4_bf[:].rearrange("p (c u i t) -> p u t i c", c=2, i=2, t=4),
-            w4_raw[:].rearrange("p (t u i c) -> p u t i c", c=2, i=2, t=4),
-        )
-        round_w1(nc.vector.tensor_copy, 1)
-        quantize(w4_codes[:], w4_scale[:], w4_bf[:])
+        round_w1(nc.vector.tensor_copy, 1, w1_second, 0, 16)
+        gather_words(1, 1, 0, HALF, "w1_second")
         quantize(w1_codes[:, H : 2 * H], w1_scale[:, H : 2 * H], w1_bf[1][:])
         gather_words(1, 1, HALF, S, "w1_bf1")
+        quantize(w4_codes[:], w4_scale[:], w4_bf[:])
 
         a_banks = []
         for c in range(CHUNKS):

@@ -50,8 +50,8 @@ def tile_list_equity_factor_exposures_kernel(
         nc.vector.memset(scale_win[64:128, :].bitcast(I32), 0)
         nc.vector.memset(scale_win[32:64, :].bitcast(I32), 0)
         nc.gpsimd.memset(warm[:, 0:8], 1.0)
+        nc.gpsimd.memset(ws_ord[:].bitcast(I32), 0)
         nc.gpsimd.memset(planes23[:].bitcast(I32), 0)
-        nc.vector.memset(ws_ord[:].bitcast(I32), 0)
         nc.scalar.activation(out=warm[:, 8:9], in_=warm[:, 0:1], func=ACT.Abs_reciprocal_sqrt)
 
         w2_raw = sb("w2_raw", 4 * H, U8)
@@ -70,6 +70,7 @@ def tile_list_equity_factor_exposures_kernel(
         nc.sync.dma_start(lists[2][:], offs2)
         nc.sync.dma_start(scale_win[0:32, :].bitcast(I32), tab_scales.bitcast(I32).rearrange("a q t -> q a t"))
         nc.sync.dma_start(lists[3][:], offs3)
+        nc.sync.dma_start(lists[1][:], offs)
         load_weight_scales(0, w2_scales)
         load_weight_scales(1, w3_scales)
         nc.sync.dma_start(
@@ -81,23 +82,9 @@ def tile_list_equity_factor_exposures_kernel(
         )
         load_words(0)
         load_words(1)
-        w1_rows = w1.rearrange("(a p j) c -> a p j c", a=2, j=4)
-        w1_first = [sb("w1_first%d" % u, 2 * H, F32) for u in range(2)]
-        w1_second = sb("w1_second", 4 * H, F32)
-        for u in range(2):
-            nc.sync.dma_start(
-                w1_first[u][:].rearrange("p (j c) -> p j c", j=4), w1_rows[0][:, :, 256 * u : 256 * (u + 1)]
-            )
-        nc.sync.dma_start(lists[1][:], offs)
-        nc.sync.dma_start(w1_second[:].rearrange("p (j c) -> p j c", j=4), w1_rows[1])
-        w4_rows = w4.rearrange("(g t i) n -> t g i n", t=4, i=8)
-        for t in range(4):
-            nc.sync.dma_start(w4_raw[:, N * t : N * (t + 1)], w4_rows[t])
-        nc.sync.dma_start(fs[:], fscale.rearrange("(p c) -> p c", c=2))
-        nc.sync.dma_start(fb[:], fbase.rearrange("(p c) -> p c", c=2))
 
-        picked23 = sb("picked23", 2 * S, U8)
-        picked1 = sb("picked1", S, U8)
+        picked_early = sb("picked_early", S, U8)
+        picked_late = sb("picked_late", 2 * S, U8)
         g_word = {}
 
         def gather(dst, window, j, lo, hi):
@@ -123,8 +110,11 @@ def tile_list_equity_factor_exposures_kernel(
         def table_scale(j, a, c):
             lo = CHUNK * c
             if j == 1:
-                return planes23[:, S * a + lo : S * a + lo + CHUNK]
-            col = 2 * S * a + S * (j - 2) + lo
+                col = 2 * S * a + S + lo
+            elif lo < HALF:
+                col = S * a + HALF * (j - 2) + lo
+            else:
+                col = 2 * S * a + HALF * (j - 2) + lo - HALF
             return planes23[:, col : col + CHUNK]
 
         w2_ord = sb("w2_ord", 4 * H, U8)
@@ -138,10 +128,27 @@ def tile_list_equity_factor_exposures_kernel(
 
         reorder(ws_ord[0:16, :], ws_raw[0:16, :], 4)
         for q in range(1, 4):
-            nc.scalar.dma_start(ws_ord[32 * q : 32 * q + 4, :].bitcast(I32), ws_ord[4 * q : 4 * q + 4, :].bitcast(I32))
-        gather(picked23[:, 0:S], scale_win, 2, 0, S)
-        gather(picked23[:, S : 2 * S], scale_win, 3, 0, S)
-        spread(nc.scalar, planes23[:], picked23)
+            nc.sync.dma_start(ws_ord[32 * q : 32 * q + 4, :].bitcast(I32), ws_ord[4 * q : 4 * q + 4, :].bitcast(I32))
+        gather(picked_early[:, 0:HALF], scale_win, 2, 0, HALF)
+        gather(picked_early[:, HALF:S], scale_win, 3, 0, HALF)
+        spread(nc.sync, planes23[:, 0 : 2 * S], picked_early)
+        w1_rows = w1.rearrange("(a p j) c -> a p j c", a=2, j=4)
+        w1_first = [sb("w1_first%d" % u, 2 * H, F32) for u in range(2)]
+        w1_second = sb("w1_second", 4 * H, F32)
+        for u in range(2):
+            nc.sync.dma_start(
+                w1_first[u][:].rearrange("p (j c) -> p j c", j=4), w1_rows[0][:, :, 256 * u : 256 * (u + 1)]
+            )
+        nc.sync.dma_start(w1_second[:].rearrange("p (j c) -> p j c", j=4), w1_rows[1])
+        w4_rows = w4.rearrange("(g t i) n -> t g i n", t=4, i=8)
+        for t in range(4):
+            nc.sync.dma_start(w4_raw[:, N * t : N * (t + 1)], w4_rows[t])
+        nc.sync.dma_start(fs[:], fscale.rearrange("(p c) -> p c", c=2))
+        nc.sync.dma_start(fb[:], fbase.rearrange("(p c) -> p c", c=2))
+
+        gather(picked_late[:, 0:HALF], scale_win, 2, HALF, S)
+        gather(picked_late[:, HALF:S], scale_win, 3, HALF, S)
+        gather(picked_late[:, S : 2 * S], scale_win, 1, 0, S)
         reorder(w3_ord[:], w3_raw[:], 2)
         reorder(w2_ord[:], w2_raw[:], 2)
 
@@ -184,6 +191,7 @@ def tile_list_equity_factor_exposures_kernel(
                 gather_words(j, a, 0, (S, HALF)[a], "words%d%d0" % (j, a))
                 for c in range(4):
                     m_passes(first_banks[c], j, a, c)
+        spread(nc.sync, planes23[:], picked_late)
         for j in (3, 2):
             gather_words(j, 1, HALF, S, "words%d11" % j)
         w1_bf = [sb("w1_bf%d" % a, 4 * H, BF16) for a in range(2)]
@@ -199,11 +207,6 @@ def tile_list_equity_factor_exposures_kernel(
         m_abs = [sb("m_abs%d" % c if c else "w1_first1", HALF, F32) for c in range(CHUNKS)]
         for c in range(4):
             damping_step(c, first_banks[c])
-        w4_bf = sb("w4_bf", 4 * N, BF16)
-        nc.scalar.copy(
-            w4_bf[:].rearrange("p (c u i t) -> p u t i c", c=2, i=2, t=4),
-            w4_raw[:].rearrange("p (t u i c) -> p u t i c", c=2, i=2, t=4),
-        )
         for c in range(4, CHUNKS):
             acc = bank(c - 4)
             for a in range(2):
@@ -213,9 +216,7 @@ def tile_list_equity_factor_exposures_kernel(
         damping_step(CHUNKS, None)
         damping_step(CHUNKS + 1, None)
 
-        gather(picked1[:], scale_win, 1, 0, S)
-        spread(nc.sync, planes23[:, 0 : 2 * S], picked1)
-        gather_words(1, 0, 0, S, "words10")
+        gather_words(1, 0, 0, S, "words310")
 
         w1_codes = sb("w1_codes", 2 * H, U32)
         w1_scale = sb("w1_scale", 2 * H, U8)
@@ -229,6 +230,11 @@ def tile_list_equity_factor_exposures_kernel(
         round_w1(nc.vector.tensor_copy, 1, w1_second, 0, 16)
         gather_words(1, 1, 0, HALF, "w1_second")
         quantize(w1_codes[:, H : 2 * H], w1_scale[:, H : 2 * H], w1_bf[1][:])
+        w4_bf = sb("w4_bf", 4 * N, BF16)
+        nc.vector.tensor_copy(
+            w4_bf[:].rearrange("p (c u i t) -> p u t i c", c=2, i=2, t=4),
+            w4_raw[:].rearrange("p (t u i c) -> p u t i c", c=2, i=2, t=4),
+        )
         gather_words(1, 1, HALF, S, "w1_bf1")
         quantize(w4_codes[:], w4_scale[:], w4_bf[:])
 

@@ -42,7 +42,7 @@ def tile_list_equity_factor_exposures_kernel(
         word_win = [sb("word_win%d" % a, T, U32) for a in range(2)]
         ws_raw = sb("ws_raw", 4 * H, U8)
         ws_ord = sb("ws_ord", 4 * H, U8)
-        planes23 = sb("planes23", 4 * S, U8)
+        planes23 = sb("planes23", 6 * S, U8)
         warm = sb("warm", 16, F32)
         fs = sb("fs", 2, F32)
         fb = sb("fb", 2, F32)
@@ -52,7 +52,6 @@ def tile_list_equity_factor_exposures_kernel(
         nc.gpsimd.memset(warm[:, 0:8], 1.0)
         nc.gpsimd.memset(ws_ord[:].bitcast(I32), 0)
         nc.gpsimd.memset(planes23[:].bitcast(I32), 0)
-        nc.scalar.activation(out=warm[:, 8:9], in_=warm[:, 0:1], func=ACT.Abs_reciprocal_sqrt)
 
         w2_raw = sb("w2_raw", 4 * H, U8)
         w3_raw = sb("w3_raw", 2 * H, U32)
@@ -73,6 +72,8 @@ def tile_list_equity_factor_exposures_kernel(
         nc.sync.dma_start(lists[1][:], offs)
         load_weight_scales(0, w2_scales)
         load_weight_scales(1, w3_scales)
+        nc.scalar.activation(out=warm[:, 8:9], in_=warm[:, 0:1], func=ACT.Abs_reciprocal_sqrt)
+        load_words(0)
         nc.sync.dma_start(
             w3_raw[:].bitcast(I32).rearrange("p (a c) -> p a c", a=2),
             w3_words.rearrange("a p c i -> a p (c i)").bitcast(I32).rearrange("a p c -> p a c"),
@@ -80,8 +81,6 @@ def tile_list_equity_factor_exposures_kernel(
         nc.sync.dma_start(
             w2_raw[:].bitcast(I32).rearrange("p (a b) -> p a b", a=2), w2_words.bitcast(I32).rearrange("a p b -> p a b")
         )
-        load_words(0)
-        load_words(1)
 
         picked_early = sb("picked_early", S, U8)
         picked_late = sb("picked_late", 2 * S, U8)
@@ -110,11 +109,11 @@ def tile_list_equity_factor_exposures_kernel(
         def table_scale(j, a, c):
             lo = CHUNK * c
             if j == 1:
-                col = 2 * S * a + S + lo
+                col = 2 * S * (a + 1) + S + lo
             elif lo < HALF:
                 col = S * a + HALF * (j - 2) + lo
             else:
-                col = 2 * S * a + HALF * (j - 2) + lo - HALF
+                col = 2 * S * (a + 1) + HALF * (j - 2) + lo - HALF
             return planes23[:, col : col + CHUNK]
 
         w2_ord = sb("w2_ord", 4 * H, U8)
@@ -132,6 +131,7 @@ def tile_list_equity_factor_exposures_kernel(
         gather(picked_early[:, 0:HALF], scale_win, 2, 0, HALF)
         gather(picked_early[:, HALF:S], scale_win, 3, 0, HALF)
         spread(nc.sync, planes23[:, 0 : 2 * S], picked_early)
+        load_words(1)
         w1_rows = w1.rearrange("(a p j) c -> a p j c", a=2, j=4)
         w1_first = [sb("w1_first%d" % u, 2 * H, F32) for u in range(2)]
         w1_second = sb("w1_second", 4 * H, F32)
@@ -139,16 +139,18 @@ def tile_list_equity_factor_exposures_kernel(
             nc.sync.dma_start(
                 w1_first[u][:].rearrange("p (j c) -> p j c", j=4), w1_rows[0][:, :, 256 * u : 256 * (u + 1)]
             )
+        gather(picked_late[:, 0:HALF], scale_win, 2, HALF, S)
+        gather(picked_late[:, HALF:S], scale_win, 3, HALF, S)
+        gather(picked_late[:, S : 2 * S], scale_win, 1, 0, S)
+        spread(nc.sync, planes23[:, 2 * S : 6 * S], picked_late)
         nc.sync.dma_start(w1_second[:].rearrange("p (j c) -> p j c", j=4), w1_rows[1])
         w4_rows = w4.rearrange("(g t i) n -> t g i n", t=4, i=8)
         for t in range(4):
             nc.sync.dma_start(w4_raw[:, N * t : N * (t + 1)], w4_rows[t])
-        nc.sync.dma_start(fs[:], fscale.rearrange("(p c) -> p c", c=2))
-        nc.sync.dma_start(fb[:], fbase.rearrange("(p c) -> p c", c=2))
+        with nc.allow_non_contiguous_dma(reason="one value a partition for each half of the factors"):
+            nc.sync.dma_start(fs[:], fscale.rearrange("(c p) -> p c", c=2))
+            nc.sync.dma_start(fb[:], fbase.rearrange("(c p) -> p c", c=2))
 
-        gather(picked_late[:, 0:HALF], scale_win, 2, HALF, S)
-        gather(picked_late[:, HALF:S], scale_win, 3, HALF, S)
-        gather(picked_late[:, S : 2 * S], scale_win, 1, 0, S)
         reorder(w3_ord[:], w3_raw[:], 2)
         reorder(w2_ord[:], w2_raw[:], 2)
 
@@ -176,8 +178,8 @@ def tile_list_equity_factor_exposures_kernel(
         def damping_step(step, acc):
             if step < CHUNKS:
                 nc.scalar.activation(
-                    out=m_abs[step][:].rearrange("p (n t) -> p n t", t=4),
-                    in_=acc[:].rearrange("p (t n) -> p n t", t=4),
+                    out=m_abs[step][:].rearrange("p (q t i) -> p q t i", t=4, i=2),
+                    in_=acc[:].rearrange("p (t q i) -> p q t i", t=4, i=2),
                     func=ACT.Abs,
                 )
             if 1 <= step <= CHUNKS:
@@ -186,19 +188,26 @@ def tile_list_equity_factor_exposures_kernel(
                 nc.scalar.activation(out=damp[step - 2][:], in_=root[step - 2][:], func=ACT.Square)
 
         first_banks = [bank(c) for c in range(4)]
+        first_words = sb("w3_raw", S, U32)
+        g_word[3, 0, 0] = first_words[:, 0:HALF]
+        g_word[3, 0, 1] = first_words[:, HALF:S]
+        gather(g_word[3, 0, 0], word_win[0], 3, 0, HALF)
+        gather_words(2, 0, 0, HALF, "w2_raw")
+        gather(g_word[3, 0, 1], word_win[0], 3, HALF, S)
         for a in range(2):
             for j in (3, 2):
-                gather_words(j, a, 0, (S, HALF)[a], "words%d%d0" % (j, a))
+                if a == 1:
+                    gather_words(j, a, 0, HALF, "words%d10" % j)
                 for c in range(4):
                     m_passes(first_banks[c], j, a, c)
-        spread(nc.sync, planes23[:], picked_late)
         for j in (3, 2):
             gather_words(j, 1, HALF, S, "words%d11" % j)
+        gather_words(2, 0, HALF, S, "words310")
         w1_bf = [sb("w1_bf%d" % a, 4 * H, BF16) for a in range(2)]
 
         def round_w1(copy, a, raw, lo, hi):
-            dst = w1_bf[a][:].rearrange("p (t g u i j) -> p t g u j i", t=4, g=16, u=2, j=4)
-            src = raw[:].rearrange("p (j g t u i) -> p t g u j i", t=4, g=hi - lo, u=2, j=4)
+            dst = w1_bf[a][:].rearrange("p (t g u i j) -> p t g u j i", t=4, g=16, u=4, j=4)
+            src = raw[:].rearrange("p (j g t u i) -> p t g u j i", t=4, g=hi - lo, u=4, j=4)
             for t in range(4):
                 copy(dst[:, t, lo:hi], src[:, t])
 
@@ -207,6 +216,10 @@ def tile_list_equity_factor_exposures_kernel(
         m_abs = [sb("m_abs%d" % c if c else "w1_first1", HALF, F32) for c in range(CHUNKS)]
         for c in range(4):
             damping_step(c, first_banks[c])
+        w4_bf = sb("w4_bf", 4 * N, BF16)
+        nc.scalar.copy(
+            w4_bf[:].rearrange("p (q i t) -> p q t i", i=2, t=4), w4_raw[:].rearrange("p (t q i) -> p q t i", i=2, t=4)
+        )
         for c in range(4, CHUNKS):
             acc = bank(c - 4)
             for a in range(2):
@@ -216,7 +229,7 @@ def tile_list_equity_factor_exposures_kernel(
         damping_step(CHUNKS, None)
         damping_step(CHUNKS + 1, None)
 
-        gather_words(1, 0, 0, S, "words310")
+        gather_words(1, 0, 0, S, "words210")
 
         w1_codes = sb("w1_codes", 2 * H, U32)
         w1_scale = sb("w1_scale", 2 * H, U8)
@@ -230,11 +243,6 @@ def tile_list_equity_factor_exposures_kernel(
         round_w1(nc.vector.tensor_copy, 1, w1_second, 0, 16)
         gather_words(1, 1, 0, HALF, "w1_second")
         quantize(w1_codes[:, H : 2 * H], w1_scale[:, H : 2 * H], w1_bf[1][:])
-        w4_bf = sb("w4_bf", 4 * N, BF16)
-        nc.vector.tensor_copy(
-            w4_bf[:].rearrange("p (c u i t) -> p u t i c", c=2, i=2, t=4),
-            w4_raw[:].rearrange("p (t u i c) -> p u t i c", c=2, i=2, t=4),
-        )
         gather_words(1, 1, HALF, S, "w1_bf1")
         quantize(w4_codes[:], w4_scale[:], w4_bf[:])
 
@@ -258,13 +266,13 @@ def tile_list_equity_factor_exposures_kernel(
         h_bf = sb("h_bf", 4 * S, BF16)
         h_codes = sb("h_codes", S, U32)
         h_scale = sb("h_scale", S, U8)
-        out_rows = out.rearrange("(p c) j -> p c j", c=2)
+        out_rows = out.rearrange("(c p) j -> p c j", c=2)
 
         def damped(c):
             nc.vector.tensor_tensor(
-                h_bf[:, HALF * c : HALF * (c + 1)].rearrange("p (n t) -> p n t", t=4),
-                a_banks[c][:].rearrange("p (t n) -> p n t", t=4),
-                damp[c][:].rearrange("p (n t) -> p n t", t=4),
+                h_bf[:, HALF * c : HALF * (c + 1)].rearrange("p (q i t) -> p q t i", t=4, i=2),
+                a_banks[c][:].rearrange("p (t q i) -> p q t i", t=4, i=2),
+                damp[c][:].rearrange("p (q t i) -> p q t i", t=4, i=2),
                 MULT,
             )
 

@@ -18,9 +18,11 @@ MULT = mybir.AluOpType.mult
 ADD = mybir.AluOpType.add
 
 P = 128
-HALF = 512
+HALF = S // 2
 CHUNK = 128
 CHUNKS = S // CHUNK
+HALF_CHUNKS = CHUNKS // 2
+ROWS_FROM = 96
 
 
 def tile_list_equity_factor_exposures_kernel(
@@ -42,68 +44,60 @@ def tile_list_equity_factor_exposures_kernel(
         word_win = [sb("word_win%d" % a, T, U32) for a in range(2)]
         ws_raw = sb("ws_raw", 4 * H, U8)
         ws_ord = sb("ws_ord", 4 * H, U8)
-        planes23 = sb("planes23", 6 * S, U8)
+        ws_planes = sb("ws_planes", 4 * H, U8)
+        tab_planes = sb("tab_planes", 6 * S, U8)
         warm = sb("warm", 16, F32)
         fs = sb("fs", 2, F32)
         fb = sb("fb", 2, F32)
 
-        nc.vector.memset(scale_win[64:128, :].bitcast(I32), 0)
-        nc.vector.memset(scale_win[32:64, :].bitcast(I32), 0)
+        nc.vector.memset(scale_win[0:ROWS_FROM, :].bitcast(I32), 0)
+        nc.vector.memset(ws_planes[:].bitcast(I32), 0)
         nc.gpsimd.memset(warm[:, 0:8], 1.0)
-        nc.gpsimd.memset(ws_ord[:].bitcast(I32), 0)
-        nc.gpsimd.memset(planes23[:].bitcast(I32), 0)
+        nc.gpsimd.memset(tab_planes[:].bitcast(I32), 0)
 
         w2_raw = sb("w2_raw", 4 * H, U8)
         w3_raw = sb("w3_raw", 2 * H, U32)
         w4_raw = sb("w4_raw", 4 * N, F32)
 
-        def load_weight_scales(w, src):
-            nc.scalar.dma_start(
-                ws_raw[0:16, 2 * H * w : 2 * H * (w + 1)].bitcast(I32).rearrange("q (a c) -> q a c", a=2),
+        def load_weight_scales(j, src):
+            nc.sync.dma_start(
+                ws_raw[0:16, 2 * H * (j - 2) : 2 * H * (j - 1)].bitcast(I32).rearrange("q (a c) -> q a c", a=2),
                 src.bitcast(I32).rearrange("a q c -> q a c"),
             )
 
         def load_words(a):
             nc.sync.dma_start(word_win[a][:].bitcast(I32), tab_words[a].rearrange("p t i -> p (t i)").bitcast(I32))
 
+        nc.sync.dma_start(scale_win[ROWS_FROM:P, :].bitcast(I32), tab_scales.bitcast(I32).rearrange("a q t -> q a t"))
+        load_weight_scales(2, w2_scales)
+        load_weight_scales(3, w3_scales)
         nc.sync.dma_start(lists[2][:], offs2)
-        nc.sync.dma_start(scale_win[0:32, :].bitcast(I32), tab_scales.bitcast(I32).rearrange("a q t -> q a t"))
         nc.sync.dma_start(lists[3][:], offs3)
         nc.sync.dma_start(lists[1][:], offs)
-        load_weight_scales(0, w2_scales)
-        load_weight_scales(1, w3_scales)
         nc.scalar.activation(out=warm[:, 8:9], in_=warm[:, 0:1], func=ACT.Abs_reciprocal_sqrt)
         load_words(0)
-        nc.sync.dma_start(
-            w3_raw[:].bitcast(I32).rearrange("p (a c) -> p a c", a=2),
-            w3_words.rearrange("a p c i -> a p (c i)").bitcast(I32).rearrange("a p c -> p a c"),
-        )
-        nc.sync.dma_start(
-            w2_raw[:].bitcast(I32).rearrange("p (a b) -> p a b", a=2), w2_words.bitcast(I32).rearrange("a p b -> p a b")
-        )
 
-        picked_early = sb("picked_early", S, U8)
         picked_late = sb("picked_late", 2 * S, U8)
-        g_word = {}
+        picked_words = {}
 
         def gather(dst, window, j, lo, hi):
             nc.vector.tensor_copy(dst, window[:].indirect(lists[j][:, lo // 16 : hi // 16]))
 
-        def gather_words(j, a, lo, hi, slot):
-            dst = sb(slot, hi - lo, U32)
+        def gather_words(j, a, lo, hi, name):
+            dst = sb(name, hi - lo, U32)
             gather(dst[:], word_win[a], j, lo, hi)
             for half in range(lo // HALF, hi // HALF):
-                g_word[j, a, half] = dst[:, HALF * half - lo : HALF * (half + 1) - lo]
+                picked_words[j, a, half] = dst[:, HALF * half - lo : HALF * (half + 1) - lo]
 
         def table_words(j, a, c):
             lo = CHUNK * c
-            return g_word[j, a, lo // HALF][:, lo % HALF : lo % HALF + CHUNK].bitcast(FP8X4)
+            return picked_words[j, a, lo // HALF][:, lo % HALF : lo % HALF + CHUNK].bitcast(FP8X4)
 
-        def spread(queue, planes, picked):
+        def spread(planes, picked):
             for q in range(4):
-                queue.dma_start(
+                nc.sync.dma_start(
                     planes[32 * q : 32 * q + 4].bitcast(I32).rearrange("r (a n) -> r a n", a=2),
-                    picked[8 * q : 8 * q + 8, :].bitcast(I32),
+                    picked[ROWS_FROM + 8 * q : ROWS_FROM + 8 * q + 8, :].bitcast(I32),
                 )
 
         def table_scale(j, a, c):
@@ -114,42 +108,52 @@ def tile_list_equity_factor_exposures_kernel(
                 col = S * a + HALF * (j - 2) + lo
             else:
                 col = 2 * S * (a + 1) + HALF * (j - 2) + lo - HALF
-            return planes23[:, col : col + CHUNK]
+            return tab_planes[:, col : col + CHUNK]
 
         w2_ord = sb("w2_ord", 4 * H, U8)
         w3_ord = sb("w3_ord", 2 * H, U32)
 
-        def reorder(dst, src, planes):
+        def reorder(dst, src, parts):
             nc.vector.tensor_copy(
-                dst.bitcast(I32).rearrange("p (a t g e) -> p a t g e", a=planes, t=4, g=16),
-                src.bitcast(I32).rearrange("p (a g t e) -> p a t g e", a=planes, t=4, g=16),
+                dst.bitcast(I32).rearrange("p (a t g e) -> p a t g e", a=parts, t=4, g=16),
+                src.bitcast(I32).rearrange("p (a g t e) -> p a t g e", a=parts, t=4, g=16),
             )
 
         reorder(ws_ord[0:16, :], ws_raw[0:16, :], 4)
-        for q in range(1, 4):
-            nc.sync.dma_start(ws_ord[32 * q : 32 * q + 4, :].bitcast(I32), ws_ord[4 * q : 4 * q + 4, :].bitcast(I32))
+        for r in range(4):
+            nc.sync.dma_start(ws_planes[r:P:32, :].bitcast(I32), ws_ord[r:16:4, :].bitcast(I32))
+        nc.sync.dma_start(
+            w3_raw[:].bitcast(I32).rearrange("p (a c) -> p a c", a=2),
+            w3_words.rearrange("a p c i -> a p (c i)").bitcast(I32).rearrange("a p c -> p a c"),
+        )
+        nc.sync.dma_start(
+            w2_raw[:].bitcast(I32).rearrange("p (a b) -> p a b", a=2), w2_words.bitcast(I32).rearrange("a p b -> p a b")
+        )
+
+        picked_early = sb("picked_early", S, U8)
         gather(picked_early[:, 0:HALF], scale_win, 2, 0, HALF)
         gather(picked_early[:, HALF:S], scale_win, 3, 0, HALF)
-        spread(nc.sync, planes23[:, 0 : 2 * S], picked_early)
+        spread(tab_planes[:, 0 : 2 * S], picked_early)
         load_words(1)
+
         w1_rows = w1.rearrange("(a p j) c -> a p j c", a=2, j=4)
         w1_first = [sb("w1_first%d" % u, 2 * H, F32) for u in range(2)]
         w1_second = sb("w1_second", 4 * H, F32)
         for u in range(2):
             nc.sync.dma_start(
-                w1_first[u][:].rearrange("p (j c) -> p j c", j=4), w1_rows[0][:, :, 256 * u : 256 * (u + 1)]
+                w1_first[u][:].rearrange("p (j c) -> p j c", j=4), w1_rows[0][:, :, H // 2 * u : H // 2 * (u + 1)]
             )
         gather(picked_late[:, 0:HALF], scale_win, 2, HALF, S)
         gather(picked_late[:, HALF:S], scale_win, 3, HALF, S)
         gather(picked_late[:, S : 2 * S], scale_win, 1, 0, S)
-        spread(nc.sync, planes23[:, 2 * S : 6 * S], picked_late)
+        spread(tab_planes[:, 2 * S : 6 * S], picked_late)
         nc.sync.dma_start(w1_second[:].rearrange("p (j c) -> p j c", j=4), w1_rows[1])
         w4_rows = w4.rearrange("(g t i) n -> t g i n", t=4, i=8)
         for t in range(4):
             nc.sync.dma_start(w4_raw[:, N * t : N * (t + 1)], w4_rows[t])
-        with nc.allow_non_contiguous_dma(reason="one value a partition for each half of the factors"):
-            nc.sync.dma_start(fs[:], fscale.rearrange("(c p) -> p c", c=2))
-            nc.sync.dma_start(fb[:], fbase.rearrange("(c p) -> p c", c=2))
+        with nc.allow_non_contiguous_dma(reason="factor 128 f + p has its scale and base level at [p, f]"):
+            nc.sync.dma_start(fs[:], fscale.rearrange("(f p) -> p f", f=2))
+            nc.sync.dma_start(fb[:], fbase.rearrange("(f p) -> p f", f=2))
 
         reorder(w3_ord[:], w3_raw[:], 2)
         reorder(w2_ord[:], w2_raw[:], 2)
@@ -165,7 +169,7 @@ def tile_list_equity_factor_exposures_kernel(
                 nc.tensor.matmul_mx(
                     out=acc[:, CHUNK * t : CHUNK * (t + 1)],
                     lhsT=lhsT,
-                    lhsT_scale=ws_ord[:, scol : scol + P],
+                    lhsT_scale=ws_planes[:, scol : scol + P],
                     rhs=table_words(j, a, c),
                     rhs_scale=table_scale(j, a, c),
                     start=(a == 0 and j == 3 and t == 0),
@@ -187,22 +191,22 @@ def tile_list_equity_factor_exposures_kernel(
             if step >= 2:
                 nc.scalar.activation(out=damp[step - 2][:], in_=root[step - 2][:], func=ACT.Square)
 
-        first_banks = [bank(c) for c in range(4)]
+        first_banks = [bank(c) for c in range(HALF_CHUNKS)]
         first_words = sb("w3_raw", S, U32)
-        g_word[3, 0, 0] = first_words[:, 0:HALF]
-        g_word[3, 0, 1] = first_words[:, HALF:S]
-        gather(g_word[3, 0, 0], word_win[0], 3, 0, HALF)
+        picked_words[3, 0, 0] = first_words[:, 0:HALF]
+        picked_words[3, 0, 1] = first_words[:, HALF:S]
+        gather(picked_words[3, 0, 0], word_win[0], 3, 0, HALF)
         gather_words(2, 0, 0, HALF, "w2_raw")
-        gather(g_word[3, 0, 1], word_win[0], 3, HALF, S)
+        gather(picked_words[3, 0, 1], word_win[0], 3, HALF, S)
         for a in range(2):
             for j in (3, 2):
                 if a == 1:
-                    gather_words(j, a, 0, HALF, "words%d10" % j)
-                for c in range(4):
+                    gather_words(j, a, 0, HALF, "second_pass_low%d" % j)
+                for c in range(HALF_CHUNKS):
                     m_passes(first_banks[c], j, a, c)
         for j in (3, 2):
-            gather_words(j, 1, HALF, S, "words%d11" % j)
-        gather_words(2, 0, HALF, S, "words310")
+            gather_words(j, 1, HALF, S, "second_pass_high%d" % j)
+        gather_words(2, 0, HALF, S, "second_pass_low3")
         w1_bf = [sb("w1_bf%d" % a, 4 * H, BF16) for a in range(2)]
 
         def round_w1(copy, a, raw, lo, hi):
@@ -214,14 +218,14 @@ def tile_list_equity_factor_exposures_kernel(
         for u in range(2):
             round_w1(nc.scalar.copy, 0, w1_first[u], 8 * u, 8 * (u + 1))
         m_abs = [sb("m_abs%d" % c if c else "w1_first1", HALF, F32) for c in range(CHUNKS)]
-        for c in range(4):
+        for c in range(HALF_CHUNKS):
             damping_step(c, first_banks[c])
         w4_bf = sb("w4_bf", 4 * N, BF16)
         nc.scalar.copy(
             w4_bf[:].rearrange("p (q i t) -> p q t i", i=2, t=4), w4_raw[:].rearrange("p (t q i) -> p q t i", i=2, t=4)
         )
-        for c in range(4, CHUNKS):
-            acc = bank(c - 4)
+        for c in range(HALF_CHUNKS, CHUNKS):
+            acc = bank(c - HALF_CHUNKS)
             for a in range(2):
                 for j in (3, 2):
                     m_passes(acc, j, a, c)
@@ -229,7 +233,7 @@ def tile_list_equity_factor_exposures_kernel(
         damping_step(CHUNKS, None)
         damping_step(CHUNKS + 1, None)
 
-        gather_words(1, 0, 0, S, "words210")
+        gather_words(1, 0, 0, S, "second_pass_low2")
 
         w1_codes = sb("w1_codes", 2 * H, U32)
         w1_scale = sb("w1_scale", 2 * H, U8)
@@ -248,7 +252,7 @@ def tile_list_equity_factor_exposures_kernel(
 
         a_banks = []
         for c in range(CHUNKS):
-            acc = bank((c + 4) % 8)
+            acc = bank((c + HALF_CHUNKS) % CHUNKS)
             a_banks.append(acc)
             for a in range(2):
                 for t in range(4):
@@ -266,11 +270,11 @@ def tile_list_equity_factor_exposures_kernel(
         h_bf = sb("h_bf", 4 * S, BF16)
         h_codes = sb("h_codes", S, U32)
         h_scale = sb("h_scale", S, U8)
-        out_rows = out.rearrange("(c p) j -> p c j", c=2)
+        out_rows = out.rearrange("(f p) j -> p f j", f=2)
 
         def damped(c):
             nc.vector.tensor_tensor(
-                h_bf[:, HALF * c : HALF * (c + 1)].rearrange("p (q i t) -> p q t i", t=4, i=2),
+                h_bf[:, 4 * CHUNK * c : 4 * CHUNK * (c + 1)].rearrange("p (q i t) -> p q t i", t=4, i=2),
                 a_banks[c][:].rearrange("p (t q i) -> p q t i", t=4, i=2),
                 damp[c][:].rearrange("p (q t i) -> p q t i", t=4, i=2),
                 MULT,
@@ -280,44 +284,35 @@ def tile_list_equity_factor_exposures_kernel(
             width = hi - lo
             result = sb("result%d" % lo, 2 * width, F32)
             tiles = {b: bank(b) for b in sorted(set(banks))}
-            for c in range(2):
-                start = 0 if banks[0] != banks[1] else width * c
-                acc = tiles[banks[c]][:, start : start + width]
+            sums = []
+            for f in range(2):
+                first = width * f if banks[0] == banks[1] else 0
+                sums.append(tiles[banks[f]][:, first : first + width])
                 nc.tensor.matmul_mx(
-                    out=acc,
-                    lhsT=w4_codes[:, P * c : P * (c + 1)].bitcast(FP8X4),
-                    lhsT_scale=w4_scale[:, P * c : P * (c + 1)],
+                    out=sums[f],
+                    lhsT=w4_codes[:, P * f : P * (f + 1)].bitcast(FP8X4),
+                    lhsT_scale=w4_scale[:, P * f : P * (f + 1)],
                     rhs=h_codes[:, lo:hi].bitcast(FP8X4),
                     rhs_scale=h_scale[:, lo:hi],
                     start=True,
                     stop=True,
                 )
-            for c in range(2):
-                start = 0 if banks[0] != banks[1] else width * c
-                if hi == S and c == 1:
-                    nc.vector.tensor_scalar(
-                        result[:, width * c : width * (c + 1)],
-                        tiles[banks[c]][:, start : start + width],
-                        fs[:, c : c + 1],
-                        fb[:, c : c + 1],
-                        MULT,
-                        ADD,
-                    )
+            for f in range(2):
+                dst = result[:, width * f : width * (f + 1)]
+                if banks[f] != banks[0]:
+                    nc.vector.tensor_scalar(dst, sums[f], fs[:, f : f + 1], fb[:, f : f + 1], MULT, ADD)
                 else:
                     nc.scalar.activation(
-                        out=result[:, width * c : width * (c + 1)],
-                        in_=tiles[banks[c]][:, start : start + width],
-                        func=ACT.Identity,
-                        scale=fs[:, c : c + 1],
-                        bias=fb[:, c : c + 1],
+                        out=dst, in_=sums[f], func=ACT.Identity, scale=fs[:, f : f + 1], bias=fb[:, f : f + 1]
                     )
-            nc.sync.dma_start(out_rows[:, :, lo:hi], result[:].rearrange("p (c j) -> p c j", c=2))
+            nc.sync.dma_start(out_rows[:, :, lo:hi], result[:].rearrange("p (f j) -> p f j", f=2))
 
-        groups = {3: (0, 256, (4, 4)), 5: (256, 512, (5, 5)), 6: (512, 768, (6, 6)), 7: (768, 896, (7, 7)), 8: (896, 1024, (0, 1))}
+        groups = [(0, 2, (4, 4)), (2, 4, (5, 5)), (4, 6, (6, 6)), (6, 7, (7, 7)), (7, 8, (0, 1))]
         for c in range(CHUNKS + 1):
             if c < CHUNKS:
                 damped(c)
-            if c in groups:
-                lo, hi, banks = groups[c]
-                quantize(h_codes[:, lo:hi], h_scale[:, lo:hi], h_bf[:, 4 * lo : 4 * hi])
-                exposures(lo, hi, banks)
+            for first_chunk, end_chunk, banks in groups:
+                if end_chunk == c:
+                    lo, hi = CHUNK * first_chunk, CHUNK * end_chunk
+                    quantize(h_codes[:, lo:hi], h_scale[:, lo:hi], h_bf[:, 4 * lo : 4 * hi])
+                    exposures(lo, hi, banks)

@@ -39,6 +39,9 @@ def tile_list_equity_factor_exposures_kernel(
         def bank(b):
             return psum.tile([P, HALF], F32, name="bank%d" % b)
 
+        def by_value(tile, lo, hi):
+            return tile[:].rearrange("p (t n) -> p t n", t=4)[:, :, lo:hi]
+
         lists = {j: keep.tile([P, S // 16], U16, name="list%d" % j) for j in (1, 2, 3)}
         scale_win = sb("scale_win", T, U8)
         word_win = [sb("word_win%d" % a, T, U32) for a in range(2)]
@@ -94,21 +97,20 @@ def tile_list_equity_factor_exposures_kernel(
             return picked_words[j, a, lo // HALF][:, lo % HALF : lo % HALF + CHUNK].bitcast(FP8X4)
 
         def spread(planes, picked):
-            for q in range(4):
+            for q in (0, 2, 1, 3):
                 nc.sync.dma_start(
                     planes[32 * q : 32 * q + 4].bitcast(I32).rearrange("r (a n) -> r a n", a=2),
                     picked[ROWS_FROM + 8 * q : ROWS_FROM + 8 * q + 8, :].bitcast(I32),
                 )
 
-        def table_scale(j, a, c):
-            lo = CHUNK * c
+        def table_scale(j, a, lo, width):
             if j == 1:
                 col = 2 * S * (a + 1) + S + lo
             elif lo < HALF:
                 col = S * a + HALF * (j - 2) + lo
             else:
                 col = 2 * S * (a + 1) + HALF * (j - 2) + lo - HALF
-            return tab_planes[:, col : col + CHUNK]
+            return tab_planes[:, col : col + width]
 
         w2_ord = sb("w2_ord", 4 * H, U8)
         w3_ord = sb("w3_ord", 2 * H, U32)
@@ -158,40 +160,36 @@ def tile_list_equity_factor_exposures_kernel(
         reorder(w3_ord[:], w3_raw[:], 2)
         reorder(w2_ord[:], w2_raw[:], 2)
 
-        def m_passes(acc, j, a, c):
-            for t in range(4):
-                col = H * a + P * t
-                if j == 2:
-                    lhsT = w2_ord[:, 2 * col : 2 * (col + P)].bitcast(FP4X4)
-                else:
-                    lhsT = w3_ord[:, col : col + P].bitcast(FP8X4)
-                scol = 2 * H * (j - 2) + col
-                nc.tensor.matmul_mx(
-                    out=acc[:, CHUNK * t : CHUNK * (t + 1)],
-                    lhsT=lhsT,
-                    lhsT_scale=ws_planes[:, scol : scol + P],
-                    rhs=table_words(j, a, c),
-                    rhs_scale=table_scale(j, a, c),
-                    start=(a == 0 and j == 3 and t == 0),
-                    stop=(a == 1 and j == 2 and t == 3),
-                )
+        def m_pass(acc, j, a, t, half):
+            col = H * a + P * t
+            if j == 2:
+                lhsT = w2_ord[:, 2 * col : 2 * (col + P)].bitcast(FP4X4)
+            else:
+                lhsT = w3_ord[:, col : col + P].bitcast(FP8X4)
+            scol = 2 * H * (j - 2) + col
+            nc.tensor.matmul_mx(
+                out=acc[:],
+                lhsT=lhsT,
+                lhsT_scale=ws_planes[:, scol : scol + P],
+                rhs=picked_words[j, a, half].bitcast(FP8X4),
+                rhs_scale=table_scale(j, a, HALF * half, HALF),
+                start=(a == 0 and j == 3),
+                stop=(a == 1 and j == 2),
+            )
 
-        root = [sb("root%d" % c, HALF, F32) for c in range(CHUNKS)]
-        damp = [sb("damp%d" % c, HALF, F32) for c in range(CHUNKS)]
+        root = [sb("root%d" % half, 4 * HALF, F32) for half in range(2)]
+        damp = [sb("damp%d" % half, 4 * HALF, F32) for half in range(2)]
 
-        def damping_step(step, acc):
-            if step < CHUNKS:
-                nc.scalar.activation(
-                    out=m_abs[step][:].rearrange("p (q t i) -> p q t i", t=4, i=2),
-                    in_=acc[:].rearrange("p (t q i) -> p q t i", t=4, i=2),
-                    func=ACT.Abs,
-                )
-            if 1 <= step <= CHUNKS:
-                nc.scalar.activation(out=root[step - 1][:], in_=m_abs[step - 1][:], func=ACT.Abs_reciprocal_sqrt, bias=1.0)
-            if step >= 2:
-                nc.scalar.activation(out=damp[step - 2][:], in_=root[step - 2][:], func=ACT.Square)
+        def inverse_root(dst, src):
+            nc.scalar.activation(out=dst, in_=src, func=ACT.Abs_reciprocal_sqrt, bias=1.0)
 
-        first_banks = [bank(c) for c in range(HALF_CHUNKS)]
+        def square(dst, src):
+            nc.scalar.activation(out=dst, in_=src, func=ACT.Square)
+
+        def magnitude(half, t, acc):
+            nc.scalar.activation(out=m_abs[half][:, HALF * t : HALF * (t + 1)], in_=acc[:], func=ACT.Abs)
+
+        first_banks = [bank(t) for t in range(4)]
         first_words = sb("w3_raw", S, U32)
         picked_words[3, 0, 0] = first_words[:, 0:HALF]
         picked_words[3, 0, 1] = first_words[:, HALF:S]
@@ -202,8 +200,8 @@ def tile_list_equity_factor_exposures_kernel(
             for j in (3, 2):
                 if a == 1:
                     gather_words(j, a, 0, HALF, "second_pass_low%d" % j)
-                for c in range(HALF_CHUNKS):
-                    m_passes(first_banks[c], j, a, c)
+                for t in range(4):
+                    m_pass(first_banks[t], j, a, t, 0)
         for j in (3, 2):
             gather_words(j, 1, HALF, S, "second_pass_high%d" % j)
         gather_words(2, 0, HALF, S, "second_pass_low3")
@@ -217,21 +215,29 @@ def tile_list_equity_factor_exposures_kernel(
 
         for u in range(2):
             round_w1(nc.scalar.copy, 0, w1_first[u], 8 * u, 8 * (u + 1))
-        m_abs = [sb("m_abs%d" % c if c else "w1_first1", HALF, F32) for c in range(CHUNKS)]
-        for c in range(HALF_CHUNKS):
-            damping_step(c, first_banks[c])
+        m_abs = [sb("w1_first1", 4 * HALF, F32), sb("m_abs1", 4 * HALF, F32)]
+        for t in range(4):
+            magnitude(0, t, first_banks[t])
+        for lo in (0, S):
+            inverse_root(root[0][:, lo : lo + S], m_abs[0][:, lo : lo + S])
+        square(damp[0][:, 0:S], root[0][:, 0:S])
         w4_bf = sb("w4_bf", 4 * N, BF16)
         nc.scalar.copy(
             w4_bf[:].rearrange("p (q i t) -> p q t i", i=2, t=4), w4_raw[:].rearrange("p (t q i) -> p q t i", i=2, t=4)
         )
-        for c in range(HALF_CHUNKS, CHUNKS):
-            acc = bank(c - HALF_CHUNKS)
+        square(damp[0][:, S : 2 * S], root[0][:, S : 2 * S])
+        for t in range(4):
+            acc = bank(t)
             for a in range(2):
                 for j in (3, 2):
-                    m_passes(acc, j, a, c)
-            damping_step(c, acc)
-        damping_step(CHUNKS, None)
-        damping_step(CHUNKS + 1, None)
+                    m_pass(acc, j, a, t, 1)
+            magnitude(1, t, acc)
+        for c in range(HALF_CHUNKS + 1):
+            lo = CHUNK * c
+            if c < HALF_CHUNKS:
+                inverse_root(by_value(root[1], lo, lo + CHUNK), by_value(m_abs[1], lo, lo + CHUNK))
+            if c >= 1:
+                square(by_value(damp[1], lo - CHUNK, lo), by_value(root[1], lo - CHUNK, lo))
 
         gather_words(1, 0, 0, S, "second_pass_low2")
 
@@ -244,11 +250,11 @@ def tile_list_equity_factor_exposures_kernel(
         w4_codes = sb("w4_codes", N, U32)
         w4_scale = sb("w4_scale", N, U8)
         quantize(w1_codes[:, 0:H], w1_scale[:, 0:H], w1_bf[0][:])
+        gather_words(1, 1, 0, HALF, "w1_first0")
         round_w1(nc.vector.tensor_copy, 1, w1_second, 0, 16)
-        gather_words(1, 1, 0, HALF, "w1_second")
-        quantize(w1_codes[:, H : 2 * H], w1_scale[:, H : 2 * H], w1_bf[1][:])
-        gather_words(1, 1, HALF, S, "w1_bf1")
         quantize(w4_codes[:], w4_scale[:], w4_bf[:])
+        quantize(w1_codes[:, H : 2 * H], w1_scale[:, H : 2 * H], w1_bf[1][:])
+        gather_words(1, 1, HALF, S, "w1_second")
 
         a_banks = []
         for c in range(CHUNKS):
@@ -262,7 +268,7 @@ def tile_list_equity_factor_exposures_kernel(
                         lhsT=w1_codes[:, col : col + P].bitcast(FP8X4),
                         lhsT_scale=w1_scale[:, col : col + P],
                         rhs=table_words(1, a, c),
-                        rhs_scale=table_scale(1, a, c),
+                        rhs_scale=table_scale(1, a, CHUNK * c, CHUNK),
                         start=(a == 0 and t == 0),
                         stop=(a == 1 and t == 3),
                     )
@@ -273,10 +279,11 @@ def tile_list_equity_factor_exposures_kernel(
         out_rows = out.rearrange("(f p) j -> p f j", f=2)
 
         def damped(c):
+            lo = CHUNK * (c % HALF_CHUNKS)
             nc.vector.tensor_tensor(
                 h_bf[:, 4 * CHUNK * c : 4 * CHUNK * (c + 1)].rearrange("p (q i t) -> p q t i", t=4, i=2),
                 a_banks[c][:].rearrange("p (t q i) -> p q t i", t=4, i=2),
-                damp[c][:].rearrange("p (q t i) -> p q t i", t=4, i=2),
+                by_value(damp[c // HALF_CHUNKS], lo, lo + CHUNK).rearrange("p t (q i) -> p q t i", i=2),
                 MULT,
             )
 

@@ -116,9 +116,9 @@ def tile_list_equity_factor_exposures_kernel(
         w3_ord = sb("w3_ord", 2 * H, U32)
 
         def reorder(dst, src, parts):
-            nc.vector.tensor_copy(
-                dst.bitcast(I32).rearrange("p (a t g e) -> p a t g e", a=parts, t=4, g=16),
-                src.bitcast(I32).rearrange("p (a g t e) -> p a t g e", a=parts, t=4, g=16),
+            nc.scalar.copy(
+                dst.bitcast(U32).rearrange("p (a t g e) -> p a t g e", a=parts, t=4, g=16),
+                src.bitcast(U32).rearrange("p (a g t e) -> p a t g e", a=parts, t=4, g=16),
             )
 
         reorder(ws_ord[0:16, :], ws_raw[0:16, :], 4)
@@ -190,11 +190,11 @@ def tile_list_equity_factor_exposures_kernel(
             nc.scalar.activation(out=m_abs[half][:, HALF * t : HALF * (t + 1)], in_=acc[:], func=ACT.Abs)
 
         first_banks = [bank(t) for t in range(4)]
-        first_words = sb("w3_raw", S, U32)
+        first_words = sb("first_words3", S, U32)
         picked_words[3, 0, 0] = first_words[:, 0:HALF]
         picked_words[3, 0, 1] = first_words[:, HALF:S]
         gather(picked_words[3, 0, 0], word_win[0], 3, 0, HALF)
-        gather_words(2, 0, 0, HALF, "w2_raw")
+        gather_words(2, 0, 0, HALF, "first_words2")
         gather(picked_words[3, 0, 1], word_win[0], 3, HALF, S)
         for a in range(2):
             for j in (3, 2):
@@ -204,7 +204,7 @@ def tile_list_equity_factor_exposures_kernel(
                     m_pass(first_banks[t], j, a, t, 0)
         for j in (3, 2):
             gather_words(j, 1, HALF, S, "second_pass_high%d" % j)
-        gather_words(2, 0, HALF, S, "second_pass_low3")
+        gather_words(2, 0, HALF, S, "first_words2_high")
         w1_bf = [sb("w1_bf%d" % a, 4 * H, BF16) for a in range(2)]
 
         def round_w1(copy, a, raw, lo, hi):

@@ -63,7 +63,7 @@ def tile_list_equity_factor_exposures_kernel(
         w4_raw = sb("w4_raw", 4 * N, F32)
 
         def load_weight_scales(j, src):
-            nc.sync.dma_start(
+            nc.scalar.dma_start(
                 ws_raw[0:16, 2 * H * (j - 2) : 2 * H * (j - 1)].bitcast(I32).rearrange("q (a c) -> q a c", a=2),
                 src.bitcast(I32).rearrange("a q c -> q a c"),
             )
@@ -72,13 +72,13 @@ def tile_list_equity_factor_exposures_kernel(
             nc.sync.dma_start(word_win[a][:].bitcast(I32), tab_words[a].rearrange("p t i -> p (t i)").bitcast(I32))
 
         nc.sync.dma_start(scale_win[ROWS_FROM:P, :].bitcast(I32), tab_scales.bitcast(I32).rearrange("a q t -> q a t"))
-        load_weight_scales(2, w2_scales)
-        load_weight_scales(3, w3_scales)
         nc.sync.dma_start(lists[2][:], offs2)
         nc.sync.dma_start(lists[3][:], offs3)
-        nc.sync.dma_start(lists[1][:], offs)
+        load_weight_scales(2, w2_scales)
+        load_weight_scales(3, w3_scales)
         nc.scalar.activation(out=warm[:, 8:9], in_=warm[:, 0:1], func=ACT.Abs_reciprocal_sqrt)
         load_words(0)
+        nc.sync.dma_start(lists[1][:], offs)
 
         picked_late = sb("picked_late", 2 * S, U8)
         picked_words = {}
@@ -218,14 +218,9 @@ def tile_list_equity_factor_exposures_kernel(
         m_abs = [sb("w1_first1", 4 * HALF, F32), sb("m_abs1", 4 * HALF, F32)]
         for t in range(4):
             magnitude(0, t, first_banks[t])
-        for lo in (0, S):
-            inverse_root(root[0][:, lo : lo + S], m_abs[0][:, lo : lo + S])
-        square(damp[0][:, 0:S], root[0][:, 0:S])
-        w4_bf = sb("w4_bf", 4 * N, BF16)
-        nc.scalar.copy(
-            w4_bf[:].rearrange("p (q i t) -> p q t i", i=2, t=4), w4_raw[:].rearrange("p (t q i) -> p q t i", i=2, t=4)
-        )
-        square(damp[0][:, S : 2 * S], root[0][:, S : 2 * S])
+        for step, dst, src in ((inverse_root, root[0], m_abs[0]), (square, damp[0], root[0])):
+            for lo in (0, S):
+                step(dst[:, lo : lo + S], src[:, lo : lo + S])
         for t in range(4):
             acc = bank(t)
             for a in range(2):
@@ -252,8 +247,12 @@ def tile_list_equity_factor_exposures_kernel(
         quantize(w1_codes[:, 0:H], w1_scale[:, 0:H], w1_bf[0][:])
         gather_words(1, 1, 0, HALF, "w1_first0")
         round_w1(nc.vector.tensor_copy, 1, w1_second, 0, 16)
-        quantize(w4_codes[:], w4_scale[:], w4_bf[:])
+        w4_bf = sb("w1_bf0", 4 * N, BF16)
+        nc.vector.tensor_copy(
+            w4_bf[:].rearrange("p (q i t) -> p q t i", i=2, t=4), w4_raw[:].rearrange("p (t q i) -> p q t i", i=2, t=4)
+        )
         quantize(w1_codes[:, H : 2 * H], w1_scale[:, H : 2 * H], w1_bf[1][:])
+        quantize(w4_codes[:], w4_scale[:], w4_bf[:])
         gather_words(1, 1, HALF, S, "w1_second")
 
         a_banks = []

@@ -243,17 +243,17 @@ def tile_list_equity_factor_exposures_kernel(
             nc.vector.quantize_mx(out=codes.bitcast(FP8X4), scales=scales, in_=values)
 
         w4_codes = sb("w4_codes", N, U32)
-        w4_scale = sb("w4_scale", N, U8)
         quantize(w1_codes[:, 0:H], w1_scale[:, 0:H], w1_bf[0][:])
         gather_words(1, 1, 0, HALF, "w1_first0")
         round_w1(nc.vector.tensor_copy, 1, w1_second, 0, 16)
-        w4_bf = sb("w1_bf0", 4 * N, BF16)
-        nc.vector.tensor_copy(
-            w4_bf[:].rearrange("p (q i t) -> p q t i", i=2, t=4), w4_raw[:].rearrange("p (t q i) -> p q t i", i=2, t=4)
-        )
-        quantize(w1_codes[:, H : 2 * H], w1_scale[:, H : 2 * H], w1_bf[1][:])
-        quantize(w4_codes[:], w4_scale[:], w4_bf[:])
+        for lo in (0, H // 2):
+            cols = slice(H + lo, H + lo + H // 2)
+            quantize(w1_codes[:, cols], w1_scale[:, cols], w1_bf[1][:, 4 * lo : 4 * lo + 2 * H])
         gather_words(1, 1, HALF, S, "w1_second")
+        w4_bf = sb("word_win1", 4 * N, BF16)
+        nc.gpsimd.tensor_scalar(
+            w4_bf[:].rearrange("p (n t) -> p n t", t=4), w4_raw[:].rearrange("p (t n) -> p n t", t=4), 1.0, 0.0, MULT, ADD
+        )
 
         a_banks = []
         for c in range(CHUNKS):
@@ -286,7 +286,7 @@ def tile_list_equity_factor_exposures_kernel(
                 MULT,
             )
 
-        def exposures(lo, hi, banks):
+        def exposures(lo, hi, banks, w4_scale):
             width = hi - lo
             result = sb("result%d" % lo, 2 * width, F32)
             tiles = {b: bank(b) for b in sorted(set(banks))}
@@ -314,11 +314,19 @@ def tile_list_equity_factor_exposures_kernel(
             nc.sync.dma_start(out_rows[:, :, lo:hi], result[:].rearrange("p (f j) -> p f j", f=2))
 
         groups = [(0, 2, (4, 4)), (2, 4, (5, 5)), (4, 6, (6, 6)), (6, 7, (7, 7)), (7, 8, (0, 1))]
+        waiting = []
         for c in range(CHUNKS + 1):
             if c < CHUNKS:
                 damped(c)
+            if c == HALF_CHUNKS:
+                w4_scale = sb("damp0", N, U8)
+                quantize(w4_codes[:], w4_scale[:], w4_bf[:])
             for first_chunk, end_chunk, banks in groups:
                 if end_chunk == c:
                     lo, hi = CHUNK * first_chunk, CHUNK * end_chunk
                     quantize(h_codes[:, lo:hi], h_scale[:, lo:hi], h_bf[:, 4 * lo : 4 * hi])
-                    exposures(lo, hi, banks)
+                    waiting.append((lo, hi, banks))
+            if c >= HALF_CHUNKS:
+                for lo, hi, banks in waiting:
+                    exposures(lo, hi, banks, w4_scale)
+                waiting = []

@@ -89,12 +89,14 @@ def tile_list_equity_factor_exposures_kernel(
         def gather_words(j, a, lo, hi, name):
             dst = sb(name, hi - lo, U32)
             gather(dst[:], word_win[a], j, lo, hi)
-            for half in range(lo // HALF, hi // HALF):
-                picked_words[j, a, half] = dst[:, HALF * half - lo : HALF * (half + 1) - lo]
+            for first in range(lo, hi, HALF):
+                end = min(hi, first + HALF)
+                picked_words.setdefault((j, a, first // HALF), []).append((first, end, dst[:, first - lo : end - lo]))
 
         def table_words(j, a, c):
             lo = CHUNK * c
-            return picked_words[j, a, lo // HALF][:, lo % HALF : lo % HALF + CHUNK].bitcast(FP8X4)
+            ((first, end, words),) = picked_words[j, a, lo // HALF]
+            return words[:, lo - first : lo - first + CHUNK].bitcast(FP8X4)
 
         def spread(planes, picked):
             for q in (0, 2, 1, 3):
@@ -167,15 +169,16 @@ def tile_list_equity_factor_exposures_kernel(
             else:
                 lhsT = w3_ord[:, col : col + P].bitcast(FP8X4)
             scol = 2 * H * (j - 2) + col
-            nc.tensor.matmul_mx(
-                out=acc[:],
-                lhsT=lhsT,
-                lhsT_scale=ws_planes[:, scol : scol + P],
-                rhs=picked_words[j, a, half].bitcast(FP8X4),
-                rhs_scale=table_scale(j, a, HALF * half, HALF),
-                start=(a == 0 and j == 3),
-                stop=(a == 1 and j == 2),
-            )
+            for lo, hi, words in picked_words[j, a, half]:
+                nc.tensor.matmul_mx(
+                    out=acc[:, lo - HALF * half : hi - HALF * half],
+                    lhsT=lhsT,
+                    lhsT_scale=ws_planes[:, scol : scol + P],
+                    rhs=words.bitcast(FP8X4),
+                    rhs_scale=table_scale(j, a, lo, hi - lo),
+                    start=(a == 0 and j == 3),
+                    stop=(a == 1 and j == 2),
+                )
 
         root = [sb("root%d" % half, 4 * HALF, F32) for half in range(2)]
         damp = [sb("damp%d" % half, 4 * HALF, F32) for half in range(2)]
@@ -190,12 +193,9 @@ def tile_list_equity_factor_exposures_kernel(
             nc.scalar.activation(out=m_abs[half][:, HALF * t : HALF * (t + 1)], in_=acc[:], func=ACT.Abs)
 
         first_banks = [bank(t) for t in range(4)]
-        first_words = sb("first_words3", S, U32)
-        picked_words[3, 0, 0] = first_words[:, 0:HALF]
-        picked_words[3, 0, 1] = first_words[:, HALF:S]
-        gather(picked_words[3, 0, 0], word_win[0], 3, 0, HALF)
-        gather_words(2, 0, 0, HALF, "first_words2")
-        gather(picked_words[3, 0, 1], word_win[0], 3, HALF, S)
+        gather_words(3, 0, 0, HALF, "first_pass_low3")
+        gather_words(2, 0, 0, HALF, "first_pass_low2")
+        gather_words(3, 0, HALF, S, "first_pass_high3")
         for a in range(2):
             for j in (3, 2):
                 if a == 1:
@@ -204,7 +204,8 @@ def tile_list_equity_factor_exposures_kernel(
                     m_pass(first_banks[t], j, a, t, 0)
         for j in (3, 2):
             gather_words(j, 1, HALF, S, "second_pass_high%d" % j)
-        gather_words(2, 0, HALF, S, "first_words2_high")
+        gather_words(2, 0, HALF, S - S // 4, "first_pass_high2")
+        gather_words(2, 0, S - S // 4, S, "second_pass_low3")
         w1_bf = [sb("w1_bf%d" % a, 4 * H, BF16) for a in range(2)]
 
         def round_w1(copy, a, raw, lo, hi):
@@ -311,7 +312,10 @@ def tile_list_equity_factor_exposures_kernel(
                     nc.scalar.activation(
                         out=dst, in_=sums[f], func=ACT.Identity, scale=fs[:, f : f + 1], bias=fb[:, f : f + 1]
                     )
-            nc.sync.dma_start(out_rows[:, :, lo:hi], result[:].rearrange("p (f j) -> p f j", f=2))
+                if banks[0] != banks[1]:
+                    (nc.sync if f else nc.scalar).dma_start(out_rows[:, f, lo:hi], dst)
+            if banks[0] == banks[1]:
+                nc.sync.dma_start(out_rows[:, :, lo:hi], result[:].rearrange("p (f j) -> p f j", f=2))
 
         groups = [(0, 2, (4, 4)), (2, 4, (5, 5)), (4, 6, (6, 6)), (6, 7, (7, 7)), (7, 8, (0, 1))]
         waiting = []

@@ -19,6 +19,7 @@ ADD = mybir.AluOpType.add
 
 P = 128
 HALF = S // 2
+QUARTER = S // 4
 CHUNK = 128
 CHUNKS = S // CHUNK
 HALF_CHUNKS = CHUNKS // 2
@@ -39,9 +40,6 @@ def tile_list_equity_factor_exposures_kernel(
         def bank(b):
             return psum.tile([P, HALF], F32, name="bank%d" % b)
 
-        def by_value(tile, lo, hi):
-            return tile[:].rearrange("p (t n) -> p t n", t=4)[:, :, lo:hi]
-
         lists = {j: keep.tile([P, S // 16], U16, name="list%d" % j) for j in (1, 2, 3)}
         scale_win = sb("scale_win", T, U8)
         word_win = [sb("word_win%d" % a, T, U32) for a in range(2)]
@@ -52,51 +50,29 @@ def tile_list_equity_factor_exposures_kernel(
         warm = sb("warm", 16, F32)
         fs = sb("fs", 2, F32)
         fb = sb("fb", 2, F32)
+        w2_raw = sb("w2_raw", 4 * H, U8)
+        w3_raw = sb("w3_raw", 2 * H, U32)
+        w4_raw = sb("w4_raw", 4 * N, F32)
+        w2_ord = sb("w2_ord", 4 * H, U8)
+        w3_ord = sb("w3_ord", 2 * H, U32)
+        picked_early = sb("picked_early", S, U8)
+        picked_late = sb("picked_late", 2 * S, U8)
+        w1_first = [sb("w1_first%d" % u, 2 * H, F32) for u in range(2)]
+        w1_second = sb("w1_second", 4 * H, F32)
 
         nc.vector.memset(scale_win[0:ROWS_FROM, :].bitcast(I32), 0)
         nc.vector.memset(ws_planes[:].bitcast(I32), 0)
         nc.gpsimd.memset(warm[:, 0:8], 1.0)
         nc.gpsimd.memset(tab_planes[:].bitcast(I32), 0)
 
-        w2_raw = sb("w2_raw", 4 * H, U8)
-        w3_raw = sb("w3_raw", 2 * H, U32)
-        w4_raw = sb("w4_raw", 4 * N, F32)
-
-        def load_weight_scales(j, src):
-            nc.scalar.dma_start(
-                ws_raw[0:16, 2 * H * (j - 2) : 2 * H * (j - 1)].bitcast(I32).rearrange("q (a c) -> q a c", a=2),
-                src.bitcast(I32).rearrange("a q c -> q a c"),
-            )
-
-        def load_words(a):
-            nc.sync.dma_start(word_win[a][:].bitcast(I32), tab_words[a].rearrange("p t i -> p (t i)").bitcast(I32))
-
-        nc.sync.dma_start(scale_win[ROWS_FROM:P, :].bitcast(I32), tab_scales.bitcast(I32).rearrange("a q t -> q a t"))
-        nc.sync.dma_start(lists[2][:], offs2)
-        nc.sync.dma_start(lists[3][:], offs3)
-        load_weight_scales(2, w2_scales)
-        load_weight_scales(3, w3_scales)
-        nc.scalar.activation(out=warm[:, 8:9], in_=warm[:, 0:1], func=ACT.Abs_reciprocal_sqrt)
-        load_words(0)
-        nc.sync.dma_start(lists[1][:], offs)
-
-        picked_late = sb("picked_late", 2 * S, U8)
-        picked_words = {}
-
         def gather(dst, window, j, lo, hi):
             nc.vector.tensor_copy(dst, window[:].indirect(lists[j][:, lo // 16 : hi // 16]))
 
-        def gather_words(j, a, lo, hi, name):
-            dst = sb(name, hi - lo, U32)
-            gather(dst[:], word_win[a], j, lo, hi)
-            for first in range(lo, hi, HALF):
-                end = min(hi, first + HALF)
-                picked_words.setdefault((j, a, first // HALF), []).append((first, end, dst[:, first - lo : end - lo]))
-
-        def table_words(j, a, c):
-            lo = CHUNK * c
-            ((first, end, words),) = picked_words[j, a, lo // HALF]
-            return words[:, lo - first : lo - first + CHUNK].bitcast(FP8X4)
+        def reorder(dst, src, parts):
+            nc.scalar.copy(
+                dst.bitcast(U32).rearrange("p (a t g e) -> p a t g e", a=parts, t=4, g=16),
+                src.bitcast(U32).rearrange("p (a g t e) -> p a t g e", a=parts, t=4, g=16),
+            )
 
         def spread(planes, picked):
             for q in (0, 2, 1, 3):
@@ -105,24 +81,20 @@ def tile_list_equity_factor_exposures_kernel(
                     picked[ROWS_FROM + 8 * q : ROWS_FROM + 8 * q + 8, :].bitcast(I32),
                 )
 
-        def table_scale(j, a, lo, width):
-            if j == 1:
-                col = 2 * S * (a + 1) + S + lo
-            elif lo < HALF:
-                col = S * a + HALF * (j - 2) + lo
-            else:
-                col = 2 * S * (a + 1) + HALF * (j - 2) + lo - HALF
-            return tab_planes[:, col : col + width]
+        def load_words(a):
+            nc.sync.dma_start(word_win[a][:].bitcast(I32), tab_words[a].rearrange("p t i -> p (t i)").bitcast(I32))
 
-        w2_ord = sb("w2_ord", 4 * H, U8)
-        w3_ord = sb("w3_ord", 2 * H, U32)
-
-        def reorder(dst, src, parts):
-            nc.scalar.copy(
-                dst.bitcast(U32).rearrange("p (a t g e) -> p a t g e", a=parts, t=4, g=16),
-                src.bitcast(U32).rearrange("p (a g t e) -> p a t g e", a=parts, t=4, g=16),
+        nc.sync.dma_start(scale_win[ROWS_FROM:P, :].bitcast(I32), tab_scales.bitcast(I32).rearrange("a q t -> q a t"))
+        nc.sync.dma_start(lists[2][:], offs2)
+        nc.sync.dma_start(lists[3][:], offs3)
+        nc.sync.dma_start(lists[1][:], offs)
+        for j, src in ((2, w2_scales), (3, w3_scales)):
+            nc.scalar.dma_start(
+                ws_raw[0:16, 2 * H * (j - 2) : 2 * H * (j - 1)].bitcast(I32).rearrange("q (a c) -> q a c", a=2),
+                src.bitcast(I32).rearrange("a q c -> q a c"),
             )
-
+        nc.scalar.activation(out=warm[:, 8:9], in_=warm[:, 0:1], func=ACT.Abs_reciprocal_sqrt)
+        load_words(0)
         reorder(ws_ord[0:16, :], ws_raw[0:16, :], 4)
         for r in range(4):
             nc.sync.dma_start(ws_planes[r:P:32, :].bitcast(I32), ws_ord[r:16:4, :].bitcast(I32))
@@ -133,16 +105,11 @@ def tile_list_equity_factor_exposures_kernel(
         nc.sync.dma_start(
             w2_raw[:].bitcast(I32).rearrange("p (a b) -> p a b", a=2), w2_words.bitcast(I32).rearrange("a p b -> p a b")
         )
-
-        picked_early = sb("picked_early", S, U8)
         gather(picked_early[:, 0:HALF], scale_win, 2, 0, HALF)
         gather(picked_early[:, HALF:S], scale_win, 3, 0, HALF)
         spread(tab_planes[:, 0 : 2 * S], picked_early)
         load_words(1)
-
         w1_rows = w1.rearrange("(a p j) c -> a p j c", a=2, j=4)
-        w1_first = [sb("w1_first%d" % u, 2 * H, F32) for u in range(2)]
-        w1_second = sb("w1_second", 4 * H, F32)
         for u in range(2):
             nc.sync.dma_start(
                 w1_first[u][:].rearrange("p (j c) -> p j c", j=4), w1_rows[0][:, :, H // 2 * u : H // 2 * (u + 1)]
@@ -150,115 +117,145 @@ def tile_list_equity_factor_exposures_kernel(
         gather(picked_late[:, 0:HALF], scale_win, 2, HALF, S)
         gather(picked_late[:, HALF:S], scale_win, 3, HALF, S)
         gather(picked_late[:, S : 2 * S], scale_win, 1, 0, S)
-        spread(tab_planes[:, 2 * S : 6 * S], picked_late)
         nc.sync.dma_start(w1_second[:].rearrange("p (j c) -> p j c", j=4), w1_rows[1])
+        spread(tab_planes[:, 2 * S : 6 * S], picked_late)
         w4_rows = w4.rearrange("(g t i) n -> t g i n", t=4, i=8)
         for t in range(4):
             nc.sync.dma_start(w4_raw[:, N * t : N * (t + 1)], w4_rows[t])
         with nc.allow_non_contiguous_dma(reason="factor 128 f + p has its scale and base level at [p, f]"):
             nc.sync.dma_start(fs[:], fscale.rearrange("(f p) -> p f", f=2))
             nc.sync.dma_start(fb[:], fbase.rearrange("(f p) -> p f", f=2))
-
         reorder(w3_ord[:], w3_raw[:], 2)
         reorder(w2_ord[:], w2_raw[:], 2)
 
-        def m_pass(acc, j, a, t, half):
+        def table_scale(j, a, lo, width):
+            if j == 1:
+                col = 2 * S * (a + 1) + S + lo
+            elif lo < HALF:
+                col = S * a + HALF * (j - 2) + lo
+            else:
+                col = 2 * S * (a + 1) + HALF * (j - 2) + lo - HALF
+            return tab_planes[:, col : col + width]
+
+        m_words = {}
+
+        def gather_m(dst, j, a, first, end):
+            gather(dst, word_win[a], j, QUARTER * first, QUARTER * end)
+            for q in range(first, end):
+                m_words[j, a, q] = dst[:, QUARTER * (q - first) : QUARTER * (q - first + 1)]
+
+        for j, a, first, end in (
+            (3, 0, 0, 2), (2, 0, 0, 2), (3, 0, 2, 4), (2, 0, 2, 3),
+            (3, 1, 0, 1), (2, 1, 0, 1), (3, 1, 1, 2), (2, 1, 1, 2), (3, 1, 2, 4), (2, 1, 2, 4),
+        ):
+            words = sb("m_words%d%d%d" % (j, a, first), QUARTER * (end - first), U32)
+            gather_m(words[:], j, a, first, end)
+
+        m_banks = [bank(b) for b in range(8)]
+
+        def m_pass(j, a, q, t):
             col = H * a + P * t
             if j == 2:
                 lhsT = w2_ord[:, 2 * col : 2 * (col + P)].bitcast(FP4X4)
             else:
                 lhsT = w3_ord[:, col : col + P].bitcast(FP8X4)
             scol = 2 * H * (j - 2) + col
-            for lo, hi, words in picked_words[j, a, half]:
-                nc.tensor.matmul_mx(
-                    out=acc[:, lo - HALF * half : hi - HALF * half],
-                    lhsT=lhsT,
-                    lhsT_scale=ws_planes[:, scol : scol + P],
-                    rhs=words.bitcast(FP8X4),
-                    rhs_scale=table_scale(j, a, lo, hi - lo),
-                    start=(a == 0 and j == 3),
-                    stop=(a == 1 and j == 2),
-                )
+            nc.tensor.matmul_mx(
+                out=m_banks[2 * q + t // 2][:, QUARTER * (t % 2) : QUARTER * (t % 2 + 1)],
+                lhsT=lhsT,
+                lhsT_scale=ws_planes[:, scol : scol + P],
+                rhs=m_words[j, a, q].bitcast(FP8X4),
+                rhs_scale=table_scale(j, a, QUARTER * q, QUARTER),
+                start=(a == 0 and j == 3 and t % 2 == 0),
+                stop=(a == 1 and j == 2 and t % 2 == 1),
+            )
 
-        root = [sb("root%d" % half, 4 * HALF, F32) for half in range(2)]
-        damp = [sb("damp%d" % half, 4 * HALF, F32) for half in range(2)]
-
-        def inverse_root(dst, src):
-            nc.scalar.activation(out=dst, in_=src, func=ACT.Abs_reciprocal_sqrt, bias=1.0)
-
-        def square(dst, src):
-            nc.scalar.activation(out=dst, in_=src, func=ACT.Square)
-
-        def magnitude(half, t, acc):
-            nc.scalar.activation(out=m_abs[half][:, HALF * t : HALF * (t + 1)], in_=acc[:], func=ACT.Abs)
-
-        first_banks = [bank(t) for t in range(4)]
-        gather_words(3, 0, 0, HALF, "first_pass_low3")
-        gather_words(2, 0, 0, HALF, "first_pass_low2")
-        gather_words(3, 0, HALF, S, "first_pass_high3")
-        for a in range(2):
-            for j in (3, 2):
-                if a == 1:
-                    gather_words(j, a, 0, HALF, "second_pass_low%d" % j)
-                for t in range(4):
-                    m_pass(first_banks[t], j, a, t, 0)
         for j in (3, 2):
-            gather_words(j, 1, HALF, S, "second_pass_high%d" % j)
-        gather_words(2, 0, HALF, S - S // 4, "first_pass_high2")
-        gather_words(2, 0, S - S // 4, S, "second_pass_low3")
-        w1_bf = [sb("w1_bf%d" % a, 4 * H, BF16) for a in range(2)]
-
-        def round_w1(copy, a, raw, lo, hi):
-            dst = w1_bf[a][:].rearrange("p (t g u i j) -> p t g u j i", t=4, g=16, u=4, j=4)
-            src = raw[:].rearrange("p (j g t u i) -> p t g u j i", t=4, g=hi - lo, u=4, j=4)
-            for t in range(4):
-                copy(dst[:, t, lo:hi], src[:, t])
-
-        for u in range(2):
-            round_w1(nc.scalar.copy, 0, w1_first[u], 8 * u, 8 * (u + 1))
-        m_abs = [sb("w1_first1", 4 * HALF, F32), sb("m_abs1", 4 * HALF, F32)]
-        for t in range(4):
-            magnitude(0, t, first_banks[t])
-        for step, dst, src in ((inverse_root, root[0], m_abs[0]), (square, damp[0], root[0])):
-            for lo in (0, S):
-                step(dst[:, lo : lo + S], src[:, lo : lo + S])
-        for t in range(4):
-            acc = bank(t)
-            for a in range(2):
-                for j in (3, 2):
-                    m_pass(acc, j, a, t, 1)
-            magnitude(1, t, acc)
-        for c in range(HALF_CHUNKS + 1):
-            lo = CHUNK * c
-            if c < HALF_CHUNKS:
-                inverse_root(by_value(root[1], lo, lo + CHUNK), by_value(m_abs[1], lo, lo + CHUNK))
-            if c >= 1:
-                square(by_value(damp[1], lo - CHUNK, lo), by_value(root[1], lo - CHUNK, lo))
-
-        gather_words(1, 0, 0, S, "second_pass_low2")
-
-        w1_codes = sb("w1_codes", 2 * H, U32)
-        w1_scale = sb("w1_scale", 2 * H, U8)
+            for q in range(2):
+                for t in range(4):
+                    m_pass(j, 0, q, t)
+        for q in range(2):
+            for j in (3, 2):
+                for t in range(4):
+                    m_pass(j, 1, q, t)
 
         def quantize(codes, scales, values):
             nc.vector.quantize_mx(out=codes.bitcast(FP8X4), scales=scales, in_=values)
 
-        w4_codes = sb("w4_codes", N, U32)
-        quantize(w1_codes[:, 0:H], w1_scale[:, 0:H], w1_bf[0][:])
-        gather_words(1, 1, 0, HALF, "w1_first0")
-        round_w1(nc.vector.tensor_copy, 1, w1_second, 0, 16)
-        for lo in (0, H // 2):
-            cols = slice(H + lo, H + lo + H // 2)
-            quantize(w1_codes[:, cols], w1_scale[:, cols], w1_bf[1][:, 4 * lo : 4 * lo + 2 * H])
-        gather_words(1, 1, HALF, S, "w1_second")
-        w4_bf = sb("word_win1", 4 * N, BF16)
-        nc.gpsimd.tensor_scalar(
-            w4_bf[:].rearrange("p (n t) -> p n t", t=4), w4_raw[:].rearrange("p (t n) -> p n t", t=4), 1.0, 0.0, MULT, ADD
-        )
+        def round_on_gpsimd(dst, src):
+            nc.gpsimd.tensor_scalar(dst, src, 1.0, 0.0, MULT, ADD)
+
+        def in_value_order(tile):
+            return tile.rearrange("p (t g e) -> p g t e", t=4, g=16)
+
+        def rows_side_by_side(raw):
+            return raw[:].rearrange("p (j c) -> p c j", j=4)
+
+        w1_codes = sb("w1_codes", 2 * H, U32)
+        w1_scale = sb("w1_scale", 2 * H, U8)
+        rounded = sb("rounded", 8 * H, BF16)
+        dst = rounded[:, 0 : 4 * H].rearrange("p (t g u i j) -> p t g u j i", t=4, g=16, u=4, j=4)
+        src = w1_first[0][:].rearrange("p (j g t u i) -> p t g u j i", t=4, g=8, u=4, j=4)
+        for t in range(4):
+            nc.scalar.copy(dst[:, t, 0:8], src[:, t])
+        round_on_gpsimd(in_value_order(rounded[:, 0 : 4 * H])[:, 8:16], rows_side_by_side(w1_first[1]))
+        round_on_gpsimd(in_value_order(rounded[:, 4 * H : 8 * H]), rows_side_by_side(w1_second))
+        a_words = {(1, 0): sb("a_words10", HALF, U32)[:]}
+        held = sb("w1_first1", HALF + QUARTER, U32)
+        gather_m(held[:, HALF:], 2, 0, 3, 4)
+        for q in range(2, 4):
+            for a in range(2):
+                for j in (3, 2):
+                    for t in range(4):
+                        m_pass(j, a, q, t)
+        a_words[0, 0] = held[:, 0:HALF]
+        for a in (1, 0):
+            gather(a_words[a, 0], word_win[a], 1, 0, HALF)
+        quantize(w1_codes[:], w1_scale[:], rounded[:])
+        held = sb("w1_second", S, U32)
+        for a in range(2):
+            a_words[a, 1] = held[:, HALF * a : HALF * (a + 1)]
+            gather(a_words[a, 1], word_win[a], 1, HALF, S)
+        w4_bf = sb("rounded", 4 * N, BF16)
+        round_on_gpsimd(w4_bf[:].rearrange("p (n t) -> p n t", t=4), w4_raw[:].rearrange("p (t n) -> p n t", t=4))
+
+        m_abs = [sb("w1_first0", 2 * S, F32), sb("m_abs1", 2 * S, F32)]
+        root = [sb("root%d" % half, 2 * S, F32) for half in range(2)]
+        damp = [sb("damp%d" % half, 2 * S, F32) for half in range(2)]
+
+        def of_bank(tiles, b):
+            return tiles[b // 4][:, HALF * (b % 4) : HALF * (b % 4 + 1)]
+
+        def of_chunk(tiles, c):
+            view = tiles[c // HALF_CHUNKS][:].rearrange("p (q t n) -> p q t n", q=2, t=4)
+            return view[:, c // 2 % 2, :, CHUNK * (c % 2) : CHUNK * (c % 2 + 1)]
+
+        def magnitude(b):
+            nc.scalar.activation(out=of_bank(m_abs, b), in_=m_banks[b][:], func=ACT.Abs)
+
+        def inverse_root(part, i):
+            nc.scalar.activation(out=part(root, i), in_=part(m_abs, i), func=ACT.Abs_reciprocal_sqrt, bias=1.0)
+
+        def square(c):
+            nc.scalar.activation(out=of_chunk(damp, c), in_=of_chunk(root, c), func=ACT.Square)
+
+        for b in range(2):
+            magnitude(b)
+        for q in range(4):
+            for i in (2 * q, 2 * q + 1):
+                inverse_root(of_chunk if q else of_bank, i)
+            for i in (2 * q, 2 * q + 1):
+                if q < 3:
+                    magnitude(i + 2)
+                square(i)
+
+        def a_rhs(a, c):
+            lo = CHUNK * (c % HALF_CHUNKS)
+            return a_words[a, c // HALF_CHUNKS][:, lo : lo + CHUNK]
 
         a_banks = []
         for c in range(CHUNKS):
-            acc = bank((c + HALF_CHUNKS) % CHUNKS)
+            acc = bank(c)
             a_banks.append(acc)
             for a in range(2):
                 for t in range(4):
@@ -267,7 +264,7 @@ def tile_list_equity_factor_exposures_kernel(
                         out=acc[:, CHUNK * t : CHUNK * (t + 1)],
                         lhsT=w1_codes[:, col : col + P].bitcast(FP8X4),
                         lhsT_scale=w1_scale[:, col : col + P],
-                        rhs=table_words(1, a, c),
+                        rhs=a_rhs(a, c).bitcast(FP8X4),
                         rhs_scale=table_scale(1, a, CHUNK * c, CHUNK),
                         start=(a == 0 and t == 0),
                         stop=(a == 1 and t == 3),
@@ -275,21 +272,20 @@ def tile_list_equity_factor_exposures_kernel(
 
         h_bf = sb("h_bf", 4 * S, BF16)
         h_codes = sb("h_codes", S, U32)
-        h_scale = sb("h_scale", S, U8)
+        w4_codes = sb("w4_codes", N, U32)
         out_rows = out.rearrange("(f p) j -> p f j", f=2)
 
         def damped(c):
-            lo = CHUNK * (c % HALF_CHUNKS)
             nc.vector.tensor_tensor(
                 h_bf[:, 4 * CHUNK * c : 4 * CHUNK * (c + 1)].rearrange("p (q i t) -> p q t i", t=4, i=2),
                 a_banks[c][:].rearrange("p (t q i) -> p q t i", t=4, i=2),
-                by_value(damp[c // HALF_CHUNKS], lo, lo + CHUNK).rearrange("p t (q i) -> p q t i", i=2),
+                of_chunk(damp, c).rearrange("p t (q i) -> p q t i", i=2),
                 MULT,
             )
 
-        def exposures(lo, hi, banks, w4_scale):
+        def exposures(lo, hi, banks, late_scale):
             width = hi - lo
-            result = sb("result%d" % lo, 2 * width, F32)
+            result = results[:, 2 * lo : 2 * hi]
             tiles = {b: bank(b) for b in sorted(set(banks))}
             sums = []
             for f in range(2):
@@ -298,14 +294,14 @@ def tile_list_equity_factor_exposures_kernel(
                 nc.tensor.matmul_mx(
                     out=sums[f],
                     lhsT=w4_codes[:, P * f : P * (f + 1)].bitcast(FP8X4),
-                    lhsT_scale=w4_scale[:, P * f : P * (f + 1)],
+                    lhsT_scale=late_scale[:, S + P * f : S + P * (f + 1)],
                     rhs=h_codes[:, lo:hi].bitcast(FP8X4),
-                    rhs_scale=h_scale[:, lo:hi],
+                    rhs_scale=late_scale[:, lo:hi],
                     start=True,
                     stop=True,
                 )
             for f in range(2):
-                dst = result[:, width * f : width * (f + 1)]
+                dst = results[:, 2 * lo + width * f : 2 * lo + width * (f + 1)]
                 if banks[f] != banks[0]:
                     nc.vector.tensor_scalar(dst, sums[f], fs[:, f : f + 1], fb[:, f : f + 1], MULT, ADD)
                 else:
@@ -315,22 +311,20 @@ def tile_list_equity_factor_exposures_kernel(
                 if banks[0] != banks[1]:
                     (nc.sync if f else nc.scalar).dma_start(out_rows[:, f, lo:hi], dst)
             if banks[0] == banks[1]:
-                nc.sync.dma_start(out_rows[:, :, lo:hi], result[:].rearrange("p (f j) -> p f j", f=2))
+                nc.sync.dma_start(out_rows[:, :, lo:hi], result.rearrange("p (f j) -> p f j", f=2))
 
-        groups = [(0, 2, (4, 4)), (2, 4, (5, 5)), (4, 6, (6, 6)), (6, 7, (7, 7)), (7, 8, (0, 1))]
-        waiting = []
-        for c in range(CHUNKS + 1):
+        results = sb("m_abs1", 2 * S, F32)
+        groups = [(0, 2, (0, 0)), (2, 4, (1, 1)), (4, 6, (2, 2)), (6, 7, (3, 3)), (7, 8, (4, 5))]
+        for c in range(HALF_CHUNKS):
+            damped(c)
+        late_scale = sb("damp0", S + N, U8)
+        quantize(w4_codes[:], late_scale[:, S : S + N], w4_bf[:])
+        done = 0
+        for c in range(HALF_CHUNKS, CHUNKS + 1):
             if c < CHUNKS:
                 damped(c)
-            if c == HALF_CHUNKS:
-                w4_scale = sb("damp0", N, U8)
-                quantize(w4_codes[:], w4_scale[:], w4_bf[:])
-            for first_chunk, end_chunk, banks in groups:
-                if end_chunk == c:
-                    lo, hi = CHUNK * first_chunk, CHUNK * end_chunk
-                    quantize(h_codes[:, lo:hi], h_scale[:, lo:hi], h_bf[:, 4 * lo : 4 * hi])
-                    waiting.append((lo, hi, banks))
-            if c >= HALF_CHUNKS:
-                for lo, hi, banks in waiting:
-                    exposures(lo, hi, banks, w4_scale)
-                waiting = []
+            while done < len(groups) and groups[done][1] <= c:
+                lo, hi = CHUNK * groups[done][0], CHUNK * groups[done][1]
+                quantize(h_codes[:, lo:hi], late_scale[:, lo:hi], h_bf[:, 4 * lo : 4 * hi])
+                exposures(lo, hi, groups[done][2], late_scale)
+                done += 1

@@ -55,8 +55,7 @@ def tile_list_equity_factor_exposures_kernel(
         w4_raw = sb("w4_raw", 4 * N, F32)
         w2_ord = sb("w2_ord", 4 * H, U8)
         w3_ord = sb("w3_ord", 2 * H, U32)
-        picked_early = sb("picked_early", S, U8)
-        picked_late = sb("picked_late", 2 * S, U8)
+        picked = [sb("picked%d" % group, S, U8) for group in range(3)]
         w1_first = [sb("w1_first%d" % u, 2 * H, F32) for u in range(2)]
         w1_second = sb("w1_second", 4 * H, F32)
 
@@ -74,11 +73,13 @@ def tile_list_equity_factor_exposures_kernel(
                 src.bitcast(U32).rearrange("p (a g t e) -> p a t g e", a=parts, t=4, g=16),
             )
 
-        def spread(planes, picked):
+        def spread(group):
             for q in (0, 2, 1, 3):
                 nc.sync.dma_start(
-                    planes[32 * q : 32 * q + 4].bitcast(I32).rearrange("r (a n) -> r a n", a=2),
-                    picked[ROWS_FROM + 8 * q : ROWS_FROM + 8 * q + 8, :].bitcast(I32),
+                    tab_planes[32 * q : 32 * q + 4, 2 * S * group : 2 * S * (group + 1)]
+                    .bitcast(I32)
+                    .rearrange("r (a n) -> r a n", a=2),
+                    picked[group][ROWS_FROM + 8 * q : ROWS_FROM + 8 * q + 8, :].bitcast(I32),
                 )
 
         def load_words(a):
@@ -105,20 +106,21 @@ def tile_list_equity_factor_exposures_kernel(
         nc.sync.dma_start(
             w2_raw[:].bitcast(I32).rearrange("p (a b) -> p a b", a=2), w2_words.bitcast(I32).rearrange("a p b -> p a b")
         )
-        gather(picked_early[:, 0:HALF], scale_win, 2, 0, HALF)
-        gather(picked_early[:, HALF:S], scale_win, 3, 0, HALF)
-        spread(tab_planes[:, 0 : 2 * S], picked_early)
+        gather(picked[0][:, 0:HALF], scale_win, 2, 0, HALF)
+        gather(picked[0][:, HALF:S], scale_win, 3, 0, HALF)
+        spread(0)
         load_words(1)
         w1_rows = w1.rearrange("(a p j) c -> a p j c", a=2, j=4)
         for u in range(2):
             nc.sync.dma_start(
                 w1_first[u][:].rearrange("p (j c) -> p j c", j=4), w1_rows[0][:, :, H // 2 * u : H // 2 * (u + 1)]
             )
-        gather(picked_late[:, 0:HALF], scale_win, 2, HALF, S)
-        gather(picked_late[:, HALF:S], scale_win, 3, HALF, S)
-        gather(picked_late[:, S : 2 * S], scale_win, 1, 0, S)
+        gather(picked[1][:, 0:HALF], scale_win, 2, HALF, S)
+        gather(picked[1][:, HALF:S], scale_win, 3, HALF, S)
+        gather(picked[2][:], scale_win, 1, 0, S)
+        spread(1)
         nc.sync.dma_start(w1_second[:].rearrange("p (j c) -> p j c", j=4), w1_rows[1])
-        spread(tab_planes[:, 2 * S : 6 * S], picked_late)
+        spread(2)
         w4_rows = w4.rearrange("(g t i) n -> t g i n", t=4, i=8)
         for t in range(4):
             nc.sync.dma_start(w4_raw[:, N * t : N * (t + 1)], w4_rows[t])
@@ -130,11 +132,9 @@ def tile_list_equity_factor_exposures_kernel(
 
         def table_scale(j, a, lo, width):
             if j == 1:
-                col = 2 * S * (a + 1) + S + lo
-            elif lo < HALF:
-                col = S * a + HALF * (j - 2) + lo
+                col = 4 * S + S * a + lo
             else:
-                col = 2 * S * (a + 1) + HALF * (j - 2) + lo - HALF
+                col = 2 * S * (lo // HALF) + S * a + HALF * (j - 2) + lo % HALF
             return tab_planes[:, col : col + width]
 
         m_words = {}

@@ -57,7 +57,7 @@ def tile_list_equity_factor_exposures_kernel(
         w3_ord = sb("w3_ord", 2 * H, U32)
         picked = [sb("picked%d" % group, S, U8) for group in range(3)]
         w1_first = [sb("w1_first%d" % u, 2 * H, F32) for u in range(2)]
-        w1_second = sb("w1_second", 4 * H, F32)
+        w1_second = [sb("w1_second%d" % u, 2 * H, F32) for u in range(2)]
 
         nc.vector.memset(scale_win[0:ROWS_FROM, :].bitcast(I32), 0)
         nc.vector.memset(ws_planes[:].bitcast(I32), 0)
@@ -119,8 +119,12 @@ def tile_list_equity_factor_exposures_kernel(
         gather(picked[1][:, HALF:S], scale_win, 3, HALF, S)
         gather(picked[2][:], scale_win, 1, 0, S)
         spread(1)
-        nc.sync.dma_start(w1_second[:].rearrange("p (j c) -> p j c", j=4), w1_rows[1])
-        spread(2)
+        for u in range(2):
+            nc.sync.dma_start(
+                w1_second[u][:].rearrange("p (j c) -> p j c", j=4), w1_rows[1][:, :, H // 2 * u : H // 2 * (u + 1)]
+            )
+            if u == 0:
+                spread(2)
         w4_rows = w4.rearrange("(g t i) n -> t g i n", t=4, i=8)
         for t in range(4):
             nc.sync.dma_start(w4_raw[:, N * t : N * (t + 1)], w4_rows[t])
@@ -153,7 +157,7 @@ def tile_list_equity_factor_exposures_kernel(
 
         m_banks = [bank(b) for b in range(8)]
 
-        def m_pass(j, a, q, t):
+        def m_pass(j, a, q, t, last=(2, 1)):
             col = H * a + P * t
             if j == 2:
                 lhsT = w2_ord[:, 2 * col : 2 * (col + P)].bitcast(FP4X4)
@@ -167,7 +171,7 @@ def tile_list_equity_factor_exposures_kernel(
                 rhs=m_words[j, a, q].bitcast(FP8X4),
                 rhs_scale=table_scale(j, a, QUARTER * q, QUARTER),
                 start=(a == 0 and j == 3 and t % 2 == 0),
-                stop=(a == 1 and j == 2 and t % 2 == 1),
+                stop=((j, a) == last and t % 2 == 1),
             )
 
         for j in (3, 2):
@@ -182,42 +186,42 @@ def tile_list_equity_factor_exposures_kernel(
         def quantize(codes, scales, values):
             nc.vector.quantize_mx(out=codes.bitcast(FP8X4), scales=scales, in_=values)
 
-        def round_on_gpsimd(dst, src):
-            nc.gpsimd.tensor_scalar(dst, src, 1.0, 0.0, MULT, ADD)
-
-        def in_value_order(tile):
-            return tile.rearrange("p (t g e) -> p g t e", t=4, g=16)
-
-        def rows_side_by_side(raw):
-            return raw[:].rearrange("p (j c) -> p c j", j=4)
-
         w1_codes = sb("w1_codes", 2 * H, U32)
         w1_scale = sb("w1_scale", 2 * H, U8)
         rounded = sb("rounded", 8 * H, BF16)
-        dst = rounded[:, 0 : 4 * H].rearrange("p (t g u i j) -> p t g u j i", t=4, g=16, u=4, j=4)
-        src = w1_first[0][:].rearrange("p (j g t u i) -> p t g u j i", t=4, g=8, u=4, j=4)
-        for t in range(4):
-            nc.scalar.copy(dst[:, t, 0:8], src[:, t])
-        round_on_gpsimd(in_value_order(rounded[:, 0 : 4 * H])[:, 8:16], rows_side_by_side(w1_first[1]))
-        round_on_gpsimd(in_value_order(rounded[:, 4 * H : 8 * H]), rows_side_by_side(w1_second))
-        a_words = {(1, 0): sb("a_words10", HALF, U32)[:]}
-        held = sb("w1_first1", HALF + QUARTER, U32)
-        gather_m(held[:, HALF:], 2, 0, 3, 4)
-        for q in range(2, 4):
-            for a in range(2):
-                for j in (3, 2):
-                    for t in range(4):
-                        m_pass(j, a, q, t)
-        a_words[0, 0] = held[:, 0:HALF]
+
+        def round_in_pairs(copy, a, u, raw):
+            dst = rounded[:].rearrange("p (t a g u i j) -> p t a g u j i", t=4, a=2, g=16, u=4, j=4)
+            src = raw[:].rearrange("p (j g t u i) -> p t g u j i", t=4, g=8, u=4, j=4)
+            for t in range(4):
+                copy(dst[:, t, a, 8 * u : 8 * (u + 1)], src[:, t])
+
+        def round_on_gpsimd(a, u, raw):
+            dst = rounded[:].rearrange("p (t a g e) -> p a g t e", t=4, a=2, g=16)[:, a, 8 * u : 8 * (u + 1)]
+            nc.gpsimd.tensor_scalar(dst, raw[:].rearrange("p (j c) -> p c j", j=4), 1.0, 0.0, MULT, ADD)
+
+        round_in_pairs(nc.scalar.copy, 0, 0, w1_first[0])
+        round_on_gpsimd(0, 1, w1_first[1])
+        round_on_gpsimd(1, 0, w1_second[0])
+        a_words = {(1, 0): sb("a_words10", HALF, U32)[:], (0, 0): sb("w1_first1", HALF, U32)[:]}
         for a in (1, 0):
             gather(a_words[a, 0], word_win[a], 1, 0, HALF)
-        quantize(w1_codes[:], w1_scale[:], rounded[:])
-        held = sb("w1_second", S, U32)
+        gather_m(sb("w1_second0", QUARTER, U32)[:], 2, 0, 3, 4)
+        for q in range(2, 4):
+            for j, a in ((3, 0), (3, 1), (2, 1), (2, 0)):
+                for t in range(4):
+                    m_pass(j, a, q, t, last=(2, 0))
+        round_in_pairs(nc.vector.tensor_copy, 1, 1, w1_second[1])
+        for lo in (0, H):
+            quantize(w1_codes[:, lo : lo + H], w1_scale[:, lo : lo + H], rounded[:, 4 * lo : 4 * (lo + H)])
+        held = sb("w1_second1", S, U32)
         for a in range(2):
             a_words[a, 1] = held[:, HALF * a : HALF * (a + 1)]
             gather(a_words[a, 1], word_win[a], 1, HALF, S)
         w4_bf = sb("rounded", 4 * N, BF16)
-        round_on_gpsimd(w4_bf[:].rearrange("p (n t) -> p n t", t=4), w4_raw[:].rearrange("p (t n) -> p n t", t=4))
+        nc.gpsimd.tensor_scalar(
+            w4_bf[:].rearrange("p (n t) -> p n t", t=4), w4_raw[:].rearrange("p (t n) -> p n t", t=4), 1.0, 0.0, MULT, ADD
+        )
 
         m_abs = [sb("w1_first0", 2 * S, F32), sb("m_abs1", 2 * S, F32)]
         root = [sb("root%d" % half, 2 * S, F32) for half in range(2)]
@@ -259,7 +263,7 @@ def tile_list_equity_factor_exposures_kernel(
             a_banks.append(acc)
             for a in range(2):
                 for t in range(4):
-                    col = H * a + P * t
+                    col = 2 * P * t + P * a
                     nc.tensor.matmul_mx(
                         out=acc[:, CHUNK * t : CHUNK * (t + 1)],
                         lhsT=w1_codes[:, col : col + P].bitcast(FP8X4),

@@ -57,7 +57,8 @@ def tile_list_equity_factor_exposures_kernel(
         w3_ord = sb("w3_ord", 2 * H, U32)
         picked = [sb("picked%d" % group, S, U8) for group in range(3)]
         w1_first = [sb("w1_first%d" % u, 2 * H, F32) for u in range(2)]
-        w1_second = [sb("w1_second%d" % u, 2 * H, F32) for u in range(2)]
+        second_blocks = ((0, 8), (8, 16))
+        w1_second = [sb("w1_second%d" % u, 4 * 32 * (hi - lo), F32) for u, (lo, hi) in enumerate(second_blocks)]
 
         nc.vector.memset(scale_win[0:ROWS_FROM, :].bitcast(I32), 0)
         nc.vector.memset(ws_planes[:].bitcast(I32), 0)
@@ -119,12 +120,9 @@ def tile_list_equity_factor_exposures_kernel(
         gather(picked[1][:, HALF:S], scale_win, 3, HALF, S)
         gather(picked[2][:], scale_win, 1, 0, S)
         spread(1)
-        for u in range(2):
-            nc.sync.dma_start(
-                w1_second[u][:].rearrange("p (j c) -> p j c", j=4), w1_rows[1][:, :, H // 2 * u : H // 2 * (u + 1)]
-            )
-            if u == 0:
-                spread(2)
+        for u, (lo, hi) in enumerate(second_blocks):
+            nc.sync.dma_start(w1_second[u][:].rearrange("p (j c) -> p j c", j=4), w1_rows[1][:, :, 32 * lo : 32 * hi])
+        spread(2)
         w4_rows = w4.rearrange("(g t i) n -> t g i n", t=4, i=8)
         for t in range(4):
             nc.sync.dma_start(w4_raw[:, N * t : N * (t + 1)], w4_rows[t])
@@ -190,39 +188,37 @@ def tile_list_equity_factor_exposures_kernel(
         w1_scale = sb("w1_scale", 2 * H, U8)
         rounded = sb("rounded", 8 * H, BF16)
 
-        def round_in_pairs(copy, a, u, raw):
+        def round_in_pairs(a, lo, hi, raw):
             dst = rounded[:].rearrange("p (t a g u i j) -> p t a g u j i", t=4, a=2, g=16, u=4, j=4)
-            src = raw[:].rearrange("p (j g t u i) -> p t g u j i", t=4, g=8, u=4, j=4)
+            src = raw[:].rearrange("p (j g t u i) -> p t g u j i", t=4, g=hi - lo, u=4, j=4)
             for t in range(4):
-                copy(dst[:, t, a, 8 * u : 8 * (u + 1)], src[:, t])
+                nc.scalar.copy(dst[:, t, a, lo:hi], src[:, t])
 
-        def round_on_gpsimd(a, u, raw):
-            dst = rounded[:].rearrange("p (t a g e) -> p a g t e", t=4, a=2, g=16)[:, a, 8 * u : 8 * (u + 1)]
-            nc.gpsimd.tensor_scalar(dst, raw[:].rearrange("p (j c) -> p c j", j=4), 1.0, 0.0, MULT, ADD)
+        def in_turn(a, lo, hi, raw):
+            dst = rounded[:].rearrange("p (t a g e) -> p a g t e", t=4, a=2, g=16)[:, a, lo:hi]
+            return dst, raw[:].rearrange("p (j c) -> p c j", j=4)
 
-        round_in_pairs(nc.scalar.copy, 0, 0, w1_first[0])
-        round_on_gpsimd(0, 1, w1_first[1])
-        round_on_gpsimd(1, 0, w1_second[0])
-        a_words = {(1, 0): sb("a_words10", HALF, U32)[:], (0, 0): sb("w1_first1", HALF, U32)[:]}
-        for a in (1, 0):
-            gather(a_words[a, 0], word_win[a], 1, 0, HALF)
-        gather_m(sb("w1_second0", QUARTER, U32)[:], 2, 0, 3, 4)
+        round_in_pairs(0, 0, 8, w1_first[0])
+        dst, src = in_turn(0, 8, 16, w1_first[1])
+        nc.scalar.copy(dst[:, 0:2], src[:, 0 : 32 * 2])
+        nc.gpsimd.tensor_scalar(dst[:, 2:8], src[:, 32 * 2 :], 1.0, 0.0, MULT, ADD)
+        nc.gpsimd.tensor_scalar(*in_turn(1, 0, 8, w1_second[0]), 1.0, 0.0, MULT, ADD)
+        nc.gpsimd.tensor_scalar(*in_turn(1, 8, 16, w1_second[1]), 1.0, 0.0, MULT, ADD)
+        a_words = {}
+
+        def gather_a(dst, a, first, end):
+            gather(dst, word_win[a], 1, QUARTER * first, QUARTER * end)
+            for q in range(first, end):
+                a_words[a, q] = dst[:, QUARTER * (q - first) : QUARTER * (q - first + 1)]
+
+        gather_a(sb("a_words10", HALF, U32)[:], 1, 0, 2)
+        held = sb("w1_first1", S, U32)
+        gather_m(held[:, 3 * QUARTER :], 2, 0, 3, 4)
+        gather_a(held[:, 0 : 3 * QUARTER], 0, 0, 3)
         for q in range(2, 4):
             for j, a in ((3, 0), (3, 1), (2, 1), (2, 0)):
                 for t in range(4):
                     m_pass(j, a, q, t, last=(2, 0))
-        round_in_pairs(nc.vector.tensor_copy, 1, 1, w1_second[1])
-        for lo in (0, H):
-            quantize(w1_codes[:, lo : lo + H], w1_scale[:, lo : lo + H], rounded[:, 4 * lo : 4 * (lo + H)])
-        held = sb("w1_second1", S, U32)
-        for a in range(2):
-            a_words[a, 1] = held[:, HALF * a : HALF * (a + 1)]
-            gather(a_words[a, 1], word_win[a], 1, HALF, S)
-        w4_bf = sb("rounded", 4 * N, BF16)
-        nc.gpsimd.tensor_scalar(
-            w4_bf[:].rearrange("p (n t) -> p n t", t=4), w4_raw[:].rearrange("p (t n) -> p n t", t=4), 1.0, 0.0, MULT, ADD
-        )
-
         m_abs = [sb("w1_first0", 2 * S, F32), sb("m_abs1", 2 * S, F32)]
         root = [sb("root%d" % half, 2 * S, F32) for half in range(2)]
         damp = [sb("damp%d" % half, 2 * S, F32) for half in range(2)]
@@ -253,9 +249,19 @@ def tile_list_equity_factor_exposures_kernel(
                     magnitude(i + 2)
                 square(i)
 
+        for lo in (0, H):
+            quantize(w1_codes[:, lo : lo + H], w1_scale[:, lo : lo + H], rounded[:, 4 * lo : 4 * (lo + H)])
+        held = sb("w1_second1", 3 * QUARTER, U32)
+        gather_a(held[:, 0:HALF], 1, 2, 4)
+        gather_a(held[:, HALF:], 0, 3, 4)
+        w4_bf = sb("rounded", 4 * N, BF16)
+        nc.gpsimd.tensor_scalar(
+            w4_bf[:].rearrange("p (n t) -> p n t", t=4), w4_raw[:].rearrange("p (t n) -> p n t", t=4), 1.0, 0.0, MULT, ADD
+        )
+
         def a_rhs(a, c):
-            lo = CHUNK * (c % HALF_CHUNKS)
-            return a_words[a, c // HALF_CHUNKS][:, lo : lo + CHUNK]
+            lo = CHUNK * (c % 2)
+            return a_words[a, c // 2][:, lo : lo + CHUNK]
 
         a_banks = []
         for c in range(CHUNKS):

@@ -119,9 +119,10 @@ def tile_list_equity_factor_exposures_kernel(
         gather(picked[1][:, 0:HALF], scale_win, 2, HALF, S)
         gather(picked[1][:, HALF:S], scale_win, 3, HALF, S)
         gather(picked[2][:], scale_win, 1, 0, S)
-        spread(1)
         for u, (lo, hi) in enumerate(second_blocks):
             nc.sync.dma_start(w1_second[u][:].rearrange("p (j c) -> p j c", j=4), w1_rows[1][:, :, 32 * lo : 32 * hi])
+            if u == 0:
+                spread(1)
         spread(2)
         w4_rows = w4.rearrange("(g t i) n -> t g i n", t=4, i=8)
         for t in range(4):
@@ -200,8 +201,8 @@ def tile_list_equity_factor_exposures_kernel(
 
         round_in_pairs(0, 0, 8, w1_first[0])
         dst, src = in_turn(0, 8, 16, w1_first[1])
-        nc.scalar.copy(dst[:, 0:2], src[:, 0 : 32 * 2])
-        nc.gpsimd.tensor_scalar(dst[:, 2:8], src[:, 32 * 2 :], 1.0, 0.0, MULT, ADD)
+        nc.scalar.copy(dst[:, 0:3], src[:, 0 : 32 * 3])
+        nc.gpsimd.tensor_scalar(dst[:, 3:8], src[:, 32 * 3 :], 1.0, 0.0, MULT, ADD)
         nc.gpsimd.tensor_scalar(*in_turn(1, 0, 8, w1_second[0]), 1.0, 0.0, MULT, ADD)
         nc.gpsimd.tensor_scalar(*in_turn(1, 8, 16, w1_second[1]), 1.0, 0.0, MULT, ADD)
         a_words = {}
@@ -216,9 +217,10 @@ def tile_list_equity_factor_exposures_kernel(
         gather_m(held[:, 3 * QUARTER :], 2, 0, 3, 4)
         gather_a(held[:, 0 : 3 * QUARTER], 0, 0, 3)
         for q in range(2, 4):
-            for j, a in ((3, 0), (3, 1), (2, 1), (2, 0)):
-                for t in range(4):
-                    m_pass(j, a, q, t, last=(2, 0))
+            for pair in range(2):
+                for j, a in ((3, 0), (3, 1), (2, 1), (2, 0)):
+                    for t in (2 * pair, 2 * pair + 1):
+                        m_pass(j, a, q, t, last=(2, 0))
         m_abs = [sb("w1_first0", 2 * S, F32), sb("m_abs1", 2 * S, F32)]
         root = [sb("root%d" % half, 2 * S, F32) for half in range(2)]
         damp = [sb("damp%d" % half, 2 * S, F32) for half in range(2)]
@@ -244,6 +246,11 @@ def tile_list_equity_factor_exposures_kernel(
         for q in range(4):
             for i in (2 * q, 2 * q + 1):
                 inverse_root(of_chunk if q else of_bank, i)
+            if q == 0:
+                magnitude(2)
+                magnitude(3)
+                square(0)
+                continue
             for i in (2 * q, 2 * q + 1):
                 if q < 3:
                     magnitude(i + 2)
@@ -254,9 +261,12 @@ def tile_list_equity_factor_exposures_kernel(
         held = sb("w1_second1", 3 * QUARTER, U32)
         gather_a(held[:, 0:HALF], 1, 2, 4)
         gather_a(held[:, HALF:], 0, 3, 4)
-        w4_bf = sb("rounded", 4 * N, BF16)
+        behind = sb("rounded", S, F32)
+        damp_second = behind[:, 0:HALF].rearrange("p (t n) -> p t n", t=4)
+        nc.gpsimd.tensor_tensor(damp_second, of_chunk(root, 1), of_chunk(root, 1), MULT)
+        w4_bf = behind[:, HALF:S].bitcast(BF16)
         nc.gpsimd.tensor_scalar(
-            w4_bf[:].rearrange("p (n t) -> p n t", t=4), w4_raw[:].rearrange("p (t n) -> p n t", t=4), 1.0, 0.0, MULT, ADD
+            w4_bf.rearrange("p (n t) -> p n t", t=4), w4_raw[:].rearrange("p (t n) -> p n t", t=4), 1.0, 0.0, MULT, ADD
         )
 
         def a_rhs(a, c):
@@ -289,7 +299,7 @@ def tile_list_equity_factor_exposures_kernel(
             nc.vector.tensor_tensor(
                 h_bf[:, 4 * CHUNK * c : 4 * CHUNK * (c + 1)].rearrange("p (q i t) -> p q t i", t=4, i=2),
                 a_banks[c][:].rearrange("p (t q i) -> p q t i", t=4, i=2),
-                of_chunk(damp, c).rearrange("p t (q i) -> p q t i", i=2),
+                (damp_second if c == 1 else of_chunk(damp, c)).rearrange("p t (q i) -> p q t i", i=2),
                 MULT,
             )
 
@@ -328,7 +338,7 @@ def tile_list_equity_factor_exposures_kernel(
         for c in range(HALF_CHUNKS):
             damped(c)
         late_scale = sb("damp0", S + N, U8)
-        quantize(w4_codes[:], late_scale[:, S : S + N], w4_bf[:])
+        quantize(w4_codes[:], late_scale[:, S : S + N], w4_bf)
         done = 0
         for c in range(HALF_CHUNKS, CHUNKS + 1):
             if c < CHUNKS:

@@ -201,8 +201,8 @@ def tile_list_equity_factor_exposures_kernel(
 
         round_in_pairs(0, 0, 8, w1_first[0])
         dst, src = in_turn(0, 8, 16, w1_first[1])
-        nc.scalar.copy(dst[:, 0:3], src[:, 0 : 32 * 3])
-        nc.gpsimd.tensor_scalar(dst[:, 3:8], src[:, 32 * 3 :], 1.0, 0.0, MULT, ADD)
+        nc.scalar.copy(dst[:, 0:2], src[:, 0 : 32 * 2])
+        nc.gpsimd.tensor_scalar(dst[:, 2:8], src[:, 32 * 2 :], 1.0, 0.0, MULT, ADD)
         nc.gpsimd.tensor_scalar(*in_turn(1, 0, 8, w1_second[0]), 1.0, 0.0, MULT, ADD)
         nc.gpsimd.tensor_scalar(*in_turn(1, 8, 16, w1_second[1]), 1.0, 0.0, MULT, ADD)
         a_words = {}
@@ -277,8 +277,8 @@ def tile_list_equity_factor_exposures_kernel(
         for c in range(CHUNKS):
             acc = bank(c)
             a_banks.append(acc)
-            for a in range(2):
-                for t in range(4):
+            for t in range(4):
+                for a in range(2):
                     col = 2 * P * t + P * a
                     nc.tensor.matmul_mx(
                         out=acc[:, CHUNK * t : CHUNK * (t + 1)],
@@ -334,17 +334,22 @@ def tile_list_equity_factor_exposures_kernel(
                 nc.sync.dma_start(out_rows[:, :, lo:hi], result.rearrange("p (f j) -> p f j", f=2))
 
         results = sb("m_abs1", 2 * S, F32)
-        groups = [(0, 2, (0, 0)), (2, 4, (1, 1)), (4, 6, (2, 2)), (6, 7, (3, 3)), (7, 8, (4, 5))]
         for c in range(HALF_CHUNKS):
             damped(c)
         late_scale = sb("damp0", S + N, U8)
         quantize(w4_codes[:], late_scale[:, S : S + N], w4_bf)
-        done = 0
-        for c in range(HALF_CHUNKS, CHUNKS + 1):
-            if c < CHUNKS:
-                damped(c)
-            while done < len(groups) and groups[done][1] <= c:
-                lo, hi = CHUNK * groups[done][0], CHUNK * groups[done][1]
-                quantize(h_codes[:, lo:hi], late_scale[:, lo:hi], h_bf[:, 4 * lo : 4 * hi])
-                exposures(lo, hi, groups[done][2], late_scale)
-                done += 1
+
+        def finish(first, end, banks):
+            lo, hi = CHUNK * first, CHUNK * end
+            quantize(h_codes[:, lo:hi], late_scale[:, lo:hi], h_bf[:, 4 * lo : 4 * hi])
+            exposures(lo, hi, banks, late_scale)
+
+        finish(0, 2, (0, 0))
+        damped(4)
+        damped(5)
+        finish(2, 4, (1, 1))
+        finish(4, 6, (2, 2))
+        damped(6)
+        damped(7)
+        finish(6, 7, (3, 3))
+        finish(7, 8, (4, 5))

@@ -148,7 +148,7 @@ def tile_list_equity_factor_exposures_kernel(
                 m_words[j, a, q] = dst[:, QUARTER * (q - first) : QUARTER * (q - first + 1)]
 
         for j, a, first, end in (
-            (3, 0, 0, 2), (2, 0, 0, 2), (3, 0, 2, 4), (2, 0, 2, 3),
+            (3, 0, 0, 2), (2, 0, 0, 3), (3, 0, 2, 4),
             (3, 1, 0, 1), (2, 1, 0, 1), (3, 1, 1, 2), (2, 1, 1, 2), (3, 1, 2, 4), (2, 1, 2, 4),
         ):
             words = sb("m_words%d%d%d" % (j, a, first), QUARTER * (end - first), U32)
@@ -201,8 +201,8 @@ def tile_list_equity_factor_exposures_kernel(
 
         round_in_pairs(0, 0, 8, w1_first[0])
         dst, src = in_turn(0, 8, 16, w1_first[1])
-        nc.scalar.copy(dst[:, 0:2], src[:, 0 : 32 * 2])
-        nc.gpsimd.tensor_scalar(dst[:, 2:8], src[:, 32 * 2 :], 1.0, 0.0, MULT, ADD)
+        nc.scalar.copy(dst[:, 0:3], src[:, 0 : 32 * 3])
+        nc.gpsimd.tensor_scalar(dst[:, 3:8], src[:, 32 * 3 :], 1.0, 0.0, MULT, ADD)
         nc.gpsimd.tensor_scalar(*in_turn(1, 0, 8, w1_second[0]), 1.0, 0.0, MULT, ADD)
         nc.gpsimd.tensor_scalar(*in_turn(1, 8, 16, w1_second[1]), 1.0, 0.0, MULT, ADD)
         a_words = {}
@@ -223,7 +223,7 @@ def tile_list_equity_factor_exposures_kernel(
                         m_pass(j, a, q, t, last=(2, 0))
         m_abs = [sb("w1_first0", 2 * S, F32), sb("m_abs1", 2 * S, F32)]
         root = [sb("root%d" % half, 2 * S, F32) for half in range(2)]
-        damp = [sb("damp%d" % half, 2 * S, F32) for half in range(2)]
+        damp = {}
 
         def of_bank(tiles, b):
             return tiles[b // 4][:, HALF * (b % 4) : HALF * (b % 4 + 1)]
@@ -239,7 +239,8 @@ def tile_list_equity_factor_exposures_kernel(
             nc.scalar.activation(out=part(root, i), in_=part(m_abs, i), func=ACT.Abs_reciprocal_sqrt, bias=1.0)
 
         def square(c):
-            nc.scalar.activation(out=of_chunk(damp, c), in_=of_chunk(root, c), func=ACT.Square)
+            damp[c] = sb("damp%d" % c, HALF, F32)[:].rearrange("p (t n) -> p t n", t=4)
+            nc.scalar.activation(out=damp[c], in_=of_chunk(root, c), func=ACT.Square)
 
         for b in range(2):
             magnitude(b)
@@ -262,8 +263,8 @@ def tile_list_equity_factor_exposures_kernel(
         gather_a(held[:, 0:HALF], 1, 2, 4)
         gather_a(held[:, HALF:], 0, 3, 4)
         behind = sb("rounded", S, F32)
-        damp_second = behind[:, 0:HALF].rearrange("p (t n) -> p t n", t=4)
-        nc.gpsimd.tensor_tensor(damp_second, of_chunk(root, 1), of_chunk(root, 1), MULT)
+        damp[1] = behind[:, 0:HALF].rearrange("p (t n) -> p t n", t=4)
+        nc.gpsimd.tensor_tensor(damp[1], of_chunk(root, 1), of_chunk(root, 1), MULT)
         w4_bf = behind[:, HALF:S].bitcast(BF16)
         nc.gpsimd.tensor_scalar(
             w4_bf.rearrange("p (n t) -> p n t", t=4), w4_raw[:].rearrange("p (t n) -> p n t", t=4), 1.0, 0.0, MULT, ADD
@@ -299,7 +300,7 @@ def tile_list_equity_factor_exposures_kernel(
             nc.vector.tensor_tensor(
                 h_bf[:, 4 * CHUNK * c : 4 * CHUNK * (c + 1)].rearrange("p (q i t) -> p q t i", t=4, i=2),
                 a_banks[c][:].rearrange("p (t q i) -> p q t i", t=4, i=2),
-                (damp_second if c == 1 else of_chunk(damp, c)).rearrange("p t (q i) -> p q t i", i=2),
+                damp[c].rearrange("p t (q i) -> p q t i", i=2),
                 MULT,
             )
 
@@ -334,9 +335,9 @@ def tile_list_equity_factor_exposures_kernel(
                 nc.sync.dma_start(out_rows[:, :, lo:hi], result.rearrange("p (f j) -> p f j", f=2))
 
         results = sb("m_abs1", 2 * S, F32)
-        for c in range(HALF_CHUNKS):
+        for c in range(HALF_CHUNKS + 1):
             damped(c)
-        late_scale = sb("damp0", S + N, U8)
+        late_scale = sb("damp4", S + N, U8)
         quantize(w4_codes[:], late_scale[:, S : S + N], w4_bf)
 
         def finish(first, end, banks):
@@ -345,7 +346,6 @@ def tile_list_equity_factor_exposures_kernel(
             exposures(lo, hi, banks, late_scale)
 
         finish(0, 2, (0, 0))
-        damped(4)
         damped(5)
         finish(2, 4, (1, 1))
         finish(4, 6, (2, 2))

from contextlib import ExitStack

import concourse.mybir as mybir

T, S, K, H, N = 4096, 1024, 1024, 512, 256
FLOPS = 2 * S * (3 * K * H + H * N)

F32 = mybir.dt.float32
BF16 = mybir.dt.bfloat16
I32 = mybir.dt.int32
U32 = mybir.dt.uint32
U16 = mybir.dt.uint16
U8 = mybir.dt.uint8
FP8X4 = mybir.dt.float8_e4m3fn_x4
FP4X4 = mybir.dt.float4_e2m1fn_x4
ACT = mybir.ActivationFunctionType
MULT = mybir.AluOpType.mult
ADD = mybir.AluOpType.add

P = 128
HALF = S // 2
QUARTER = S // 4
CHUNK = 128
CHUNKS = S // CHUNK
HALF_CHUNKS = CHUNKS // 2
ROWS_FROM = 96


def tile_list_equity_factor_exposures_kernel(
    tc, tab_words, tab_scales, offs, offs2, offs3, w1, w2_words, w2_scales, w3_words, w3_scales, w4, fscale, fbase, out
):
    nc = tc.nc
    with ExitStack() as ctx:
        keep = ctx.enter_context(tc.tile_pool(name="keep", bufs=1))
        psum = ctx.enter_context(tc.psum_pool(name="psum", bufs=1))

        def sb(name, cols, dtype):
            return keep.tile([P, cols], dtype, name=name, align_bytes=64)

        def bank(b):
            return psum.tile([P, HALF], F32, name="bank%d" % b)

        lists = {j: keep.tile([P, S // 16], U16, name="list%d" % j) for j in (1, 2, 3)}
        scale_win = sb("scale_win", T, U8)
        word_win = [sb("word_win%d" % a, T, U32) for a in range(2)]
        ws_raw = sb("ws_raw", 4 * H, U8)
        ws_ord = sb("ws_ord", 4 * H, U8)
        ws_planes = sb("ws_planes", 4 * H, U8)
        tab_planes = sb("tab_planes", 6 * S, U8)
        warm = sb("warm", 16, F32)
        fs = sb("fs", 2, F32)
        fb = sb("fb", 2, F32)
        w2_raw = sb("w2_raw", 4 * H, U8)
        w3_raw = sb("w3_raw", 2 * H, U32)
        w4_raw = sb("w4_raw", 4 * N, F32)
        w2_ord = sb("w2_ord", 4 * H, U8)
        w3_ord = sb("w3_ord", 2 * H, U32)
        picked = [sb("picked%d" % group, S, U8) for group in range(3)]
        w1_first = [sb("w1_first%d" % u, 2 * H, F32) for u in range(2)]
        second_blocks = ((0, 8), (8, 16))
        w1_second = [sb("w1_second%d" % u, 4 * 32 * (hi - lo), F32) for u, (lo, hi) in enumerate(second_blocks)]

        nc.vector.memset(scale_win[0:ROWS_FROM, :].bitcast(I32), 0)
        nc.vector.memset(ws_planes[:].bitcast(I32), 0)
        nc.gpsimd.memset(warm[:, 0:8], 1.0)
        nc.gpsimd.memset(tab_planes[:].bitcast(I32), 0)

        def gather(dst, window, j, lo, hi):
            nc.vector.tensor_copy(dst, window[:].indirect(lists[j][:, lo // 16 : hi // 16]))

        def reorder(dst, src, parts):
            nc.scalar.copy(
                dst.bitcast(U32).rearrange("p (a t g e) -> p a t g e", a=parts, t=4, g=16),
                src.bitcast(U32).rearrange("p (a g t e) -> p a t g e", a=parts, t=4, g=16),
            )

        def spread(group):
            for q in (0, 2, 1, 3):
                nc.sync.dma_start(
                    tab_planes[32 * q : 32 * q + 4, 2 * S * group : 2 * S * (group + 1)]
                    .bitcast(I32)
                    .rearrange("r (a n) -> r a n", a=2),
                    picked[group][ROWS_FROM + 8 * q : ROWS_FROM + 8 * q + 8, :].bitcast(I32),
                )

        def load_words(a):
            nc.sync.dma_start(word_win[a][:].bitcast(I32), tab_words[a].rearrange("p t i -> p (t i)").bitcast(I32))

        nc.sync.dma_start(scale_win[ROWS_FROM:P, :].bitcast(I32), tab_scales.bitcast(I32).rearrange("a q t -> q a t"))
        nc.sync.dma_start(lists[2][:], offs2)
        nc.sync.dma_start(lists[3][:], offs3)
        nc.sync.dma_start(lists[1][:], offs)
        for j, src in ((2, w2_scales), (3, w3_scales)):
            nc.scalar.dma_start(
                ws_raw[0:16, 2 * H * (j - 2) : 2 * H * (j - 1)].bitcast(I32).rearrange("q (a c) -> q a c", a=2),
                src.bitcast(I32).rearrange("a q c -> q a c"),
            )
        nc.scalar.activation(out=warm[:, 8:9], in_=warm[:, 0:1], func=ACT.Abs_reciprocal_sqrt)
        load_words(0)
        reorder(ws_ord[0:16, :], ws_raw[0:16, :], 4)
        for r in range(4):
            nc.sync.dma_start(ws_planes[r:P:32, :].bitcast(I32), ws_ord[r:16:4, :].bitcast(I32))
        nc.sync.dma_start(
            w3_raw[:].bitcast(I32).rearrange("p (a c) -> p a c", a=2),
            w3_words.rearrange("a p c i -> a p (c i)").bitcast(I32).rearrange("a p c -> p a c"),
        )
        nc.sync.dma_start(
            w2_raw[:].bitcast(I32).rearrange("p (a b) -> p a b", a=2), w2_words.bitcast(I32).rearrange("a p b -> p a b")
        )
        gather(picked[0][:, 0:HALF], scale_win, 2, 0, HALF)
        gather(picked[0][:, HALF:S], scale_win, 3, 0, HALF)
        spread(0)
        load_words(1)
        w1_rows = w1.rearrange("(a p j) c -> a p j c", a=2, j=4)
        for u in range(2):
            nc.sync.dma_start(
                w1_first[u][:].rearrange("p (j c) -> p j c", j=4), w1_rows[0][:, :, H // 2 * u : H // 2 * (u + 1)]
            )
        gather(picked[1][:, 0:HALF], scale_win, 2, HALF, S)
        gather(picked[1][:, HALF:S], scale_win, 3, HALF, S)
        gather(picked[2][:], scale_win, 1, 0, S)
        for u, (lo, hi) in enumerate(second_blocks):
            nc.sync.dma_start(w1_second[u][:].rearrange("p (j c) -> p j c", j=4), w1_rows[1][:, :, 32 * lo : 32 * hi])
            if u == 0:
                spread(1)
        spread(2)
        w4_rows = w4.rearrange("(g t i) n -> t g i n", t=4, i=8)
        for t in range(4):
            nc.sync.dma_start(w4_raw[:, N * t : N * (t + 1)], w4_rows[t])
        with nc.allow_non_contiguous_dma(reason="factor 128 f + p has its scale and base level at [p, f]"):
            nc.sync.dma_start(fs[:], fscale.rearrange("(f p) -> p f", f=2))
            nc.sync.dma_start(fb[:], fbase.rearrange("(f p) -> p f", f=2))
        reorder(w3_ord[:], w3_raw[:], 2)
        reorder(w2_ord[:], w2_raw[:], 2)

        def table_scale(j, a, lo, width):
            if j == 1:
                col = 4 * S + S * a + lo
            else:
                col = 2 * S * (lo // HALF) + S * a + HALF * (j - 2) + lo % HALF
            return tab_planes[:, col : col + width]

        m_words = {}

        def gather_m(dst, j, a, first, end):
            gather(dst, word_win[a], j, QUARTER * first, QUARTER * end)
            for q in range(first, end):
                m_words[j, a, q] = dst[:, QUARTER * (q - first) : QUARTER * (q - first + 1)]

        for j, a, first, end in (
            (3, 0, 0, 2), (2, 0, 0, 3), (3, 0, 2, 4),
            (3, 1, 0, 1), (2, 1, 0, 1), (3, 1, 1, 2), (2, 1, 1, 2), (3, 1, 2, 4), (2, 1, 2, 4),
        ):
            words = sb("m_words%d%d%d" % (j, a, first), QUARTER * (end - first), U32)
            gather_m(words[:], j, a, first, end)

        m_banks = [bank(b) for b in range(8)]

        def m_pass(j, a, q, t, last=(2, 1)):
            col = H * a + P * t
            if j == 2:
                lhsT = w2_ord[:, 2 * col : 2 * (col + P)].bitcast(FP4X4)
            else:
                lhsT = w3_ord[:, col : col + P].bitcast(FP8X4)
            scol = 2 * H * (j - 2) + col
            nc.tensor.matmul_mx(
                out=m_banks[2 * q + t // 2][:, QUARTER * (t % 2) : QUARTER * (t % 2 + 1)],
                lhsT=lhsT,
                lhsT_scale=ws_planes[:, scol : scol + P],
                rhs=m_words[j, a, q].bitcast(FP8X4),
                rhs_scale=table_scale(j, a, QUARTER * q, QUARTER),
                start=(a == 0 and j == 3 and t % 2 == 0),
                stop=((j, a) == last and t % 2 == 1),
            )

        for j in (3, 2):
            for q in range(2):
                for t in range(4):
                    m_pass(j, 0, q, t)
        for q in range(2):
            for j in (3, 2):
                for t in range(4):
                    m_pass(j, 1, q, t)

        def quantize(codes, scales, values):
            nc.vector.quantize_mx(out=codes.bitcast(FP8X4), scales=scales, in_=values)

        w1_codes = sb("w1_codes", 2 * H, U32)
        w1_scale = sb("w1_scale", 2 * H, U8)
        rounded = sb("rounded", 8 * H, BF16)

        def round_in_pairs(a, lo, hi, raw):
            dst = rounded[:].rearrange("p (t a g u i j) -> p t a g u j i", t=4, a=2, g=16, u=4, j=4)
            src = raw[:].rearrange("p (j g t u i) -> p t g u j i", t=4, g=hi - lo, u=4, j=4)
            for t in range(4):
                nc.scalar.copy(dst[:, t, a, lo:hi], src[:, t])

        def in_turn(a, lo, hi, raw):
            dst = rounded[:].rearrange("p (t a g e) -> p a g t e", t=4, a=2, g=16)[:, a, lo:hi]
            return dst, raw[:].rearrange("p (j c) -> p c j", j=4)

        round_in_pairs(0, 0, 8, w1_first[0])
        dst, src = in_turn(0, 8, 16, w1_first[1])
        nc.scalar.copy(dst[:, 0:3], src[:, 0 : 32 * 3])
        nc.gpsimd.tensor_scalar(dst[:, 3:8], src[:, 32 * 3 :], 1.0, 0.0, MULT, ADD)
        nc.gpsimd.tensor_scalar(*in_turn(1, 0, 8, w1_second[0]), 1.0, 0.0, MULT, ADD)
        nc.gpsimd.tensor_scalar(*in_turn(1, 8, 16, w1_second[1]), 1.0, 0.0, MULT, ADD)
        a_words = {}

        def gather_a(dst, a, first, end):
            gather(dst, word_win[a], 1, QUARTER * first, QUARTER * end)
            for q in range(first, end):
                a_words[a, q] = dst[:, QUARTER * (q - first) : QUARTER * (q - first + 1)]

        gather_a(sb("a_words10", HALF, U32)[:], 1, 0, 2)
        held = sb("w1_first1", S, U32)
        gather_m(held[:, 3 * QUARTER :], 2, 0, 3, 4)
        gather_a(held[:, 0 : 3 * QUARTER], 0, 0, 3)
        for q in range(2, 4):
            for pair in range(2):
                for j, a in ((3, 0), (3, 1), (2, 1), (2, 0)):
                    for t in (2 * pair, 2 * pair + 1):
                        m_pass(j, a, q, t, last=(2, 0))
        m_abs = [sb("w1_first0", 2 * S, F32), sb("m_abs1", 2 * S, F32)]
        root = [sb("root%d" % half, 2 * S, F32) for half in range(2)]
        damp = {}

        def of_bank(tiles, b):
            return tiles[b // 4][:, HALF * (b % 4) : HALF * (b % 4 + 1)]

        def of_chunk(tiles, c):
            view = tiles[c // HALF_CHUNKS][:].rearrange("p (q t n) -> p q t n", q=2, t=4)
            return view[:, c // 2 % 2, :, CHUNK * (c % 2) : CHUNK * (c % 2 + 1)]

        def magnitude(b):
            nc.scalar.activation(out=of_bank(m_abs, b), in_=m_banks[b][:], func=ACT.Abs)

        def inverse_root(part, i):
            nc.scalar.activation(out=part(root, i), in_=part(m_abs, i), func=ACT.Abs_reciprocal_sqrt, bias=1.0)

        def square(c):
            damp[c] = sb("damp%d" % c, HALF, F32)[:].rearrange("p (t n) -> p t n", t=4)
            nc.scalar.activation(out=damp[c], in_=of_chunk(root, c), func=ACT.Square)

        for b in range(2):
            magnitude(b)
        for q in range(4):
            for i in (2 * q, 2 * q + 1):
                inverse_root(of_chunk if q else of_bank, i)
            if q == 0:
                magnitude(2)
                magnitude(3)
                square(0)
                continue
            for i in (2 * q, 2 * q + 1):
                if q < 3:
                    magnitude(i + 2)
                square(i)

        for lo in (0, H):
            quantize(w1_codes[:, lo : lo + H], w1_scale[:, lo : lo + H], rounded[:, 4 * lo : 4 * (lo + H)])
        held = sb("w1_second1", 3 * QUARTER, U32)
        gather_a(held[:, 0:HALF], 1, 2, 4)
        gather_a(held[:, HALF:], 0, 3, 4)
        behind = sb("rounded", S, F32)
        damp[1] = behind[:, 0:HALF].rearrange("p (t n) -> p t n", t=4)
        nc.gpsimd.tensor_tensor(damp[1], of_chunk(root, 1), of_chunk(root, 1), MULT)
        w4_bf = behind[:, HALF:S].bitcast(BF16)
        nc.gpsimd.tensor_scalar(
            w4_bf.rearrange("p (n t) -> p n t", t=4), w4_raw[:].rearrange("p (t n) -> p n t", t=4), 1.0, 0.0, MULT, ADD
        )

        def a_rhs(a, c):
            lo = CHUNK * (c % 2)
            return a_words[a, c // 2][:, lo : lo + CHUNK]

        a_banks = []
        for c in range(CHUNKS):
            acc = bank(c)
            a_banks.append(acc)
            for t in range(4):
                for a in range(2):
                    col = 2 * P * t + P * a
                    nc.tensor.matmul_mx(
                        out=acc[:, CHUNK * t : CHUNK * (t + 1)],
                        lhsT=w1_codes[:, col : col + P].bitcast(FP8X4),
                        lhsT_scale=w1_scale[:, col : col + P],
                        rhs=a_rhs(a, c).bitcast(FP8X4),
                        rhs_scale=table_scale(1, a, CHUNK * c, CHUNK),
                        start=(a == 0 and t == 0),
                        stop=(a == 1 and t == 3),
                    )

        h_bf = sb("h_bf", 4 * S, BF16)
        h_codes = sb("h_codes", S, U32)
        w4_codes = sb("w4_codes", N, U32)
        out_rows = out.rearrange("(f p) j -> p f j", f=2)

        def damped(c):
            nc.vector.tensor_tensor(
                h_bf[:, 4 * CHUNK * c : 4 * CHUNK * (c + 1)].rearrange("p (q i t) -> p q t i", t=4, i=2),
                a_banks[c][:].rearrange("p (t q i) -> p q t i", t=4, i=2),
                damp[c].rearrange("p t (q i) -> p q t i", i=2),
                MULT,
            )

        def exposures(lo, hi, banks, late_scale):
            width = hi - lo
            result = results[:, 2 * lo : 2 * hi]
            tiles = {b: bank(b) for b in sorted(set(banks))}
            sums = []
            for f in range(2):
                first = width * f if banks[0] == banks[1] else 0
                sums.append(tiles[banks[f]][:, first : first + width])
                nc.tensor.matmul_mx(
                    out=sums[f],
                    lhsT=w4_codes[:, P * f : P * (f + 1)].bitcast(FP8X4),
                    lhsT_scale=late_scale[:, S + P * f : S + P * (f + 1)],
                    rhs=h_codes[:, lo:hi].bitcast(FP8X4),
                    rhs_scale=late_scale[:, lo:hi],
                    start=True,
                    stop=True,
                )
            for f in range(2):
                dst = results[:, 2 * lo + width * f : 2 * lo + width * (f + 1)]
                if banks[f] != banks[0]:
                    nc.vector.tensor_scalar(dst, sums[f], fs[:, f : f + 1], fb[:, f : f + 1], MULT, ADD)
                else:
                    nc.scalar.activation(
                        out=dst, in_=sums[f], func=ACT.Identity, scale=fs[:, f : f + 1], bias=fb[:, f : f + 1]
                    )
                if banks[0] != banks[1]:
                    (nc.sync if f else nc.scalar).dma_start(out_rows[:, f, lo:hi], dst)
            if banks[0] == banks[1]:
                nc.sync.dma_start(out_rows[:, :, lo:hi], result.rearrange("p (f j) -> p f j", f=2))

        results = sb("m_abs1", 2 * S, F32)
        for c in range(HALF_CHUNKS + 1):
            damped(c)
        late_scale = sb("damp4", S + N, U8)
        quantize(w4_codes[:], late_scale[:, S : S + N], w4_bf)

        def finish(first, end, banks):
            lo, hi = CHUNK * first, CHUNK * end
            quantize(h_codes[:, lo:hi], late_scale[:, lo:hi], h_bf[:, 4 * lo : 4 * hi])
            exposures(lo, hi, banks, late_scale)

        finish(0, 2, (0, 0))
        damped(5)
        finish(2, 4, (1, 1))
        finish(4, 6, (2, 2))
        damped(6)
        damped(7)
        finish(6, 7, (3, 3))
        finish(7, 8, (4, 5))
